import numpy as np, ml_dtypes
CORES = [3,11,19,27,35,43,51,59]
N = 8
import mx_ref
BF = ml_dtypes.bfloat16
def tile(rs):
    return np.stack(rs, axis=2).reshape(128, -1).astype(BF)
def pick(q, e):
    c = np.concatenate([q[0].reshape(128, -1, 4), np.zeros((128, 1, 4), np.uint8)], axis=1); s = np.concatenate([q[1], np.ones((16, 1), np.uint8)], axis=1)
    return (np.ascontiguousarray(c[:, e].reshape(128, -1)), np.ascontiguousarray(s[:, e]))
def join(*qs):
    return (np.concatenate([q[0] for q in qs], axis=1), np.concatenate([q[1] for q in qs], axis=1))
def put(q, e, v):
    c, s = q[0].reshape(128, -1, 4).copy(), q[1].copy(); c[:, e] = v[0].reshape(128, -1, 4); s[:, e] = v[1]
    return (c.reshape(128, -1), s)
def pk(c, s):
    return (np.ascontiguousarray(c), mx_ref.live(s))
def emit(q):
    return q[0], q[1]
def packed(v, rng):
    q = [mx_ref.quantize(np.ascontiguousarray(v[r])) for r in range(N)]
    return np.stack([a for a, b in q]), np.stack([mx_ref.plane(b, rng) for a, b in q])
def values_of_codes():
    e, c = np.zeros((128, 128, 4), np.float32), np.zeros((128, 2, 4), np.uint8)
    e[np.arange(128), np.arange(128), 0] = 1
    c[:127, :, 0] = np.arange(256).reshape(2, 128).T[:127]
    return mx_ref.matmul(mx_ref.quantize(e.reshape(128, 512).astype(BF)), (c.reshape(128, 8), np.full((16, 2), 127, np.uint8))).T.reshape(-1).astype(np.float64)
CODE_VALUE, SCALE_VALUE = values_of_codes(), 2.0 ** (np.arange(256) - 127.0)
def decode(q):
    return (CODE_VALUE[q[0]].reshape(16, 8, -1, 4) * SCALE_VALUE[q[1]][:, None, :, None] + 0.0).reshape(128, -1).astype(np.float32)
def f(rng, *shape):
    return mx_ref.flush((rng.standard_normal(shape, dtype=np.float32) * np.exp2(rng.integers(-2, 3, shape[:-1] + (1,)))).astype(BF))
def wide(rng, *shape, cols=0):
    v = rng.standard_normal(shape, dtype=np.float32) * np.exp2(rng.integers(-12, 13, shape)).astype(np.float32)
    if cols: v *= np.repeat(np.exp2(rng.integers(-cols, cols + 1, shape[:-2] + (1, shape[-1] // 4))) * (rng.random(shape[:-2] + (1, shape[-1] // 4)) > 0.0625), 4, axis=-1).astype(np.float32)
    return mx_ref.flush(v.astype(BF))
C, A, R = 256, 128, 3
def numbers_of(rng):
    return {"x": np.array(f(rng, N, 128, 4 * C)), "u": np.array(f(rng, N, 128, 512)), "v": np.array(f(rng, N, 128, 512))}
def layers(rng):
    return np.array(f(rng, N, 128, 2048)).reshape(N, 8, 16, 4, 8, 16, 4)
def weights(rng, w):
    c, s = packed(np.ascontiguousarray(w).reshape(N, 128, 2048), rng)
    return {"wc": c, "ws": s}
def setup_inputs(rng):
    return {**numbers_of(rng), **weights(rng, layers(rng))}
def setup_inputs_ties(rng):
    d = numbers_of(rng)
    x = d["x"].reshape(N, 8, 16, C, 4)
    u = d["u"].reshape(N, 128, 128, 4)
    e = rng.permutation(N)
    for i, r in enumerate(e):
        k = np.arange(C) % 3
        if i % 2 == 0: k = k[rng.permutation(C)]
        if i == 0: k = np.zeros(C, int)
        a = x[r][:, :8, :3].copy()
        a[:, :, 2] = 0
        x[r][:, :8] = a[:, :, k]
        if i % 4 in (0, 3):
            u[r][:, ::16] = u[r][:, :1].copy()
            u[r][:, 1::16] = u[r][:, 1:2].copy()
    x[e[1]] = 0
    h = u.reshape(N, 8, 16, 128, 4)
    h[:, :, 8:, ::16] = 0
    h[:, :, 8:, 1::16] = 0
    w = layers(rng)
    w[:, :, :, :, :, :8] = 0
    return {"x": x.reshape(N, 128, 4 * C), "u": u.reshape(N, 128, 512), "v": d["v"], **weights(rng, w)}
def setup_inputs_near(rng):
    d = numbers_of(rng)
    x = d["x"].astype(np.float32).reshape(N, 8, 16, C, 4)
    u = d["u"].reshape(N, 128, 128, 4)
    u[:, :, ::16] = 0
    u[:, :, 1::16] = 0
    x[:, :, 0] = 0
    x[:, :, 8:] = 0
    o = rng.permutation(N) % 4
    for r in range(N):
        k = 1.0 if o[r] == 0 else 2.0 ** -30
        if o[r] < 3: x[r, :, 8] = ((rng.integers(0, 16, (8, C))[:, :, None] >> np.arange(4)) & 1) * np.exp2(np.arange(4) - 23.0)
        if o[r] < 2:
            x[r, :, 0, :, 0] = rng.integers(0, 2, (8, C)) * 2.0 - 1.0
            x[r, :, 11, :, 0] = 2.0 ** -10
        if o[r] == 2:
            for g in rng.permutation(8)[:4]: x[r, g, 0, rng.integers(C), 0] = 2.0 ** 16 * rng.choice([-1.0, 1.0])
        if o[r] == 3:
            s = rng.integers(0, 2, (8, C)) * 0.125
            x[r, :, 10, :, 0] = (1.0 + s) * 2.0 ** -30
            x[r, :, 12, :, 0] = (1.125 - s) * 2.0 ** -30
        for h in range(0, 128, 16):
            for c, a in ((h, h), (h + 1, (h + 16) % 128)):
                if o[r] < 3:
                    u[r, a, c, 0] = 2.0 ** 30 if o[r] == 2 else k
                    u[r, a + 8, c] = k
                if o[r] < 2: u[r, a + 11, c, 0] = k
                if o[r] == 3:
                    u[r, a + 10, c, 0] = 1.25 * k
                    u[r, a + 12, c, 0] = 1.125 * k
    w = layers(rng)
    for i in [0] + [8 + j for j in range(8)]:
        w[:, :, i] = 0
        w[:, :, :, :, :, i] = 0
    return {"x": x.reshape(N, 128, 4 * C).astype(BF), "u": u.reshape(N, 128, 512), "v": d["v"], **weights(rng, w)}
def setup_inputs_ends(rng):
    d = numbers_of(rng)
    o = (np.arange(N) + rng.integers(N)) % 4
    x = np.zeros((N, 8, 16, C, 4), np.float32)
    u = d["u"].reshape(N, 128, 128, 4)
    for r in range(N):
        a = 2.0 ** 30 * (1.0 - 0.1 * rng.random((128, 8, 2, 4)))
        if o[r] == 0:
            x[r] = -2.0 ** 29 * (0.8 + 0.075 * rng.random((8, 16, C, 4)))
            a[:, :, 0] *= np.exp2(-1.0 * np.concatenate([rng.permutation(4), rng.permutation(4)]))[:, None]
            d["v"][r] = (2.0 ** 30 * rng.choice([-1.0, 1.0], (128, 512))).astype(np.float32).astype(BF)
        if o[r] == 1:
            x[r] = 2.0 ** 29 * np.where((rng.permutation(C) % 2 == 0)[:, None], 0.875, -0.7 - 0.07 * rng.random((8, 16, C, 4)))
            a *= rng.choice([-1.0, 1.0], (8, 2))[None, :, :, None]
        if o[r] == 2:
            x[r] = 2.0 ** -30 * rng.choice([-1.0, 1.0], (8, 16, C, 4))
            a = 2.0 ** -30 * rng.choice([-1.0, 1.0], (128, 8, 2, 4))
            a[0, :, :, 0] = 0
            d["v"][r] = (2.0 ** -30 * rng.choice([-1.0, 1.0], (128, 512))).astype(np.float32).astype(BF)
        if o[r] == 3:
            x[r] = (1.0 + rng.random((8, 16, 1, 4))) * rng.choice([-1.0, 1.0], (8, 16, 1, 4))
            a = (1.0 + rng.random((128, 1, 2, 4))) * rng.choice([-1.0, 1.0], (128, 1, 2, 4)) * np.ones((1, 8, 1, 1))
        a = a.astype(np.float32).astype(BF)
        u[r][:, ::16] = a[:, :, 0]
        u[r][:, 1::16] = a[:, :, 1]
    w = np.zeros((N, 128, 4, 128, 4), np.float32)
    i = np.arange(128)
    for b in range(4): w[:, i, b, i, b] = 2
    return {"x": x.reshape(N, 128, 4 * C).astype(BF), "u": u.reshape(N, 128, 512), "v": d["v"], **weights(rng, w.astype(BF))}
def setup_inputs_odd(rng):
    d = numbers_of(rng)
    k = (N, 8, 16, C, 4)
    x = (129.0 + 2.0 * rng.integers(0, 64, k)) * np.exp2(rng.integers(-21, -14, k)) * rng.choice([-1.0, 1.0], k)
    x[:, :, ::8] = 0
    x[:, :, ::8, :, 0] = np.where(rng.random((N, 8, 2, C)) < 0.5, 1.96875, 1.875)
    w = layers(rng)
    w[:, :, ::8] = 0
    w[:, :, :, :, :, ::8] = 0
    return {"x": x.astype(np.float32).reshape(N, 128, 4 * C).astype(BF), "u": d["u"], "v": d["v"], **weights(rng, w)}
def setup_inputs_spread(rng):
    d = setup_inputs(rng)
    d["x"] = np.clip(wide(rng, N, 128, 4 * C, cols=2).astype(np.float32), -65536.0, 65536.0).astype(BF)
    return d
def check_inputs(d):
    b = []
    for k in ("x", "u", "v"):
        a = np.abs(d[k].astype(np.float32))
        if not (np.isfinite(a).all() and ((a == 0) | (a >= 2.0 ** -30) & (a <= 2.0 ** 30)).all()): b.append("a value of " + k)
    none, least, most = [emit(mx_ref.quantize(np.full((128, 16), k, np.float32).astype(BF)))[1][0, 0] for k in (0.0, 2.0 ** -30, 2.0 ** 30)]
    total = 0.0
    for r in range(N):
        if ((d["wc"][r] == 0x7F) | (d["wc"][r] == 0xFF)).any(): b.append("wc: a code that is no number")
        s = mx_ref.live(d["ws"][r])
        if ((s != none) & ((s < least) | (s > most))).any(): b.append("ws: a scale out of range")
        w = np.abs(decode(pk(d["wc"][r], d["ws"][r])).astype(np.float64)).reshape(128, 512, 4)
        total = max(total, float(np.max(np.sum(w, axis=(0, 2)))))
    a = float(np.max(np.abs(d["x"].astype(np.float32))))
    if not a * (1.0 + total * 0.015625) ** 3 <= 2.0 ** 29: b.append("x and W: a * (1 + s)**3")
    return b
def departures(s):
    half = np.argsort(-s[::16].reshape(2, 4 * C), axis=1, kind="stable") // C
    leaf = np.argsort(-s[1::16], axis=1, kind="stable")
    e = np.zeros((8, C), np.int64)
    for g in range(8): e[g, leaf[g]] = 2 * np.flatnonzero(half[g // 4] == g % 4) + g // 4
    return e.reshape(-1)
def reference(x, u, v, wc, ws):
    qu = [mx_ref.quantize(u[r]) for r in range(N)]
    lay = [pk(wc[r], ws[r]) for r in range(N)]
    now = [x[r] for r in range(N)]
    for t in range(R):
        own, dep, sent = [], [], []
        for r in range(N):
            q = mx_ref.quantize(now[r])
            dep.append(departures(mx_ref.matmul(qu[r], q) + np.float32(0.0)))
            own.append(decode(q).reshape(8, 16, C, 4).transpose(0, 2, 1, 3).reshape(8 * C, 16, 4))
            p = own[r][np.argsort(dep[r])]
            e = ((p[:4 * C] + p[4 * C:]) * np.float32(0.5)).astype(BF)
            sent.append(mx_ref.quantize(np.ascontiguousarray(e.reshape(A, 8, 16, 4).transpose(1, 2, 0, 3)).reshape(128, 4 * A)))
        for r in range(N):
            q = sent[r - 1]
            h = tile([mx_ref.matmul(pick(lay[r], np.arange(128 * b, 128 * b + 128)), q) * np.float32(0.015625) for b in range(4)])
            h = h.reshape(8, 16, A, 4).transpose(2, 0, 1, 3).reshape(8 * A, 16, 4).astype(np.float32)
            z = (own[r] + h[dep[r] % (4 * C)]).astype(BF)
            now[r] = np.ascontiguousarray(z.reshape(8, C, 16, 4).transpose(0, 2, 1, 3)).reshape(128, 4 * C)
    y, op = np.zeros((N, 128, C), np.float32), np.zeros((N, 8, C), np.float32)
    oc, osc = np.zeros((N, 128, 4 * C), np.uint8), np.zeros((N, 16, C), np.uint8)
    for r in range(N):
        q = mx_ref.quantize(now[r])
        y[r] = mx_ref.matmul(mx_ref.quantize(v[r]), q)
        op[r] = dep[r].reshape(8, C)
        oc[r], osc[r] = emit(q)
    return {"y": y, "op": op, "oc": oc, "osc": osc}

@@ -1,0 +1,515 @@
+from concourse.mybir import dt, AluOpType as A, ActivationFunctionType as F
+import comms_topo
+
+R = 3
+SCRATCH = {}
+SEMAPHORES = ["sV", "sS", "sP", "sG", "ls"] + ["arr%d" % t for t in range(R)] + ["lst%d" % t for t in range(R)] + ["d%d" % i for i in range(40)]
+
+
+def _b(name, n, d, where="sbuf"):
+    SCRATCH[name] = (where, [128, n], d)
+
+
+def _q(name, n):
+    _b(name, n, "float8_e4m3fn_x4")
+    _b(name + "_s", n, "uint8")
+
+
+for _t in range(R):
+    _q("qx%d" % _t, 768)
+    _q("land%d" % _t, 256)
+    _b("lin%d" % _t, 64, "uint16")
+    _b("el%d" % _t, 64, "uint16")
+for _n, _w in (("qx3", 256), ("qn", 256), ("qu", 128), ("qr", 2048), ("qv", 128), ("wq", 512), ("qwr", 2048), ("cc", 1024),
+               ("cid", 512), ("cwn", 2048), ("ke", 128), ("m2q", 1024), ("mq", 4096), ("qw", 256), ("qe", 128)):
+    _q(_n, _w)
+for _n, _w in (("xb", 1024), ("xs", 1024), ("xn", 1024), ("ub", 512), ("vb", 512), ("zero", 1024), ("cst", 3080), ("zc", 2600),
+               ("kb", 512), ("onesb", 128), ("halfb", 128), ("negb", 256), ("thr0", 256), ("thr1", 256), ("mt", 8192), ("m2", 4096),
+               ("dd", 8192), ("win", 4096), ("winh", 2048), ("fx", 1024), ("etmp", 512), ("eb", 512), ("ww", 1024),
+               ("ab", 256), ("da", 256), ("dn", 256), ("dat", 256)):
+    _b(_n, _w, "bfloat16")
+for _n in ("mk16", "rs16", "mk4", "rs4", "msk", "scn", "psb", "awin", "it16", "it4", "dfull", "ysb", "cols", "itb", "leaf"):
+    _b(_n, 256, "float32")
+_b("lw", 1024, "float32")
+_b("cf", 8, "float32")
+_b("kc", 16, "float32")
+for _n, _w in (("ci", 8), ("il", 128), ("il2", 128), ("il3", 128), ("xi", 64), ("xi2", 64), ("xi3", 64)):
+    _b(_n, _w, "int32")
+for _n, _w in (("ulist", 128), ("wlist", 128), ("n1l", 16), ("n2l", 16), ("pl", 16), ("ql", 16), ("xl", 64)):
+    _b(_n, _w, "uint16")
+SCRATCH["ld"] = ("dram", [32, 1024], "float32")
+_b("pr0", 1024, "float32", "psum")
+_b("pr1", 1024, "float32", "psum")
+for _k in range(4, 8):
+    _b("pb%d" % _k, 512, "float32", "psum")
+
+SAME = ((1, 1, 1, 2, 2, 2, 2, 2), (1, 0, 0, 0, 0, 0, 0, 0))
+OTHER = ((0, 1, 1, 1, 2, 2, 2, 2), (3, 2, 0, 0, 0, 0, 0, 0))
+
+
+def rank_program(g, core, T, topo):
+    rank = T.rank_of(core)
+    if rank is None:
+        return
+    nxt = T.cores[(rank + 1) % len(T.cores)]
+    prv = T.cores[(rank - 1) % len(T.cores)]
+    rid, pid, _se = topo.addr(nxt)
+    mask = topo.mask(core, nxt)
+    n_eng = len(topo.engines(core, nxt))
+    n_in = len(topo.engines(prv, core))
+
+    eng = {"V": g.vector, "S": g.scalar, "P": g.tensor, "G": g, "Y": g.sync}
+    cnt = {"V": 0, "S": 0, "P": 0, "G": 0}
+    waited = {e: {} for e in eng}
+    lastw, readers, total = {}, {}, {}
+    ndma, nrem = [0], [0]
+
+    def need(e, reads, writes, acc=False):
+        w = {}
+        own = "s" + e
+
+        def add(sv):
+            if w.get(sv[0], 0) < sv[1]:
+                w[sv[0]] = sv[1]
+        for k in reads:
+            if k in lastw:
+                add(lastw[k])
+            if k[0] == "K":
+                for sv in readers.get(k, ()):
+                    if sv[0] != own:
+                        add(sv)
+        for k in writes:
+            if k in lastw and not (acc and lastw[k][0] == own):
+                add(lastw[k])
+            for sv in readers.get(k, ()):
+                if sv[0] != own:
+                    add(sv)
+        for s, v in w.items():
+            if waited[e].get(s, 0) < v:
+                eng[e].wait_ge(T.sem[s], v)
+                waited[e][s] = v
+
+    def note(sv, reads, writes):
+        for k in reads:
+            readers.setdefault(k, []).append(sv)
+        for k in writes:
+            lastw[k] = sv
+            readers[k] = []
+        total[sv[0]] = max(total.get(sv[0], 0), sv[1])
+
+    def op(e, fn, args, reads, writes, acc=False, **kw):
+        need(e, reads, writes, acc)
+        cnt[e] += 1
+        fn(*args, **kw).then_inc(T.sem["s" + e], 1)
+        note(("s" + e, cnt[e]), reads, writes)
+
+    def dmas(e, pairs, reads, writes):
+        need(e, reads, writes)
+        s = "d%d" % ndma[0]
+        ndma[0] += 1
+        for out, in_ in pairs:
+            eng[e].dma_start(out, in_).then_inc(T.sem[s], 16)
+        note((s, 16 * len(pairs)), reads, writes)
+
+    def remote(out, in_, sem, reads):
+        need("G", reads, [])
+        g.remote_dma(out, in_, T.sem[sem], T.sem.ls, pid, rid, mask)
+        nrem[0] += 1
+
+    V, S, P = g.vector, g.scalar, g.tensor
+
+    def cv(name, a, b):
+        return T[name][:, a:b].bitcast(dt.uint8)
+
+    def quant(name, a, b, src, key, reads, s0=0):
+        op("V", V.quantize_mx, (T[name][:, a:b], T[name + "_s"][:, a:b], T[src][:, s0:s0 + 4 * (b - a)]), reads, [key])
+
+    def bank(k, n):
+        if k < 4:
+            return T["pr%d" % (k // 2)][:, 512 * (k % 2):512 * (k % 2) + n]
+        return T["pb%d" % k][:, 0:n]
+
+    def mm(k, n, l, la, r, ra, start, stop, reads):
+        op("P", P.matmul_mx, (bank(k, n), T[l][:, la:la + 128], T[l + "_s"][:, la:la + 128],
+                              T[r][:, ra:ra + n], T[r + "_s"][:, ra:ra + n], start, stop),
+           reads, [("K", k)], acc=not start)
+
+    def ts(out, in0, s1, o0, reads, writes, s2=None, o1=None):
+        op("V", V.tensor_scalar, (out, in0, s1, s2, o0) if o1 is None else (out, in0, s1, s2, o0, o1), reads, writes)
+
+    def tt(out, a, b, o, reads, writes):
+        op("V", V.tensor_tensor, (out, a, b, o), reads, writes)
+
+    def vcopy(out, in_, reads, writes):
+        op("V", V.tensor_copy, (out, in_), reads, writes)
+
+    def act(out, in_, f, reads, writes, **kw):
+        op("S", S.activation, (out, in_, f), reads, writes, **kw)
+
+    def memset(ap, c, writes, reads=()):
+        op("V", V.memset, (ap, c), list(reads), writes)
+
+    def iota(name, pat, base, cm):
+        op("G", g.iota, (T[name][:], pat, base, cm), [], [name], allow_small_or_imprecise_dtypes=True)
+
+    def select(out, in_, pat, cmp, base, cm, reads, writes):
+        op("G", g.affine_select, (out, in_, pat, cmp, 0.0, base, cm), reads, writes)
+
+    dmas("S", [(T.ub[:], T.u[:, :])], [], ["ub"])
+    dmas("Y", [(T.xb[:], T.x[:, :])], [], ["xb"])
+    dmas("Y", [(cv("wq", 0, 512), T.wc[:, :])], [], ["wq"])
+    dmas("Y", [(T.wq_s[:], T.ws[:, :])], [], ["wqs"])
+    dmas("Y", [(T.vb[:], T.v[:, :])], [], ["vb"])
+
+    iota("il", [[1, 2], [16, 8], [0, 8]], 0, 0)
+    iota("ci", [[0, 8]], 0, 1)
+    memset(T.zero[:], 0.0, ["zero"])
+    memset(T.negb[:], -2.0 ** -120, ["negb"])
+    memset(T.onesb[:], 1.0, ["onesb"])
+    memset(T.halfb[:], 0.5, ["halfb"])
+    vcopy(T.ulist[:], T.il[:], ["il"], ["ulist"])
+    for b in range(2):
+        select(T["thr%d" % b][:], T.negb[:], [[1, 256]], A.is_ge, -1 - 128 * b, -1, ["negb"], ["thr%d" % b])
+    for i in range(3):
+        act(T.zc[:, 1024 * i:min(2600, 1024 * i + 1024)], T.zero[:, 0:min(1024, 2600 - 1024 * i)], F.Copy, ["zero"], ["zz%d" % i])
+    zz = ["zz0", "zz1", "zz2"]
+    select(T.zc[:, 2084:2596:4], T.onesb[:], [[-1, 128]], A.is_equal, 0, 1, ["onesb"] + zz, ["zc4"])
+    for s in range(4):
+        select(T.zc[:, s * 520 + 4:s * 520 + 516:4], T.halfb[:], [[0, 4], [-64, 2], [-1, 16]], A.is_equal, -16 * s, 1, ["halfb"] + zz, ["zc%d" % s])
+    quant("qx0", 0, 256, "zero", "z0", ["zero"])
+    quant("qx0", 512, 768, "zero", "z0b", ["zero"])
+    quant("qu", 0, 128, "ub", "qu", ["ub"])
+
+    def pick_u(a):
+        lst = T.ulist[:, a // 16:a // 16 + 32]
+        vcopy(T.qr[:, a:a + 512].bitcast(dt.uint32), T.qu[:, 0:128].bitcast(dt.uint32).indirect(lst), ["qu", "ulist"], [("qr", a // 512)])
+        act(T.qr_s[:, a:a + 512], T.qu_s[:, 0:128].indirect(lst), F.Copy, ["qu", "ulist"], [("qrs", a // 512)])
+    pick_u(0)
+    quant("qx0", 256, 512, "xb", ("qx", 0), ["xb"])
+    act(T.xn[:], T.xb[:], F.Copy, ["xb"], ["xn"], scale=-1.0)
+
+    def col(c):
+        return T.cf[:, c:c + 1]
+
+    def kc(c):
+        return T.kc[:, c:c + 1]
+
+    def qrk(s, gr):
+        i = (8 * s + gr) // 4
+        return [("qr", i), ("qrs", i)]
+
+    def setup_cols():
+        for c, sh, an in ((1, 0, 15), (2, 2, 3), (3, 0, 3), (4, 4, 3), (5, 0, 1), (6, 6, 1)):
+            ts(T.ci[:, c:c + 1], T.ci[:, 0:1], sh, A.logical_shift_right, ["ci"], ["ci%d" % c], an, A.bitwise_and)
+        vcopy(T.cf[:, 0:7], T.ci[:, 0:7], ["ci"] + ["ci%d" % c for c in range(1, 7)], ["cf"])
+
+    def setup_pool():
+        iota("it16", [[0, 16], [1, 16]], 0, 0)
+        iota("it4", [[0, 64], [1, 4]], 0, 0)
+        for nm, q in (("rs16", 16), ("rs4", 4)):
+            iota(nm, [[0, 256]], 1, 0)
+            select(T[nm][:], T[nm][:], [[0, 256 // q], [1, q]], A.not_equal, 0, 0, [nm], [nm])
+        iota("itb", [[1, 256]], 0, 0)
+        iota("il2", [[32, 16], [16, 2], [0, 4]], 0, 0)
+
+    def setup_windows(ss):
+        for s in ss:
+            for b in range(4):
+                a = 128 * (4 * s + b)
+                quant("cwn", a, a + 128, "zc", ("cwn", s, b), zz + ["zc%d" % s], s0=520 * s + 4 - b)
+
+    def setup_own():
+        for b in range(4):
+            quant("cid", 128 * b, 128 * b + 128, "zc", ("cid", b), zz + ["zc4"], s0=2084 - b)
+
+    def setup_ones():
+        memset(T.cst[:], 0.0, ["cst"])
+        memset(T.cst[:, 448:512], 1.0, ["cst8"], ["cst"])
+        for t in range(4):
+            if t < 2:
+                memset(T.cst[:, 1476 + t:1540:4], 1.0, ["cst%d" % t], ["cst"])
+            o = 2504 + 64 * (t // 2)
+            memset(T.cst[:, o + t:o + 64:4], 1.0 - 0.5 * (t % 2), ["cst%d" % (4 + t)], ["cst"])
+        for i, o in enumerate((0, 1028, 1026, 2056)):
+            quant("cc", 256 * i, 256 * i + 256, "cst", "cc%d" % (i // 2), ["cst", "cst0", "cst1", "cst4", "cst5", "cst6", "cst7", "cst8"], s0=o)
+
+    def setup_lists():
+        ts(T.mk16[:], T.it16[:], col(1), A.is_equal, ["it16", "cf"], ["mk16"])
+        ts(T.mk4[:], T.it4[:], col(2), A.is_equal, ["it4", "cf"], ["mk4"])
+        ts(kc(1), col(1), 0.0, A.is_equal, ["cf"], ["kc1"], 32.0, A.mult)
+        ts(kc(2), col(1), 1.0, A.is_equal, ["cf"], ["kc2"])
+        tt(kc(3), kc(1), kc(2), A.add, ["kc1", "kc2"], ["kc3"])
+        tt(kc(5), kc(3), col(6), A.mult, ["kc3", "cf"], ["kc5"])
+        tt(kc(4), kc(3), kc(5), A.subtract, ["kc3", "kc5"], ["kc4"])
+        memset(T.kb[:], 0.0, ["kb"])
+        for q in range(8):
+            ts(T.kb[:, 64 * q + q // 2:64 * q + 64:4], T.onesb[:, 0:16], kc(4 + q % 2), A.mult,
+               ["onesb", "kc4", "kc5", "kb"], ["kb%d" % q])
+        quant("ke", 0, 128, "kb", "ke", ["kb"] + ["kb%d" % q for q in range(8)])
+        act(kc(6), col(3), F.Copy, ["cf"], ["kc6"], scale=1024.0)
+        act(kc(7), col(3), F.Copy, ["cf"], ["kc7"], scale=512.0)
+        act(kc(8), col(4), F.Copy, ["cf"], ["kc8"], scale=8.0, bias=-208.0)
+        act(kc(9), kc(8), F.Copy, ["kc8"], ["kc9"], scale=-1.0, bias=6128.0)
+        act(kc(10), col(5), F.Identity, ["kc8", "kc9", "cf"], ["kc10"], scale=kc(9), bias=kc(8))
+        act(kc(11), col(5), F.Copy, ["cf"], ["kc11"], scale=-33.0, bias=1.0)
+        act(kc(12), col(4), F.Copy, ["cf"], ["kc12"], scale=256.0)
+        act(T.itb[:], T.itb[:], F.Identity, ["itb", "kc12"], ["itb"], bias=kc(12))
+        ts(T.il3[:], T.il2[:], col(1), A.add, ["il2", "cf"], ["il3"])
+        vcopy(T.wlist[:], T.il3[:], ["il3"], ["wlist"])
+        for t in (1, 2):
+            dmas("Y", [(cv("qx%d" % t, a, a + 256), cv("qx0", a, a + 256)) for a in (0, 512)] +
+                 [(T["qx%d_s" % t][:, a:a + 256], T.qx0_s[:, a:a + 256]) for a in (0, 512)], ["z0", "z0b"], ["z%d" % t])
+
+    def wrap(src, mk, rs, srckeys):
+        tt(T.msk[:], src, T[mk][:], A.mult, srckeys + [mk], ["msk"])
+        op("V", V.tensor_tensor_scan, (T.scn[:], T[rs][:], T.msk[:], 0.0, A.mult, A.add), [rs, "msk"], ["scn"])
+
+    for t in range(R):
+        qx = "qx%d" % t
+        X = ("qx", t)
+        zk = ["z0", "z0b"] if t == 0 else ["z%d" % t]
+        remote(cv("land%d" % t, 0, 256), cv(qx, 256, 512), "arr%d" % t, [X])
+        remote(T["land%d_s" % t][:], T[qx + "_s"][:, 256:512], "arr%d" % t, [X])
+        iota("ww", [[0, 1024]], 0, 0)
+        land, lin = "land%d" % t, "lin%d" % t
+        lastw[land] = ("arr%d" % t, 2 * n_in)
+        lastw[lin] = ("lst%d" % t, n_in)
+        total["arr%d" % t] = 2 * n_in
+        total["lst%d" % t] = n_in
+
+        for b in range(2):
+            mm((4, 7)[b], 128, qx, 256 + 128 * b, "qu", 0, True, True, [X, "qu"])
+
+        def rows(h, i):
+            for j in range(2):
+                gr = 4 * h + 2 * i + j
+                mm(2 * h + i, 512, "qr", 128 * gr, qx, 256 - 256 * j, j == 0, j == 1, [X] + zk + qrk(0, gr))
+        rows(0, 0)
+        for b in range(2):
+            vcopy(T.cols[:, 128 * b:128 * b + 128], bank((4, 7)[b], 128), [("K", (4, 7)[b])], [("cols", b)])
+        quant("qn", 0, 256, "xn", "qn", ["xn"] if t == 0 else [("xn", 0), ("xn", 1)])
+        flip = {"V": 0, "S": 0}
+
+        def diff(e, s, gr, b, lo):
+            k = {"V": (5, 6), "S": (7, 4)}[e][flip[e] % 2]
+            flip[e] += 1
+            a = 128 * (8 * s + gr)
+            mm(k, 128, "qr", a, "qn", lo, True, False, qrk(s, gr) + ["qn"])
+            mm(k, 128, qx, 256 + 128 * b, "qr", a, False, True, qrk(s, gr) + [X])
+            return k
+
+        pairs = [(gr, b) for gr in range(8) for b in range(2)]
+        same, other = list(pairs), list(pairs)
+        s2k = [("m2", gr, b, i) for gr, b in pairs for i in range(2)]
+
+        def s2_same(n):
+            for gr, b in same[:n]:
+                k = diff("V", 1, gr, b, 128 * b)
+                o = 1024 * (gr // 2) + 512 * b
+                tt(T.m2[:, o + 2 * (gr % 2):o + 512:4], bank(k, 128), T["thr%d" % b][:, 128 * b:128 * b + 128], A.is_gt,
+                   [("K", k), "thr%d" % b], [("m2", gr, b, 0)])
+            del same[:n]
+
+        def s2_other(n):
+            for gr, b in other[:n]:
+                k = diff("S", 1, gr, b, 128 - 128 * b)
+                o = 1024 * (gr // 2) + 512 - 512 * b
+                act(T.m2[:, o + 2 * (gr % 2) + 1:o + 512:4], bank(k, 128), F.Sign, [("K", k)], [("m2", gr, b, 1)],
+                    bias=(1 - 2 * b) * 2.0 ** -120)
+            del other[:n]
+
+        def sign(h, k):
+            c = 128 * (k % 2) + 16 * (4 * h + k // 2)
+            for a, n in ((0, 1), (1, 1)) if h + k == 0 else ((0, 2),):
+                act(T.dd[:, 1024 * k + 512 * a:1024 * k + 512 * (a + n)], T["pr%d" % h][:, 512 * a:512 * (a + n)], F.Sign,
+                    [("K", 2 * h + i) for i in range(a, a + n)] + [("cols", k % 2)], [("dd", k, i) for i in range(a, a + n)],
+                    scale=-1.0, bias=T.cols[:, c:c + 1])
+
+        def fix(h, k):
+            b, tq, base, dg = k % 2, k % 4, 4096 * (k // 4), 128 * k
+            dk = [("dd", k, 0), ("dd", k, 1)]
+            if dg:
+                ts(T.mt[:, base + tq:base + 4 * dg:4], T.dd[:, 1024 * k:1024 * k + dg], 0.0, A.is_gt, dk, [("mt", k, 0)])
+            if dg + 128 < 1024:
+                ts(T.mt[:, base + 4 * (dg + 128) + tq:base + 4096:4], T.dd[:, 1024 * k + dg + 128:1024 * k + 1024], 0.0, A.is_ge, dk, [("mt", k, 1)])
+            kk = diff("V", 0, 4 * h + k // 2, b, 128 * b)
+            tt(T.mt[:, base + 4 * dg + tq:base + 4 * (dg + 128):4], bank(kk, 128), T["thr%d" % b][:, 128 * b:128 * b + 128], A.is_gt,
+               [("K", kk), "thr%d" % b], [("mt", k, 2)])
+
+        def qm(h, i):
+            m0 = 1024 * (2 * h + i)
+            for a in (0, 512):
+                quant("mq", m0 + a, m0 + a + 512, "mt", ("mq", h, i, a), [("mt", k, e) for k in range(4 * i, 4 * i + 4) for e in range(3)],
+                      s0=4096 * i + 4 * a)
+
+        def count(h, i, gis, first=False, last=False):
+            m0 = 1024 * (2 * h + i)
+            for gi in gis:
+                gr = 4 * h + gi
+                mk = [("mq", h, i, 512 * (gi // 2)), "cc0", "cc1"]
+                if gi // 2 == i:
+                    mm(1, 256, "cc", 256 * (1 + gi % 2) + 112 - 16 * gr, "mq", m0 + 256 * gi, first and gi % 2 == 0, last and gi % 2 == 1, mk)
+            for gi in gis:
+                gr = 4 * h + gi
+                mk = [("mq", h, i, 512 * (gi // 2)), "cc0", "cc1"]
+                mm(0, 256, "cc", 112 - 16 * gr, "mq", m0 + 256 * gi, first and gi == 0, last and gi == 3, mk)
+
+        wins = [(s, b) for s in range(4) for b in range(4)] + [(4, b) for b in range(4)]
+        wn = [0]
+        pend = []
+
+        def win_mm(n):
+            for _i in range(n):
+                if wins:
+                    s, b = wins.pop(0)
+                    k = (7, 2, 3, 5, 6)[wn[0] % 5]
+                    wn[0] += 1
+                    if s < 4:
+                        mm(k, 256, "cwn", 128 * (4 * s + b), land, 0, True, True, [land, ("cwn", s, b)])
+                    else:
+                        mm(k, 256, "cid", 128 * b, qx, 256, True, True, [X, ("cid", b)])
+                    pend.append((k, s, b))
+
+        def win_cp(n):
+            for _i in range(n):
+                if pend:
+                    k, s, b = pend.pop(0)
+                    if s < 4:
+                        o = 1024 * b + 256 * s
+                        act(T.win[:, o:o + 256], bank(k, 256), F.Copy, [("K", k)], [("win", s, b)])
+                    else:
+                        act(T.fx[:, b:1024:4], bank(k, 256), F.Copy, [("K", k)], [("fx", b)])
+
+        if t == 0:
+            rows(0, 1)
+            sign(0, 0)
+            pick_u(1024)
+            s2_same(2)
+            setup_cols()
+            setup_windows((0, 1))
+            setup_pool()
+        else:
+            s2_same(1)
+            rows(0, 1)
+            s2_same(1)
+        for k in range(8):
+            if t or k:
+                sign(0, k)
+            if t == 0 and k in (1, 2):
+                pick_u(1024 * k - 512)
+            s2_other(OTHER[0][k])
+            if k in (2, 4):
+                rows(1, k // 2 - 1)
+            s2_same(SAME[0][k])
+            fix(0, k)
+            if t == 0 and 2 < k < 7:
+                (setup_ones, lambda: setup_windows((2,)), lambda: setup_windows((3,)), setup_own)[k - 3]()
+            if k % 4 == 3:
+                qm(0, k // 4)
+        if t == 0:
+            setup_lists()
+        for k in range(8):
+            sign(1, k)
+            s2_other(OTHER[1][k])
+            s2_same(SAME[1][k])
+            fix(1, k)
+            if k == 1:
+                for a in (0, 512):
+                    quant("m2q", a, a + 512, "m2", ("m2q", a), s2k, s0=4 * a)
+            if k == 2:
+                for q in range(4):
+                    mm(4, 256, "cc", 768 + 112 - 32 * q, "m2q", 256 * q, q == 0, q == 3, [("m2q", 512 * (q // 2)), "cc1"])
+            if k == 3:
+                count(0, 0, range(4), True)
+                qm(1, 0)
+                wrap(bank(4, 256), "mk16", "rs16", [("K", 4)])
+                ts(T.n2l[:], T.scn[:, 15:256:16], 64.0, A.add, ["scn"], ["n2l"])
+                vcopy(T.leaf[:, 0:256].indirect(T.n2l[:, 0:16]), T.itb[:], ["itb", "n2l"], ["leaf"])
+                dmas("Y", [(T.ld[16 * (q // 4):16 * (q // 4) + 16, 256 * (q % 4):256 * (q % 4) + 256], T.leaf[16 * q:16 * q + 16, :]) for q in range(8)], ["leaf"], ["ld"])
+                dmas("Y", [(T.lw[16 * q:16 * q + 16, :], T.ld[16 * (q % 2):16 * (q % 2) + 16, :]) for q in range(8)], ["ld"], ["lw"])
+            if k == 4:
+                count(0, 1, range(4))
+            if k == 5:
+                count(1, 0, range(4))
+        qm(1, 1)
+        win_mm(3)
+        count(1, 1, (0, 1))
+        win_cp(3)
+        count(1, 1, (2, 3), last=True)
+
+        act(T.ab[:], bank(1, 256), F.Copy, [("K", 1)], ["ab"], scale=0.03125, bias=191.515625)
+        act(T.da[:], T.ab[:], F.Identity, ["ab", "kc10", "kc11"], ["da"], scale=kc(11), bias=kc(10))
+        act(T.dn[:], bank(1, 256), F.Copy, [("K", 1), "cf"], ["dn"], scale=col(5))
+        wrap(bank(0, 256), "mk16", "rs16", [("K", 0)])
+        vcopy(T.pl[:], T.scn[:, 15:256:16], ["scn"], ["pl"])
+        tt(T.dat[:], T.dn[:], T.da[:], A.add, ["dn", "da"], ["dat"])
+        vcopy(T.ww[:, 0:1024].indirect(T.pl[:, 0:16]), T.dat[:], ["pl", "dat"], ["ww"])
+        quant("qw", 0, 256, "ww", "qw", ["ww"])
+        win_mm(5)
+        mm(4, 256, "ke", 0, "qw", 0, True, True, ["ke", "qw"])
+        win_cp(5)
+        while wins or pend:
+            win_mm(3)
+            win_cp(3)
+        wrap(bank(4, 256), "mk16", "rs16", [("K", 4)])
+        ts(T.ql[:], T.scn[:, 15:256:16], 528.0, A.add, ["scn"], ["ql"])
+        wrap(T.lw[:, 0:1024].indirect(T.ql[:, 0:16]), "mk4", "rs4", ["lw", "ql"])
+        el = "el%d" % t
+        ts(T[el][:], T.scn[:, 3:256:4], kc(6), A.add, ["scn", "kc6"], [el])
+        remote(T[lin][:], T[el][:], "lst%d" % t, [el])
+
+        wrap(bank(1, 256), "mk16", "rs16", [("K", 1)])
+        vcopy(T.n1l[:], T.scn[:, 15:256:16], ["scn"], ["n1l"])
+        vcopy(T.psb[:], bank(0, 256), [("K", 0)], ["psb"])
+        vcopy(T.awin[:, 0:256].indirect(T.n1l[:, 0:16]), T.psb[:], ["n1l", "psb"], ["awin"])
+        wrap(T.awin[:, 0:256].indirect(T.n2l[:, 0:16]), "mk4", "rs4", ["awin", "n2l"])
+        if t == R - 1:
+            vcopy(T.dfull[:], T.awin[:, 0:256].indirect(T.n2l[:, 0:16]), ["awin", "n2l"], ["dfull"])
+            ts(T.dfull[:], T.dfull[:], 2.0, A.mult, ["dfull", "cf"], ["dfull"], col(6), A.add)
+            dmas("Y", [(T.op[q:q + 1, :], T.dfull[16 * q:16 * q + 1, :]) for q in range(8)], ["dfull"], ["op"])
+            quant("qv", 0, 128, "vb", "qv", ["vb"])
+        if t == 0:
+            vcopy(T.qwr[:].bitcast(dt.uint32), T.wq[:, 0:512].bitcast(dt.uint32).indirect(T.wlist[:, 0:128]), ["wq", "wlist"], ["qwr"])
+            act(T.qwr_s[:], T.wq_s[:, 0:512].indirect(T.wlist[:, 0:128]), F.Copy, ["wqs", "wlist"], ["qwrs"])
+
+        wk = [("win", s, b) for s in range(4) for b in range(4)] + [lin]
+        for i in range(2):
+            act(T.etmp[:, 256 * i:256 * i + 256], T.win[:, 0:4096].indirect(T[lin][:, 16 * i:16 * i + 16]), F.Copy, wk, [("etmp", i)])
+            tt(T.eb[:, 256 * i:256 * i + 256], T.win[:, 0:4096].indirect(T[lin][:, 32 + 16 * i:48 + 16 * i]), T.etmp[:, 256 * i:256 * i + 256], A.add,
+               wk + [("etmp", i)], [("eb", i)])
+        quant("qe", 0, 128, "eb", "qe", [("eb", 0), ("eb", 1)])
+        vcopy(T.xi[:], T.scn[:, 3:256:4], ["scn"], ["xi"])
+        ts(T.xi2[:], T.xi[:], 2, A.logical_shift_right, ["xi"], ["xi2"], 127, A.bitwise_and)
+        ts(T.xi3[:], T.xi[:], 3, A.bitwise_and, ["xi"], ["xi3"])
+        ts(T.xi3[:], T.xi3[:], 128.0, A.mult, ["xi3", "kc7"], ["xi3"], kc(7), A.add)
+        tt(T.xi2[:], T.xi2[:], T.xi3[:], A.add, ["xi2", "xi3"], ["xi2"])
+        vcopy(T.xl[:], T.xi2[:], ["xi2"], ["xl"])
+        for i in range(16):
+            k, s, b = i % 8, i // 4, i % 4
+            mm(k, 128, "qwr", 128 * (4 * b + s), "qe", 0, True, True, ["qwr", "qwrs", "qe"])
+            o = 512 * b + 128 * s
+            if i % 2:
+                ts(T.winh[:, o:o + 128], bank(k, 128), 0.015625, A.mult, [("K", k)], [("winh", i)])
+            else:
+                act(T.winh[:, o:o + 128], bank(k, 128), F.Copy, [("K", k)], [("winh", i)], scale=0.015625)
+        hk = [("winh", i) for i in range(16)] + ["xl"] + [("fx", b) for b in range(4)]
+        for i in range(2):
+            c = 512 * i
+            tt(T.xs[:, c:c + 512], T.winh[:, 0:2048].indirect(T.xl[:, 32 * i:32 * i + 32]), T.fx[:, c:c + 512], A.add, hk, [("xs", i)])
+            if t < R - 1:
+                act(T.xn[:, c:c + 512], T.xs[:, c:c + 512], F.Copy, [("xs", i)], [("xn", i), "xn"] if t == 0 else [("xn", i)], scale=-1.0)
+        if t < R - 1:
+            quant("qx%d" % (t + 1), 256, 512, "xs", ("qx", t + 1), [("xs", 0), ("xs", 1)])
+        else:
+            quant("qx3", 0, 256, "xs", "qx3", [("xs", 0), ("xs", 1)])
+
+    mm(0, 256, "qv", 0, "qx3", 0, True, True, ["qv", "qx3"])
+    dmas("Y", [(T.oc[:, :], cv("qx3", 0, 256))], ["qx3"], ["oc"])
+    dmas("S", [(T.osc[4 * k:4 * k + 4, :], T.qx3_s[32 * k:32 * k + 4, 0:256]) for k in range(4)], ["qx3"], ["osc"])
+    vcopy(T.ysb[:], bank(0, 256), [("K", 0)], ["ysb"])
+    dmas("Y", [(T.y[:, :], T.ysb[:])], ["ysb"], ["y"])
+    total["ls"] = nrem[0] * n_eng
+    for e in cnt:
+        total["s" + e] = cnt[e]
+    for s in sorted(total):
+        g.wait_ge(T.sem[s], total[s])

@@ -3,7 +3,7 @@ import comms_topo
 
 R = 3
 SCRATCH = {}
-SEMAPHORES = ["sV", "sS", "sP", "sG", "ls"] + ["arr%d" % t for t in range(R)] + ["lst%d" % t for t in range(R)] + ["d%d" % i for i in range(40)]
+SEMAPHORES = ["sV", "sS", "sP", "sG", "ls"] + ["arr%d" % t for t in range(R)] + ["lst%d" % t for t in range(R)] + ["d%d" % i for i in range(30)]
 
 
 def _b(name, n, d, where="sbuf"):
@@ -16,35 +16,34 @@ def _q(name, n):
 
 
 for _t in range(R):
-    _q("qx%d" % _t, 768)
+    _q("qx%d" % _t, 256)
     _q("land%d" % _t, 256)
-    _b("lin%d" % _t, 64, "uint16")
-    _b("el%d" % _t, 64, "uint16")
-for _n, _w in (("qx3", 256), ("qn", 256), ("qu", 128), ("qr", 2048), ("qv", 128), ("wq", 512), ("qwr", 2048), ("cc", 1024),
-               ("cid", 512), ("cwn", 2048), ("ke", 128), ("m2q", 1024), ("mq", 4096), ("qw", 256), ("qe", 128)):
+    _b("lin%d" % _t, 16, "uint16")
+    _b("el%d" % _t, 16, "uint16")
+for _n, _w in (("qx3", 256), ("qu", 128), ("qr", 640), ("qv", 128), ("wq", 512), ("qwr", 2048), ("kq", 768),
+               ("cid", 512), ("cwn", 2048), ("m1q", 256), ("m2q", 256), ("qw", 256), ("qe", 128)):
     _q(_n, _w)
-for _n, _w in (("xb", 1024), ("xs", 1024), ("xn", 1024), ("ub", 512), ("vb", 512), ("zero", 1024), ("cst", 3080), ("zc", 2600),
-               ("kb", 512), ("onesb", 128), ("halfb", 128), ("negb", 256), ("thr0", 256), ("thr1", 256), ("mt", 8192), ("m2", 4096),
-               ("dd", 8192), ("win", 4096), ("winh", 2048), ("fx", 1024), ("etmp", 512), ("eb", 512), ("ww", 1024),
-               ("ab", 256), ("da", 256), ("dn", 256), ("dat", 256)):
+for _n, _w in (("xb", 1024), ("xs", 1024), ("ub", 512), ("vb", 512), ("zero", 1024), ("zc", 2600), ("kb", 3072), ("onesb", 128),
+               ("halfb", 128), ("gcol", 128), ("colid", 128), ("rq", 256), ("eq", 512), ("cs", 512), ("mp", 1024), ("sb", 4096),
+               ("dd", 1024), ("m1", 1024), ("m2", 1024), ("win", 4096), ("winh", 2048), ("fx", 1024), ("etmp", 512),
+               ("eb", 512), ("ww", 1024), ("dat", 256)):
     _b(_n, _w, "bfloat16")
-for _n in ("mk16", "rs16", "mk4", "rs4", "msk", "scn", "psb", "awin", "it16", "it4", "dfull", "ysb", "cols", "itb", "leaf"):
+for _n in ("mk16", "rs16", "dw", "dv", "it16", "itb", "msk", "scn", "vv", "vs", "leaf", "c0s", "csort", "crow", "dfull", "ysb"):
     _b(_n, 256, "float32")
-_b("lw", 1024, "float32")
-_b("cf", 8, "float32")
-_b("kc", 16, "float32")
-for _n, _w in (("ci", 8), ("il", 128), ("il2", 128), ("il3", 128), ("xi", 64), ("xi2", 64), ("xi3", 64)):
+for _n, _w in (("lw", 1024), ("rr", 512), ("sw", 512), ("qp", 768), ("cf", 24), ("acc", 64), ("cw", 32), ("uu", 32), ("nx", 32),
+               ("smask", 32), ("sg", 32), ("sig", 32), ("w2", 32), ("iq", 16), ("tq", 16)):
+    _b(_n, _w, "float32")
+for _n, _w in (("ci", 8), ("il", 48), ("il2", 128), ("il3", 128), ("ir", 16), ("ic", 8), ("ki", 64), ("xi", 32)):
     _b(_n, _w, "int32")
-for _n, _w in (("ulist", 128), ("wlist", 128), ("n1l", 16), ("n2l", 16), ("pl", 16), ("ql", 16), ("xl", 64)):
+for _n, _w in (("ulist", 48), ("wlist", 128), ("rep", 16), ("cl", 8), ("nl", 32), ("kl", 48), ("pl", 16), ("ql", 16), ("xl", 16)):
     _b(_n, _w, "uint16")
 SCRATCH["ld"] = ("dram", [32, 1024], "float32")
-_b("pr0", 1024, "float32", "psum")
-_b("pr1", 1024, "float32", "psum")
-for _k in range(4, 8):
+for _k in range(8):
     _b("pb%d" % _k, 512, "float32", "psum")
 
-SAME = ((1, 1, 1, 2, 2, 2, 2, 2), (1, 0, 0, 0, 0, 0, 0, 0))
-OTHER = ((0, 1, 1, 1, 2, 2, 2, 2), (3, 2, 0, 0, 0, 0, 0, 0))
+BIG = 1e29
+STEP = 4096.0
+ON_V = (range(3, 13), range(4, 11))
 
 
 def rank_program(g, core, T, topo):
@@ -125,8 +124,6 @@ def rank_program(g, core, T, topo):
         op("V", V.quantize_mx, (T[name][:, a:b], T[name + "_s"][:, a:b], T[src][:, s0:s0 + 4 * (b - a)]), reads, [key])
 
     def bank(k, n):
-        if k < 4:
-            return T["pr%d" % (k // 2)][:, 512 * (k % 2):512 * (k % 2) + n]
         return T["pb%d" % k][:, 0:n]
 
     def mm(k, n, l, la, r, ra, start, stop, reads):
@@ -140,6 +137,9 @@ def rank_program(g, core, T, topo):
     def tt(out, a, b, o, reads, writes):
         op("V", V.tensor_tensor, (out, a, b, o), reads, writes)
 
+    def scan(out, d0, d1, init, o0, o1, reads, writes):
+        op("V", V.tensor_tensor_scan, (out, d0, d1, init, o0, o1), reads, writes)
+
     def vcopy(out, in_, reads, writes):
         op("V", V.tensor_copy, (out, in_), reads, writes)
 
@@ -149,8 +149,8 @@ def rank_program(g, core, T, topo):
     def memset(ap, c, writes, reads=()):
         op("V", V.memset, (ap, c), list(reads), writes)
 
-    def iota(name, pat, base, cm):
-        op("G", g.iota, (T[name][:], pat, base, cm), [], [name], allow_small_or_imprecise_dtypes=True)
+    def iota(name, pat, base, cm, a=0, b=None):
+        op("G", g.iota, (T[name][:, a:b], pat, base, cm), [], [name if b is None else (name, a)], allow_small_or_imprecise_dtypes=True)
 
     def select(out, in_, pat, cmp, base, cm, reads, writes):
         op("G", g.affine_select, (out, in_, pat, cmp, 0.0, base, cm), reads, writes)
@@ -161,115 +161,144 @@ def rank_program(g, core, T, topo):
     dmas("Y", [(T.wq_s[:], T.ws[:, :])], [], ["wqs"])
     dmas("Y", [(T.vb[:], T.v[:, :])], [], ["vb"])
 
-    iota("il", [[1, 2], [16, 8], [0, 8]], 0, 0)
+    C = {k: i for i, k in enumerate(("p", "l", "a0", "a1", "h", "g", "a", "m", "e0", "e1", "x0", "x1", "x2", "k0", "k1", "ramp",
+                                     "off", "t0", "t1", "t2", "t3", "t4", "t5", "t6"))}
+
+    def col(k):
+        return T.cf[:, C[k]:C[k] + 1]
+
+    def aff(k, src, scale, bias):
+        rd = [x for x in (src, scale, bias) if isinstance(x, str)]
+        act(col(k), col(src), F.Identity, ["cf"] + rd, [k], scale=col(scale) if isinstance(scale, str) else scale,
+            bias=col(bias) if isinstance(bias, str) else bias)
+
     iota("ci", [[0, 8]], 0, 1)
+    iota("il", [[1, 2], [16, 8]], 0, 0, 0, 16)
+    iota("it16", [[0, 16], [1, 16]], 0, 0)
+    iota("ir", [[16, 16]], 15, 0)
+    for s in (1, 2, 3):
+        iota("il", [[64, 2], [32 - 64 * (s // 2), 2], [16 - 32 * (s % 2), 2]], 16 * s, 0, 8 + 8 * s, 16 + 8 * s)
     memset(T.zero[:], 0.0, ["zero"])
-    memset(T.negb[:], -2.0 ** -120, ["negb"])
     memset(T.onesb[:], 1.0, ["onesb"])
     memset(T.halfb[:], 0.5, ["halfb"])
-    vcopy(T.ulist[:], T.il[:], ["il"], ["ulist"])
-    for b in range(2):
-        select(T["thr%d" % b][:], T.negb[:], [[1, 256]], A.is_ge, -1 - 128 * b, -1, ["negb"], ["thr%d" % b])
+    memset(T.acc[:], 0.0, ["acc"])
+    vcopy(T.ulist[:, 0:16], T.il[:, 0:16], [("il", 0)], ["ul0"])
+    for k, sh, an in (("l", 0, 15), ("a0", 4, 1), ("a1", 5, 1), ("h", 6, 1), ("g", 4, 7), ("a", 4, 3), ("m", 5, 3)):
+        ts(T.ci[:, C[k]:C[k] + 1], T.ci[:, 0:1], sh, A.logical_shift_right, ["ci"], ["ci" + k], an, A.bitwise_and)
+    vcopy(T.cf[:, 0:8], T.ci[:, 0:8], ["ci"] + ["ci" + k for k in ("l", "a0", "a1", "h", "g", "a", "m")], ["cf"])
+    ts(T.mk16[:], T.it16[:], col("l"), A.is_equal, ["it16", "cf"], ["mk16"])
+    ts(T.rs16[:], T.it16[:], 0.0, A.not_equal, ["it16"], ["rs16"])
+    vcopy(T.rep[:], T.ir[:], ["ir"], ["rep"])
+    vcopy(T.ulist[:, 16:40], T.il[:, 16:40], [("il", 16), ("il", 24), ("il", 32)], ["ul1"])
     for i in range(3):
         act(T.zc[:, 1024 * i:min(2600, 1024 * i + 1024)], T.zero[:, 0:min(1024, 2600 - 1024 * i)], F.Copy, ["zero"], ["zz%d" % i])
     zz = ["zz0", "zz1", "zz2"]
-    select(T.zc[:, 2084:2596:4], T.onesb[:], [[-1, 128]], A.is_equal, 0, 1, ["onesb"] + zz, ["zc4"])
-    for s in range(4):
-        select(T.zc[:, s * 520 + 4:s * 520 + 516:4], T.halfb[:], [[0, 4], [-64, 2], [-1, 16]], A.is_equal, -16 * s, 1, ["halfb"] + zz, ["zc%d" % s])
-    quant("qx0", 0, 256, "zero", "z0", ["zero"])
-    quant("qx0", 512, 768, "zero", "z0b", ["zero"])
+    act(T.rq[:], T.mk16[:], F.Copy, ["mk16"], ["rq"], scale=-1.0, bias=1.0)
+    act(T.dw[:], T.mk16[:], F.Copy, ["mk16"], ["dw"], scale=-BIG, bias=STEP)
+    act(T.dv[:], T.mk16[:], F.Copy, ["mk16"], ["dv"], scale=-BIG)
+    iota("gcol", [[1, 8], [0, 16]], 0, 0)
+    iota("colid", [[1, 128]], 0, 0)
     quant("qu", 0, 128, "ub", "qu", ["ub"])
 
-    def pick_u(a):
-        lst = T.ulist[:, a // 16:a // 16 + 32]
-        vcopy(T.qr[:, a:a + 512].bitcast(dt.uint32), T.qu[:, 0:128].bitcast(dt.uint32).indirect(lst), ["qu", "ulist"], [("qr", a // 512)])
-        act(T.qr_s[:, a:a + 512], T.qu_s[:, 0:128].indirect(lst), F.Copy, ["qu", "ulist"], [("qrs", a // 512)])
-    pick_u(0)
-    quant("qx0", 256, 512, "xb", ("qx", 0), ["xb"])
-    act(T.xn[:], T.xb[:], F.Copy, ["xb"], ["xn"], scale=-1.0)
+    def pick_u(a, b, key):
+        lst = T.ulist[:, a // 16:b // 16]
+        vcopy(T.qr[:, a:b].bitcast(dt.uint32), T.qu[:, 0:128].bitcast(dt.uint32).indirect(lst), ["qu", key], [("qr", a)])
+        act(T.qr_s[:, a:b], T.qu_s[:, 0:128].indirect(lst), F.Copy, ["qu", key], [("qrs", a)])
+    pick_u(0, 256, "ul0")
+    quant("qx0", 0, 256, "xb", ("qx", 0), ["xb"])
 
-    def col(c):
-        return T.cf[:, c:c + 1]
+    def setup_signs():
+        aff("e0", "a0", 2.0, -1.0)
+        aff("e1", "a1", 2.0, -1.0)
+        aff("x0", "e0", -1.0, "g")
+        aff("x1", "e1", -2.0, "g")
+        aff("x2", "e0", -1.0, "x1")
+        aff("ramp", "l", STEP, -15.0 * STEP)
+        aff("off", "a", 256.0, "ramp")
 
-    def kc(c):
-        return T.kc[:, c:c + 1]
+    def setup_search():
+        aff("t0", "l", 16.0, 7.5)
+        aff("t1", "l", 16.0, -120.0)
+        for i in range(2):
+            e = "e%d" % i
+            ts(T.ic[:, i:i + 1], col(e), 7.5, A.mult, [e, "t0"], [("ic", i)], col("t0"), A.add)
+            ts(T.ic[:, 2 + 2 * i:3 + 2 * i], col("t1"), col(e), A.mult, [e, "t1"], [("ic", 2 + i)], 135.0, A.add)
+            ts(T.smask[:, 16 * i:16 * i + 16], T.mk16[:, 0:16], col(e), A.mult, [e, "mk16"], [("smask", i)])
+            aff("t2", e, 7.5, 7.5)
+            ts(col("k%d" % i), col("l"), col("t2"), A.not_equal, ["cf", "t2"], ["k%d" % i])
+        vcopy(T.cl[:, 0:3], T.ic[:, 0:3], [("ic", i) for i in range(3)], ["cl0"])
+        vcopy(T.cl[:, 4:5], T.ic[:, 4:5], [("ic", 3)], ["cl1"])
+        memset(T.m1[:, 3:1024:4], 0.0, ["m1z"])
+        memset(T.m2[:, 3:1024:4], 0.0, ["m2z"])
 
-    def qrk(s, gr):
-        i = (8 * s + gr) // 4
-        return [("qr", i), ("qrs", i)]
+    def setup_counts():
+        for i in range(3):
+            act(T.kb[:, 1024 * i + 3:1024 * i + 1024:4], T.zero[:, 0:256], F.Copy, ["zero"], [("kbz", i)])
+        for t in range(3):
+            e, k, x = "e%d" % min(t, 1), "k%d" % min(t, 1), "x%d" % t
+            aff("t3", k, 16.0 ** t, 0.0)
+            ts(T.kb[:, t:512:4], T.gcol[:], col("g"), A.is_equal, ["gcol", "cf", "t3"], [("kb", 0, t)], col("t3"), A.mult)
+            ts(T.kb[:, 512 + t:1024:4], T.gcol[:], col(x), A.is_equal, ["gcol", x, e], [("kb", 1, t)], col(e), A.mult)
+            aff("t4", k, e, 0.0)
+            aff("t5", "t4", 16.0, 0.0)
+            ts(T.kb[:, 1024 + t:1536:4], T.gcol[:], col(x), A.is_equal, ["gcol", x, "t5"], [("kb", 2, t)], col("t5"), A.mult)
+            aff("t6", x, 16.0, 2.0 * t + 1.0)
+            ts(T.kb[:, 1536 + t:2048:4], T.colid[:], col("t6"), A.is_equal, ["colid", "t6", e], [("kb", 3, t)], col(e), A.mult)
+            aff("t6", x, 16.0, 2.0 * t)
+            ts(T.kb[:, 2048 + t:2560:4], T.colid[:], col("t6"), A.is_equal, ["colid", "t6", "t4"], [("kb", 4, t)], col("t4"), A.mult)
+        quant("kq", 0, 128, "kb", ("kq", 0), [("kb", 0, t) for t in range(3)] + [("kbz", 0)])
 
-    def setup_cols():
-        for c, sh, an in ((1, 0, 15), (2, 2, 3), (3, 0, 3), (4, 4, 3), (5, 0, 1), (6, 6, 1)):
-            ts(T.ci[:, c:c + 1], T.ci[:, 0:1], sh, A.logical_shift_right, ["ci"], ["ci%d" % c], an, A.bitwise_and)
-        vcopy(T.cf[:, 0:7], T.ci[:, 0:7], ["ci"] + ["ci%d" % c for c in range(1, 7)], ["cf"])
+    def setup_counts2():
+        quant("kq", 128, 640, "kb", ("kq", 1), [("kb", i, t) for i in range(1, 5) for t in range(3)] + [("kbz", i) for i in range(3)], s0=512)
+
+    def setup_merge():
+        ts(T.ic[:, 6:7], T.ci[:, 0:1], 1, A.bitwise_and, ["ci"], [("ic", 6)])
+        ts(col("t3"), T.ic[:, 6:7], -15.0, A.mult, [("ic", 6)], ["t3"], 16.0, A.add)
+        for t in range(4):
+            aff("t4", "h", 1.0, 2.0 * t)
+            ts(T.kb[:, 2560 + t:3072:4], T.gcol[:], col("t4"), A.is_equal, ["gcol", "t4", "t3", ("kbz", 2)], [("kb", 5, t)], col("t3"), A.mult)
+        quant("kq", 640, 768, "kb", ("kq", 5), [("kb", 5, t) for t in range(4)], s0=2560)
+        aff("t5", "l", 4.0 - STEP, "m")
+        act(T.iq[:], T.itb[:, 0:16], F.Identity, ["itb", "t5"], ["iq"], scale=64.0, bias=col("t5"))
+        act(T.iq[:], T.iq[:], F.Copy, ["iq"], ["iq"], bias=15.0 * STEP)
+        aff("t6", "a", 256.0, 0.0)
+        act(T.itb[:], T.itb[:], F.Identity, ["itb", "t6", "iq"], ["itb"], bias=col("t6"))
 
     def setup_pool():
-        iota("it16", [[0, 16], [1, 16]], 0, 0)
-        iota("it4", [[0, 64], [1, 4]], 0, 0)
-        for nm, q in (("rs16", 16), ("rs4", 4)):
-            iota(nm, [[0, 256]], 1, 0)
-            select(T[nm][:], T[nm][:], [[0, 256 // q], [1, q]], A.not_equal, 0, 0, [nm], [nm])
         iota("itb", [[1, 256]], 0, 0)
+        for s in range(4):
+            select(T.zc[:, s * 520 + 4:s * 520 + 516:4], T.halfb[:], [[0, 4], [-64, 2], [-1, 16]], A.is_equal, -16 * s, 1, ["halfb"] + zz, ["zc%d" % s])
+        select(T.zc[:, 2084:2596:4], T.onesb[:], [[-1, 128]], A.is_equal, 0, 1, ["onesb"] + zz, ["zc4"])
         iota("il2", [[32, 16], [16, 2], [0, 4]], 0, 0)
 
     def setup_windows(ss):
         for s in ss:
             for b in range(4):
-                a = 128 * (4 * s + b)
-                quant("cwn", a, a + 128, "zc", ("cwn", s, b), zz + ["zc%d" % s], s0=520 * s + 4 - b)
+                if s < 4:
+                    a = 128 * (4 * s + b)
+                    quant("cwn", a, a + 128, "zc", ("cwn", s, b), zz + ["zc%d" % s], s0=520 * s + 4 - b)
+                else:
+                    quant("cid", 128 * b, 128 * b + 128, "zc", ("cid", b), zz + ["zc4"], s0=2084 - b)
 
-    def setup_own():
-        for b in range(4):
-            quant("cid", 128 * b, 128 * b + 128, "zc", ("cid", b), zz + ["zc4"], s0=2084 - b)
-
-    def setup_ones():
-        memset(T.cst[:], 0.0, ["cst"])
-        memset(T.cst[:, 448:512], 1.0, ["cst8"], ["cst"])
-        for t in range(4):
-            if t < 2:
-                memset(T.cst[:, 1476 + t:1540:4], 1.0, ["cst%d" % t], ["cst"])
-            o = 2504 + 64 * (t // 2)
-            memset(T.cst[:, o + t:o + 64:4], 1.0 - 0.5 * (t % 2), ["cst%d" % (4 + t)], ["cst"])
-        for i, o in enumerate((0, 1028, 1026, 2056)):
-            quant("cc", 256 * i, 256 * i + 256, "cst", "cc%d" % (i // 2), ["cst", "cst0", "cst1", "cst4", "cst5", "cst6", "cst7", "cst8"], s0=o)
-
-    def setup_lists():
-        ts(T.mk16[:], T.it16[:], col(1), A.is_equal, ["it16", "cf"], ["mk16"])
-        ts(T.mk4[:], T.it4[:], col(2), A.is_equal, ["it4", "cf"], ["mk4"])
-        ts(kc(1), col(1), 0.0, A.is_equal, ["cf"], ["kc1"], 32.0, A.mult)
-        ts(kc(2), col(1), 1.0, A.is_equal, ["cf"], ["kc2"])
-        tt(kc(3), kc(1), kc(2), A.add, ["kc1", "kc2"], ["kc3"])
-        tt(kc(5), kc(3), col(6), A.mult, ["kc3", "cf"], ["kc5"])
-        tt(kc(4), kc(3), kc(5), A.subtract, ["kc3", "kc5"], ["kc4"])
-        memset(T.kb[:], 0.0, ["kb"])
-        for q in range(8):
-            ts(T.kb[:, 64 * q + q // 2:64 * q + 64:4], T.onesb[:, 0:16], kc(4 + q % 2), A.mult,
-               ["onesb", "kc4", "kc5", "kb"], ["kb%d" % q])
-        quant("ke", 0, 128, "kb", "ke", ["kb"] + ["kb%d" % q for q in range(8)])
-        act(kc(6), col(3), F.Copy, ["cf"], ["kc6"], scale=1024.0)
-        act(kc(7), col(3), F.Copy, ["cf"], ["kc7"], scale=512.0)
-        act(kc(8), col(4), F.Copy, ["cf"], ["kc8"], scale=8.0, bias=-208.0)
-        act(kc(9), kc(8), F.Copy, ["kc8"], ["kc9"], scale=-1.0, bias=6128.0)
-        act(kc(10), col(5), F.Identity, ["kc8", "kc9", "cf"], ["kc10"], scale=kc(9), bias=kc(8))
-        act(kc(11), col(5), F.Copy, ["cf"], ["kc11"], scale=-33.0, bias=1.0)
-        act(kc(12), col(4), F.Copy, ["cf"], ["kc12"], scale=256.0)
-        act(T.itb[:], T.itb[:], F.Identity, ["itb", "kc12"], ["itb"], bias=kc(12))
-        ts(T.il3[:], T.il2[:], col(1), A.add, ["il2", "cf"], ["il3"])
+    def setup_w():
+        ts(T.il3[:], T.il2[:], col("l"), A.add, ["il2", "cf"], ["il3"])
         vcopy(T.wlist[:], T.il3[:], ["il3"], ["wlist"])
-        for t in (1, 2):
-            dmas("Y", [(cv("qx%d" % t, a, a + 256), cv("qx0", a, a + 256)) for a in (0, 512)] +
-                 [(T["qx%d_s" % t][:, a:a + 256], T.qx0_s[:, a:a + 256]) for a in (0, 512)], ["z0", "z0b"], ["z%d" % t])
+        for b in range(4):
+            a, lst = 512 * b, T.wlist[:, 32 * b:32 * b + 32]
+            vcopy(T.qwr[:, a:a + 512].bitcast(dt.uint32), T.wq[:, 0:512].bitcast(dt.uint32).indirect(lst), ["wq", "wlist"], [("qwr", b)])
+            act(T.qwr_s[:, a:a + 512], T.wq_s[:, 0:512].indirect(lst), F.Copy, ["wqs", "wlist"], [("qwrs", b)])
 
-    def wrap(src, mk, rs, srckeys):
-        tt(T.msk[:], src, T[mk][:], A.mult, srckeys + [mk], ["msk"])
-        op("V", V.tensor_tensor_scan, (T.scn[:], T[rs][:], T.msk[:], 0.0, A.mult, A.add), [rs, "msk"], ["scn"])
+    def wrap(src, keys):
+        scan(T.scn[:], T.dw[:], src, 0.0, A.add, A.max, keys + ["dw"], ["scn"])
+        return T.scn[:, 15:256:16]
 
     for t in range(R):
         qx = "qx%d" % t
         X = ("qx", t)
-        zk = ["z0", "z0b"] if t == 0 else ["z%d" % t]
-        remote(cv("land%d" % t, 0, 256), cv(qx, 256, 512), "arr%d" % t, [X])
-        remote(T["land%d_s" % t][:], T[qx + "_s"][:, 256:512], "arr%d" % t, [X])
+        remote(cv("land%d" % t, 0, 256), cv(qx, 0, 256), "arr%d" % t, [X])
+        remote(T["land%d_s" % t][:], T[qx + "_s"][:], "arr%d" % t, [X])
+        if t == 0:
+            setup_pool()
         iota("ww", [[0, 1024]], 0, 0)
         land, lin = "land%d" % t, "lin%d" % t
         lastw[land] = ("arr%d" % t, 2 * n_in)
@@ -277,235 +306,232 @@ def rank_program(g, core, T, topo):
         total["arr%d" % t] = 2 * n_in
         total["lst%d" % t] = n_in
 
-        for b in range(2):
-            mm((4, 7)[b], 128, qx, 256 + 128 * b, "qu", 0, True, True, [X, "qu"])
+        u0, u1 = [("qr", 0), ("qrs", 0)], [("qr", 256), ("qrs", 256)]
+        mm(0, 256, "qr", 0, qx, 0, True, True, [X] + u0)
+        mm(1, 256, "qr", 0, qx, 0, True, True, [X] + u0)
+        mm(2, 256, "qr", 128, qx, 0, True, True, [X] + u0)
 
-        def rows(h, i):
-            for j in range(2):
-                gr = 4 * h + 2 * i + j
-                mm(2 * h + i, 512, "qr", 128 * gr, qx, 256 - 256 * j, j == 0, j == 1, [X] + zk + qrk(0, gr))
-        rows(0, 0)
-        for b in range(2):
-            vcopy(T.cols[:, 128 * b:128 * b + 128], bank((4, 7)[b], 128), [("K", (4, 7)[b])], [("cols", b)])
-        quant("qn", 0, 256, "xn", "qn", ["xn"] if t == 0 else [("xn", 0), ("xn", 1)])
-        flip = {"V": 0, "S": 0}
+        def row(s):
+            return T.rr[:, 256 * s:256 * s + 256]
 
-        def diff(e, s, gr, b, lo):
-            k = {"V": (5, 6), "S": (7, 4)}[e][flip[e] % 2]
-            flip[e] += 1
-            a = 128 * (8 * s + gr)
-            mm(k, 128, "qr", a, "qn", lo, True, False, qrk(s, gr) + ["qn"])
-            mm(k, 128, qx, 256 + 128 * b, "qr", a, False, True, qrk(s, gr) + [X])
-            return k
+        def mine(s, c):
+            return T.sw[:, 256 * s + 16 * c + 15:256 * s + 16 * c + 16]
 
-        pairs = [(gr, b) for gr in range(8) for b in range(2)]
-        same, other = list(pairs), list(pairs)
-        s2k = [("m2", gr, b, i) for gr, b in pairs for i in range(2)]
+        def lanes(s, src, keys):
+            tt(T.msk[:], src, T.mk16[:], A.mult, keys + ["mk16"], ["msk"])
+            scan(T.sw[:, 256 * s:256 * s + 256], T.rs16[:], T.msk[:], 0.0, A.mult, A.add, ["rs16", "msk"], [("sw", s)])
 
-        def s2_same(n):
-            for gr, b in same[:n]:
-                k = diff("V", 1, gr, b, 128 * b)
-                o = 1024 * (gr // 2) + 512 * b
-                tt(T.m2[:, o + 2 * (gr % 2):o + 512:4], bank(k, 128), T["thr%d" % b][:, 128 * b:128 * b + 128], A.is_gt,
-                   [("K", k), "thr%d" % b], [("m2", gr, b, 0)])
-            del same[:n]
+        def ties(s):
+            o = 256 * s
+            tt(T.eq[:, o:o + 256], T.sw[:, o:o + 256].indirect(T.rep[:, 0:16]), row(s), A.is_equal, [("sw", s), "rep", ("rr", s)], [("eq", s)])
+            scan(T.cs[:, o:o + 256], T.rq[:], T.eq[:, o:o + 256], 0.0, A.mult, A.add, ["rq", ("eq", s)], [("cs", s)])
+            ts(T.cw[:, 16 * s:16 * s + 16], T.cs[:, o + 15:o + 256:16], -2.0, A.mult, [("cs", s)], [("cw", s)])
 
-        def s2_other(n):
-            for gr, b in other[:n]:
-                k = diff("S", 1, gr, b, 128 - 128 * b)
-                o = 1024 * (gr // 2) + 512 - 512 * b
-                act(T.m2[:, o + 2 * (gr % 2) + 1:o + 512:4], bank(k, 128), F.Sign, [("K", k)], [("m2", gr, b, 1)],
-                    bias=(1 - 2 * b) * 2.0 ** -120)
-            del other[:n]
+        flip = [0, 0]
+        owed = []
 
-        def sign(h, k):
-            c = 128 * (k % 2) + 16 * (4 * h + k // 2)
-            for a, n in ((0, 1), (1, 1)) if h + k == 0 else ((0, 2),):
-                act(T.dd[:, 1024 * k + 512 * a:1024 * k + 512 * (a + n)], T["pr%d" % h][:, 512 * a:512 * (a + n)], F.Sign,
-                    [("K", 2 * h + i) for i in range(a, a + n)] + [("cols", k % 2)], [("dd", k, i) for i in range(a, a + n)],
-                    scale=-1.0, bias=T.cols[:, c:c + 1])
+        def sum_v():
+            if owed:
+                s, c, o = owed.pop(0)
+                a = 2048 * s + 128 * c
+                scan(T.sb[:, a:a + 128], T.mp[:, o:o + 128], T.mp[:, o + 128:o + 256], T.cw[:, 16 * s + c:16 * s + c + 1], A.add, A.add,
+                     [("mp", o, 0), ("mp", o, 1), ("cw", s)], [("sb", s, c), ("mp", o)])
 
-        def fix(h, k):
-            b, tq, base, dg = k % 2, k % 4, 4096 * (k // 4), 128 * k
-            dk = [("dd", k, 0), ("dd", k, 1)]
-            if dg:
-                ts(T.mt[:, base + tq:base + 4 * dg:4], T.dd[:, 1024 * k:1024 * k + dg], 0.0, A.is_gt, dk, [("mt", k, 0)])
-            if dg + 128 < 1024:
-                ts(T.mt[:, base + 4 * (dg + 128) + tq:base + 4096:4], T.dd[:, 1024 * k + dg + 128:1024 * k + 1024], 0.0, A.is_ge, dk, [("mt", k, 1)])
-            kk = diff("V", 0, 4 * h + k // 2, b, 128 * b)
-            tt(T.mt[:, base + 4 * dg + tq:base + 4 * (dg + 128):4], bank(kk, 128), T["thr%d" % b][:, 128 * b:128 * b + 128], A.is_gt,
-               [("K", kk), "thr%d" % b], [("mt", k, 2)])
+        def pass_v(s, cs):
+            for c in cs:
+                o, e = 256 * (flip[0] % 4), 16 * c + 16
+                flip[0] += 1
+                rd = [("rr", s), ("sw", s), ("mp", o)]
+                ts(T.mp[:, o:o + e], T.rr[:, 256 * s:256 * s + e], mine(s, c), A.is_ge, rd, [("mp", o, 0)], 2.0, A.mult)
+                ts(T.mp[:, o + e:o + 256], T.rr[:, 256 * s + e:256 * s + 256], mine(s, c), A.is_gt, rd, [("mp", o, 1)], 2.0, A.mult)
+                if len(owed) > 1:
+                    sum_v()
+                owed.append((s, c, o))
 
-        def qm(h, i):
-            m0 = 1024 * (2 * h + i)
-            for a in (0, 512):
-                quant("mq", m0 + a, m0 + a + 512, "mt", ("mq", h, i, a), [("mt", k, e) for k in range(4 * i, 4 * i + 4) for e in range(3)],
-                      s0=4096 * i + 4 * a)
+        owes = []
 
-        def count(h, i, gis, first=False, last=False):
-            m0 = 1024 * (2 * h + i)
-            for gi in gis:
-                gr = 4 * h + gi
-                mk = [("mq", h, i, 512 * (gi // 2)), "cc0", "cc1"]
-                if gi // 2 == i:
-                    mm(1, 256, "cc", 256 * (1 + gi % 2) + 112 - 16 * gr, "mq", m0 + 256 * gi, first and gi % 2 == 0, last and gi % 2 == 1, mk)
-            for gi in gis:
-                gr = 4 * h + gi
-                mk = [("mq", h, i, 512 * (gi // 2)), "cc0", "cc1"]
-                mm(0, 256, "cc", 112 - 16 * gr, "mq", m0 + 256 * gi, first and gi == 0, last and gi == 3, mk)
+        def sum_s():
+            if owes:
+                s, c, o = owes.pop(0)
+                e = 16 * c + 16
+                act(T.dd[:, o:o + e], T.dd[:, o:o + e], F.Sign, [("dd", o), "acc"], [("acc", s, c, 0), ("dd", o, 0)], scale=-1.0, bias=0.5,
+                    accum_out=T.acc[:, 32 * s + c:32 * s + c + 1])
+                if e < 256:
+                    act(T.dd[:, o + e:o + 256], T.dd[:, o + e:o + 256], F.Sign, [("dd", o), "acc"], [("acc", s, c, 1), ("dd", o, 1)],
+                        scale=-1.0, bias=-0.5, accum_out=T.acc[:, 32 * s + 16 + c:32 * s + 17 + c])
 
-        wins = [(s, b) for s in range(4) for b in range(4)] + [(4, b) for b in range(4)]
+        def pass_s(s, cs):
+            for c in cs:
+                o = 256 * (flip[1] % 4)
+                flip[1] += 1
+                act(T.dd[:, o:o + 256], row(s), F.Sign, [("rr", s), ("sw", s), ("dd", o, 0), ("dd", o, 1)], [("dd", o)], scale=-1.0, bias=mine(s, c))
+                sum_s()
+                owes.append((s, c, o))
+
+        def numbers_s(s):
+            u = T.uu[:, 16 * s:16 * s + 16]
+            tt(u, T.acc[:, 32 * s:32 * s + 16], T.acc[:, 32 * s + 16:32 * s + 32], A.add,
+               [("acc", s, c, i) for c in range(16) for i in range(2)] + ["acc"], [("uu", s)])
+            tt(u, u, T.cw[:, 16 * s:16 * s + 16], A.add, [("uu", s), ("cw", s)], [("uu", s)])
+            ts(T.nl[:, 16 * s:16 * s + 16], u, 0.5, A.mult, [("uu", s)], [("nl", s)], 128.0, A.add)
+
+        def numbers_v(s):
+            a, b = ON_V[s][0], ON_V[s][-1] + 1
+            ts(T.nl[:, 16 * s + a:16 * s + b], T.sb[:, 2048 * s + 128 * a + 127:2048 * s + 128 * b:128], 0.5, A.mult,
+               [("sb", s, c) for c in ON_V[s]], [("nl", s)])
+
+        def raised(s):
+            ts(T.nx[:, 16 * s:16 * s + 16], T.nl[:, 16 * s:16 * s + 16], col("off"), A.add, [("nl", s), "off"], [("nx", s)])
+
+        on_s = [[c for c in range(16) if c not in ON_V[s]] for s in range(2)]
+        v1, v2 = list(ON_V[0]), list(ON_V[1])
+        lanes(0, bank(0, 256), [("K", 0)])
+        act(row(0), bank(1, 256), F.Copy, [("K", 1)], [("rr", 0)])
+        act(row(1), bank(2, 256), F.Copy, [("K", 2)], [("rr", 1)])
+        if t == 0:
+            pick_u(256, 640, "ul1")
+            setup_signs()
+        for s in range(3):
+            mm(4 + s, 256, "qr", 256 + 128 * s, qx, 0, True, True, [X] + u1)
+        ties(0)
+        pass_s(0, on_s[0])
+        sum_s()
+        pass_v(0, v1[:4])
+        lanes(1, bank(2, 256), [("K", 2)])
+        if t == 0:
+            setup_search()
+        pass_v(0, v1[4:])
+        for s in range(3):
+            act(T.qp[:, 256 * s:256 * s + 256], bank(4 + s, 256), F.Copy, [("K", 4 + s), "e0", "e1"], [("qp", s)], scale=col("e%d" % min(s, 1)))
+        pass_s(1, on_s[1][:2])
+        sum_v()
+        numbers_s(0)
+        sum_v()
+        numbers_v(0)
+
+        vcopy(T.vv[:, 0:256].indirect(T.nl[:, 0:16]), row(0), [("nl", 0), ("rr", 0)], ["vv"])
+        tt(T.sg[:], T.vv[:, 0:256].indirect(T.cl[:, 0:2]), T.smask[:], A.mult, ["vv", "cl0", ("smask", 0), ("smask", 1)], ["sg"])
+        scan(T.vs[:], T.dv[:], T.vv[:], 0.0, A.add, A.max, ["dv", "vv"], ["vs"])
+        scan(T.sig[:], T.rs16[:, 0:32], T.sg[:], 0.0, A.mult, A.add, ["rs16", "sg"], ["sig"])
+        if t == 0:
+            setup_counts()
+        for i in range(2):
+            act(T.w2[:, 16 * i:16 * i + 16], T.vs[:, 0:256].indirect(T.cl[:, 2 + 2 * i:3 + 2 * i]), F.Copy, ["vs", "cl0", "cl1", "e%d" % i],
+                [("w2", i)], scale=col("e%d" % i))
+        pass_s(1, on_s[1][2:])
+        sum_s()
+        for s in range(3):
+            i = 16 * min(s, 1) + 15
+            ts(T.m1[:, s:1024:4], T.qp[:, 256 * s:256 * s + 256], T.sig[:, i:i + 1], A.is_lt, [("qp", s), "sig"], [("m1", s)])
+        quant("m1q", 0, 256, "m1", "m1q", [("m1", s) for s in range(3)] + ["m1z"])
+        mm(7, 256, "kq", 0, "m1q", 0, True, True, [("kq", 0), "m1q"])
+        ties(1)
+        raised(0)
+        if t == 0:
+            setup_counts2()
+        ts(T.ki[:, 48:64], wrap(bank(7, 256), [("K", 7)]), col("ramp"), A.add, ["scn", "ramp"], ["kp"])
+        pass_v(1, v2[:1])
+        for s in range(3):
+            ts(T.ki[:, 16 * s:16 * s + 16], T.ki[:, 48:64], 4 * s, A.logical_shift_right, ["kp"], [("ki", s)], 15, A.bitwise_and)
+        pass_v(1, v2[1:2])
+        vcopy(T.kl[:], T.ki[:, 0:48], [("ki", s) for s in range(3)], ["kl"])
+        pass_v(1, v2[2:3])
+        for s in range(3):
+            i = 16 * min(s, 1)
+            tt(T.m2[:, s:1024:4], T.w2[:, i:i + 16].indirect(T.kl[:, 16 * s:16 * s + 16]), T.qp[:, 256 * s:256 * s + 256], A.is_gt,
+               [("w2", min(s, 1)), "kl", ("qp", s)], [("m2", s)])
+        quant("m2q", 0, 256, "m2", "m2q", [("m2", s) for s in range(3)] + ["m2z"])
+        for k, a in ((0, 128), (1, 384), (4, 128)):
+            mm(k, 256, "kq", a + 128, "m1q", 0, True, False, [("kq", 1), "m1q"])
+            mm(k, 256, "kq", a, "m2q", 0, False, True, [("kq", 1), "m2q"])
+        pass_v(1, v2[3:])
+        sum_v()
+        numbers_s(1)
+        sum_v()
+        numbers_v(1)
+        if t == 0:
+            setup_merge()
+        vcopy(T.leaf[:, 0:256].indirect(T.nl[:, 16:32]), T.itb[:], ["itb", ("nl", 1)], ["leaf"])
+        dmas("Y", [(T.ld[16 * (q // 4):16 * (q // 4) + 16, 256 * (q % 4):256 * (q % 4) + 256], T.leaf[16 * q:16 * q + 16, :]) for q in range(8)], ["leaf"], ["ld"])
+        dmas("Y", [(T.lw[16 * q:16 * q + 16, :], T.ld[16 * (q % 2):16 * (q % 2) + 16, :]) for q in range(8)], ["ld"], ["lw"])
+
+        wins = [(s, b) for b in range(4) for s in range(4)] + [(4, b) for b in range(4)]
         wn = [0]
-        pend = []
 
-        def win_mm(n):
+        def windows(n):
             for _i in range(n):
                 if wins:
                     s, b = wins.pop(0)
-                    k = (7, 2, 3, 5, 6)[wn[0] % 5]
+                    k = (2, 3, 6, 7)[wn[0] % 4]
                     wn[0] += 1
                     if s < 4:
                         mm(k, 256, "cwn", 128 * (4 * s + b), land, 0, True, True, [land, ("cwn", s, b)])
-                    else:
-                        mm(k, 256, "cid", 128 * b, qx, 256, True, True, [X, ("cid", b)])
-                    pend.append((k, s, b))
-
-        def win_cp(n):
-            for _i in range(n):
-                if pend:
-                    k, s, b = pend.pop(0)
-                    if s < 4:
                         o = 1024 * b + 256 * s
                         act(T.win[:, o:o + 256], bank(k, 256), F.Copy, [("K", k)], [("win", s, b)])
                     else:
-                        act(T.fx[:, b:1024:4], bank(k, 256), F.Copy, [("K", k)], [("fx", b)])
+                        mm(k, 256, "cid", 128 * b, qx, 0, True, True, [X, ("cid", b)])
+                        act(T.fx[:, 256 * b:256 * b + 256], bank(k, 256), F.Copy, [("K", k)], [("fx", b)])
 
+        act(T.dat[:], bank(1, 256), F.Copy, [("K", 1)], ["dat"])
+        act(T.c0s[:], bank(4, 256), F.Copy, [("K", 4)], ["c0s"])
+        tt(T.tq[:], wrap(bank(0, 256), [("K", 0)]), T.nx[:, 0:16], A.add, ["scn", ("nx", 0)], ["tq"])
         if t == 0:
-            rows(0, 1)
-            sign(0, 0)
-            pick_u(1024)
-            s2_same(2)
-            setup_cols()
-            setup_windows((0, 1))
-            setup_pool()
-        else:
-            s2_same(1)
-            rows(0, 1)
-            s2_same(1)
-        for k in range(8):
-            if t or k:
-                sign(0, k)
-            if t == 0 and k in (1, 2):
-                pick_u(1024 * k - 512)
-            s2_other(OTHER[0][k])
-            if k in (2, 4):
-                rows(1, k // 2 - 1)
-            s2_same(SAME[0][k])
-            fix(0, k)
-            if t == 0 and 2 < k < 7:
-                (setup_ones, lambda: setup_windows((2,)), lambda: setup_windows((3,)), setup_own)[k - 3]()
-            if k % 4 == 3:
-                qm(0, k // 4)
+            setup_windows((0,))
+        vcopy(T.pl[:], T.tq[:], ["tq"], ["pl"])
         if t == 0:
-            setup_lists()
-        for k in range(8):
-            sign(1, k)
-            s2_other(OTHER[1][k])
-            s2_same(SAME[1][k])
-            fix(1, k)
-            if k == 1:
-                for a in (0, 512):
-                    quant("m2q", a, a + 512, "m2", ("m2q", a), s2k, s0=4 * a)
-            if k == 2:
-                for q in range(4):
-                    mm(4, 256, "cc", 768 + 112 - 32 * q, "m2q", 256 * q, q == 0, q == 3, [("m2q", 512 * (q // 2)), "cc1"])
-            if k == 3:
-                count(0, 0, range(4), True)
-                qm(1, 0)
-                wrap(bank(4, 256), "mk16", "rs16", [("K", 4)])
-                ts(T.n2l[:], T.scn[:, 15:256:16], 64.0, A.add, ["scn"], ["n2l"])
-                vcopy(T.leaf[:, 0:256].indirect(T.n2l[:, 0:16]), T.itb[:], ["itb", "n2l"], ["leaf"])
-                dmas("Y", [(T.ld[16 * (q // 4):16 * (q // 4) + 16, 256 * (q % 4):256 * (q % 4) + 256], T.leaf[16 * q:16 * q + 16, :]) for q in range(8)], ["leaf"], ["ld"])
-                dmas("Y", [(T.lw[16 * q:16 * q + 16, :], T.ld[16 * (q % 2):16 * (q % 2) + 16, :]) for q in range(8)], ["ld"], ["lw"])
-            if k == 4:
-                count(0, 1, range(4))
-            if k == 5:
-                count(1, 0, range(4))
-        qm(1, 1)
-        win_mm(3)
-        count(1, 1, (0, 1))
-        win_cp(3)
-        count(1, 1, (2, 3), last=True)
-
-        act(T.ab[:], bank(1, 256), F.Copy, [("K", 1)], ["ab"], scale=0.03125, bias=191.515625)
-        act(T.da[:], T.ab[:], F.Identity, ["ab", "kc10", "kc11"], ["da"], scale=kc(11), bias=kc(10))
-        act(T.dn[:], bank(1, 256), F.Copy, [("K", 1), "cf"], ["dn"], scale=col(5))
-        wrap(bank(0, 256), "mk16", "rs16", [("K", 0)])
-        vcopy(T.pl[:], T.scn[:, 15:256:16], ["scn"], ["pl"])
-        tt(T.dat[:], T.dn[:], T.da[:], A.add, ["dn", "da"], ["dat"])
+            setup_windows((1,))
         vcopy(T.ww[:, 0:1024].indirect(T.pl[:, 0:16]), T.dat[:], ["pl", "dat"], ["ww"])
+        if t:
+            windows(4)
         quant("qw", 0, 256, "ww", "qw", ["ww"])
-        win_mm(5)
-        mm(4, 256, "ke", 0, "qw", 0, True, True, ["ke", "qw"])
-        win_cp(5)
-        while wins or pend:
-            win_mm(3)
-            win_cp(3)
-        wrap(bank(4, 256), "mk16", "rs16", [("K", 4)])
-        ts(T.ql[:], T.scn[:, 15:256:16], 528.0, A.add, ["scn"], ["ql"])
-        wrap(T.lw[:, 0:1024].indirect(T.ql[:, 0:16]), "mk4", "rs4", ["lw", "ql"])
+        mm(5, 256, "kq", 640, "qw", 0, True, True, [("kq", 5), "qw"])
+        if t == 0:
+            setup_windows((2, 3, 4))
+        windows(20)
+        raised(1)
+        tt(T.tq[:], T.iq[:], wrap(bank(5, 256), [("K", 5)]), A.subtract, ["scn", "iq"], ["tq"])
+        vcopy(T.ql[:], T.tq[:], ["tq"], ["ql"])
+        vcopy(T.csort[:, 0:256].indirect(T.nl[:, 0:16]), T.c0s[:], [("nl", 0), "c0s"], ["csort"])
+        vcopy(T.crow[:], T.lw[:, 0:1024].indirect(T.ql[:, 0:16]), ["lw", "ql"], ["crow"])
         el = "el%d" % t
-        ts(T[el][:], T.scn[:, 3:256:4], kc(6), A.add, ["scn", "kc6"], [el])
+        ts(T[el][:], wrap(T.crow[:], ["crow"]), col("ramp"), A.add, ["scn", "ramp"], [el])
         remote(T[lin][:], T[el][:], "lst%d" % t, [el])
 
-        wrap(bank(1, 256), "mk16", "rs16", [("K", 1)])
-        vcopy(T.n1l[:], T.scn[:, 15:256:16], ["scn"], ["n1l"])
-        vcopy(T.psb[:], bank(0, 256), [("K", 0)], ["psb"])
-        vcopy(T.awin[:, 0:256].indirect(T.n1l[:, 0:16]), T.psb[:], ["n1l", "psb"], ["awin"])
-        wrap(T.awin[:, 0:256].indirect(T.n2l[:, 0:16]), "mk4", "rs4", ["awin", "n2l"])
+        vcopy(T.crow[:], T.csort[:, 0:256].indirect(T.nl[:, 16:32]), ["csort", ("nl", 1)], ["crow"])
+        tt(T.xi[:, 0:16], wrap(T.crow[:], ["crow"]), T.nx[:, 16:32], A.add, ["scn", ("nx", 1)], ["xi"])
+        ts(T.xi[:, 16:32], T.xi[:, 0:16], 511, A.bitwise_and, ["xi"], ["xi2"])
+        vcopy(T.xl[:], T.xi[:, 16:32], ["xi2"], ["xl"])
         if t == R - 1:
-            vcopy(T.dfull[:], T.awin[:, 0:256].indirect(T.n2l[:, 0:16]), ["awin", "n2l"], ["dfull"])
-            ts(T.dfull[:], T.dfull[:], 2.0, A.mult, ["dfull", "cf"], ["dfull"], col(6), A.add)
+            tt(T.msk[:], T.csort[:], T.itb[:], A.add, ["csort", "itb"], ["msk"])
+            ts(T.dfull[:], T.msk[:, 0:256].indirect(T.nl[:, 16:32]), 2.0, A.mult, ["msk", ("nl", 1), "cf"], ["dfull"], col("h"), A.add)
             dmas("Y", [(T.op[q:q + 1, :], T.dfull[16 * q:16 * q + 1, :]) for q in range(8)], ["dfull"], ["op"])
             quant("qv", 0, 128, "vb", "qv", ["vb"])
         if t == 0:
-            vcopy(T.qwr[:].bitcast(dt.uint32), T.wq[:, 0:512].bitcast(dt.uint32).indirect(T.wlist[:, 0:128]), ["wq", "wlist"], ["qwr"])
-            act(T.qwr_s[:], T.wq_s[:, 0:512].indirect(T.wlist[:, 0:128]), F.Copy, ["wqs", "wlist"], ["qwrs"])
+            setup_w()
 
-        wk = [("win", s, b) for s in range(4) for b in range(4)] + [lin]
-        for i in range(2):
-            act(T.etmp[:, 256 * i:256 * i + 256], T.win[:, 0:4096].indirect(T[lin][:, 16 * i:16 * i + 16]), F.Copy, wk, [("etmp", i)])
-            tt(T.eb[:, 256 * i:256 * i + 256], T.win[:, 0:4096].indirect(T[lin][:, 32 + 16 * i:48 + 16 * i]), T.etmp[:, 256 * i:256 * i + 256], A.add,
-               wk + [("etmp", i)], [("eb", i)])
-        quant("qe", 0, 128, "eb", "qe", [("eb", 0), ("eb", 1)])
-        vcopy(T.xi[:], T.scn[:, 3:256:4], ["scn"], ["xi"])
-        ts(T.xi2[:], T.xi[:], 2, A.logical_shift_right, ["xi"], ["xi2"], 127, A.bitwise_and)
-        ts(T.xi3[:], T.xi[:], 3, A.bitwise_and, ["xi"], ["xi3"])
-        ts(T.xi3[:], T.xi3[:], 128.0, A.mult, ["xi3", "kc7"], ["xi3"], kc(7), A.add)
-        tt(T.xi2[:], T.xi2[:], T.xi3[:], A.add, ["xi2", "xi3"], ["xi2"])
-        vcopy(T.xl[:], T.xi2[:], ["xi2"], ["xl"])
+        for b in range(4):
+            wk = [("win", s, b) for s in range(4)] + [lin]
+            w = T.win[:, 1024 * b:1024 * b + 1024]
+            act(T.etmp[:, 128 * b:128 * b + 128], w.indirect(T[lin][:, 0:8]), F.Copy, wk, [("etmp", b)])
+            tt(T.eb[:, b:512:4], w.indirect(T[lin][:, 8:16]), T.etmp[:, 128 * b:128 * b + 128], A.add, wk + [("etmp", b)], [("eb", b)])
+        quant("qe", 0, 128, "eb", "qe", [("eb", b) for b in range(4)])
         for i in range(16):
-            k, s, b = i % 8, i // 4, i % 4
-            mm(k, 128, "qwr", 128 * (4 * b + s), "qe", 0, True, True, ["qwr", "qwrs", "qe"])
-            o = 512 * b + 128 * s
-            if i % 2:
-                ts(T.winh[:, o:o + 128], bank(k, 128), 0.015625, A.mult, [("K", k)], [("winh", i)])
+            k, b, s = i % 8, i // 4, i % 4
+            mm(k, 128, "qwr", 128 * i, "qe", 0, True, True, [("qwr", b), ("qwrs", b), "qe"])
+            out = T.winh[:, 512 * b + s:512 * b + 512:4]
+            if i in (1, 3, 7, 11):
+                ts(out, bank(k, 128), 0.015625, A.mult, [("K", k)], [("winh", i)])
             else:
-                act(T.winh[:, o:o + 128], bank(k, 128), F.Copy, [("K", k)], [("winh", i)], scale=0.015625)
-        hk = [("winh", i) for i in range(16)] + ["xl"] + [("fx", b) for b in range(4)]
-        for i in range(2):
-            c = 512 * i
-            tt(T.xs[:, c:c + 512], T.winh[:, 0:2048].indirect(T.xl[:, 32 * i:32 * i + 32]), T.fx[:, c:c + 512], A.add, hk, [("xs", i)])
-            if t < R - 1:
-                act(T.xn[:, c:c + 512], T.xs[:, c:c + 512], F.Copy, [("xs", i)], [("xn", i), "xn"] if t == 0 else [("xn", i)], scale=-1.0)
-        if t < R - 1:
-            quant("qx%d" % (t + 1), 256, 512, "xs", ("qx", t + 1), [("xs", 0), ("xs", 1)])
-        else:
-            quant("qx3", 0, 256, "xs", "qx3", [("xs", 0), ("xs", 1)])
+                act(out, bank(k, 128), F.Copy, [("K", k)], [("winh", i)], scale=0.015625)
+            if s == 3:
+                tt(T.xs[:, b:1024:4], T.winh[:, 512 * b:512 * b + 512].indirect(T.xl[:, 0:16]), T.fx[:, 256 * b:256 * b + 256], A.add,
+                   [("winh", 4 * b + j) for j in range(4)] + ["xl", ("fx", b)], [("xs", b)])
+        quant("qx%d" % (t + 1), 0, 256, "xs", ("qx", t + 1), [("xs", b) for b in range(4)])
 
-    mm(0, 256, "qv", 0, "qx3", 0, True, True, ["qv", "qx3"])
-    dmas("Y", [(T.oc[:, :], cv("qx3", 0, 256))], ["qx3"], ["oc"])
-    dmas("S", [(T.osc[4 * k:4 * k + 4, :], T.qx3_s[32 * k:32 * k + 4, 0:256]) for k in range(4)], ["qx3"], ["osc"])
+    X = ("qx", R)
+    mm(0, 256, "qv", 0, "qx3", 0, True, True, ["qv", X])
+    dmas("Y", [(T.oc[:, :], cv("qx3", 0, 256))], [X], ["oc"])
+    dmas("S", [(T.osc[4 * k:4 * k + 4, :], T.qx3_s[32 * k:32 * k + 4, 0:256]) for k in range(4)], [X], ["osc"])
     vcopy(T.ysb[:], bank(0, 256), [("K", 0)], ["ysb"])
     dmas("Y", [(T.y[:, :], T.ysb[:])], ["ysb"], ["y"])
     total["ls"] = nrem[0] * n_eng

@@ -19,31 +19,31 @@ for _t in range(R):
     _q("qx%d" % _t, 256)
     _q("land%d" % _t, 256)
     _b("lin%d" % _t, 16, "uint16")
-    _b("el%d" % _t, 16, "uint16")
-for _n, _w in (("qx3", 256), ("qu", 128), ("qr", 640), ("qv", 128), ("wq", 512), ("qwr", 2048), ("kq", 768),
-               ("cid", 512), ("cwn", 2048), ("m1q", 256), ("m2q", 256), ("qw", 256), ("qe", 128)):
+for _n, _w in (("qx3", 256), ("qu", 128), ("qr", 640), ("qv", 128), ("wq", 512), ("qwr", 2048), ("kq", 896), ("mq", 1408),
+               ("cid", 512), ("m1q", 256), ("m2q", 256), ("qw", 256), ("qe", 128)):
     _q(_n, _w)
-for _n, _w in (("xb", 1024), ("xs", 1024), ("ub", 512), ("vb", 512), ("zero", 1024), ("zc", 2600), ("kb", 3072), ("onesb", 128),
-               ("halfb", 128), ("gcol", 128), ("colid", 128), ("rq", 256), ("eq", 512), ("cs", 512), ("mp", 1024), ("sb", 4096),
-               ("dd", 1024), ("m1", 1024), ("m2", 1024), ("win", 4096), ("winh", 2048), ("fx", 1024), ("etmp", 512),
+for _n, _w in (("xb", 1024), ("xs", 1024), ("ub", 512), ("vb", 512), ("zero", 1024), ("zc", 528), ("kb", 3584), ("onesb", 128),
+               ("gcol", 224), ("colid", 136), ("it16", 256), ("msks", 1280), ("cs", 512), ("mt", 5632), ("sb", 4096),
+               ("dd", 1024), ("m1", 1024), ("m2", 1024), ("win", 4096), ("winh", 2048), ("fx", 1024), ("fp", 1024), ("etmp", 512),
                ("eb", 512), ("ww", 1024), ("dat", 256)):
     _b(_n, _w, "bfloat16")
-for _n in ("mk16", "rs16", "dw", "dv", "it16", "itb", "msk", "scn", "vv", "vs", "leaf", "c0s", "csort", "crow", "dfull", "ysb"):
+for _n in ("itb", "scn", "vv", "vs", "leaf", "c0s", "csort", "crow", "dfull", "ysb"):
     _b(_n, 256, "float32")
-for _n, _w in (("lw", 1024), ("rr", 512), ("sw", 512), ("qp", 768), ("cf", 24), ("acc", 64), ("cw", 32), ("uu", 32), ("nx", 32),
-               ("smask", 32), ("sg", 32), ("sig", 32), ("w2", 32), ("iq", 16), ("tq", 16)):
+for _n, _w in (("lw", 1024), ("rr", 512), ("rm", 512), ("sw", 512), ("qp", 768), ("cf", 48), ("acc", 32), ("bd", 32), ("uu", 32),
+               ("nf", 32), ("nx", 32), ("smask", 32), ("sg", 32), ("sig", 32), ("w2", 32), ("iq", 32), ("tq", 16)):
     _b(_n, _w, "float32")
-for _n, _w in (("ci", 8), ("il", 48), ("il2", 128), ("il3", 128), ("ir", 16), ("ic", 8), ("ki", 64), ("xi", 32)):
+for _n, _w in (("ci", 16), ("il", 48), ("il2", 128), ("il3", 128), ("ir", 32), ("ki", 64), ("xi", 32)):
     _b(_n, _w, "int32")
-for _n, _w in (("ulist", 48), ("wlist", 128), ("rep", 16), ("cl", 8), ("nl", 32), ("kl", 48), ("pl", 16), ("ql", 16), ("xl", 16)):
+for _n, _w in (("ulist", 48), ("wlist", 128), ("rep", 16), ("cl", 8), ("nl", 32), ("kl", 48), ("pl", 16), ("ql", 16), ("xl", 16), ("el", 48)):
     _b(_n, _w, "uint16")
-SCRATCH["ld"] = ("dram", [32, 1024], "float32")
 for _k in range(8):
     _b("pb%d" % _k, 512, "float32", "psum")
 
 BIG = 1e29
 STEP = 4096.0
-ON_V = (range(3, 13), range(4, 11))
+ON_S = (range(7, 13), range(1, 13))
+M_AT, M_COLS = (0, 256, 448, 576), (256, 192, 128, 128)
+H_ON_V = (1, 3, 5, 7, 11)
 
 
 def rank_program(g, core, T, topo):
@@ -149,55 +149,75 @@ def rank_program(g, core, T, topo):
     def memset(ap, c, writes, reads=()):
         op("V", V.memset, (ap, c), list(reads), writes)
 
-    def iota(name, pat, base, cm, a=0, b=None):
-        op("G", g.iota, (T[name][:, a:b], pat, base, cm), [], [name if b is None else (name, a)], allow_small_or_imprecise_dtypes=True)
+    def iota(ap, key, pat, base, cm):
+        op("G", g.iota, (ap, pat, base, cm), [], [key], allow_small_or_imprecise_dtypes=True)
 
     def select(out, in_, pat, cmp, base, cm, reads, writes):
         op("G", g.affine_select, (out, in_, pat, cmp, 0.0, base, cm), reads, writes)
 
+    def spread(e, dst, src, n, reads):
+        dmas(e, [(T[dst][16 * q:16 * q + 16, n * a:n * a + n], T[src][64 * (q % 2) + 16 * a:64 * (q % 2) + 16 * a + 16, :])
+                 for q in range(8) for a in range(4)], reads, [dst])
+
     dmas("S", [(T.ub[:], T.u[:, :])], [], ["ub"])
     dmas("Y", [(T.xb[:], T.x[:, :])], [], ["xb"])
+
+    names = ("p", "l", "a0", "a1", "h", "g", "a", "m", "odd", "e0", "e1", "x0", "x1", "x2", "y0", "y1", "y2", "ramp", "off", "t0", "t1",
+             "s0", "s1", "w0", "pad", "w1", "n0", "n1", "k0", "k1", "ke0", "ke1", "kf0", "kf1", "kg", "kh", "wm", "iqb", "ak", "bb", "hh")
+    C = {k: i for i, k in enumerate(names)}
+
+    def col(k, n=1, step=1):
+        return T.cf[:, C[k]:C[k] + (n - 1) * step + 1:step]
+
+    def aff(k, src, scale, bias, n=1, step=1):
+        rd = [x for x in (scale, bias) if isinstance(x, str)] + [names[C[src] + i] for i in range(n)]
+        act(col(k, n, step), col(src, n), F.Identity, ["cf"] + rd, [names[C[k] + i * step] for i in range(n)],
+            scale=col(scale) if isinstance(scale, str) else scale, bias=col(bias) if isinstance(bias, str) else bias)
+
+    def msk(k, n=256):
+        return T.msks[:, 256 * k:256 * k + n]
+
+    iota(T.ci[:, 0:9], "ci", [[0, 9]], 0, 1)
+    iota(T.il[:, 0:16], ("il", 0), [[1, 2], [16, 8]], 0, 0)
+    iota(T.it16[:], "it16", [[0, 16], [1, 16]], 0, 0)
+    iota(T.ir[:, 0:16], "ir", [[16, 16]], 15, 0)
+    for s in (1, 2, 3):
+        iota(T.il[:, 8 + 8 * s:16 + 8 * s], ("il", s), [[64, 2], [32 - 64 * (s // 2), 2], [16 - 32 * (s % 2), 2]], 16 * s, 0)
+    iota(T.gcol[:], "gcol", [[1, 14], [0, 16]], -6, 0)
+    iota(T.colid[:], "colid", [[1, 136]], -5, 0)
+    iota(T.ir[:, 16:32], "ir2", [[64, 16]], 0, 0)
+    memset(T.zero[:], 0.0, ["zero"])
+    memset(T.cf[:], 0.0, ["cf"])
+    for k, sh, an in (("l", 0, 15), ("a0", 4, 1), ("a1", 5, 1), ("h", 6, 1), ("g", 4, 7), ("a", 4, 3), ("m", 5, 3), ("odd", 0, 1)):
+        ts(T.ci[:, C[k]:C[k] + 1], T.ci[:, 0:1], sh, A.logical_shift_right, ["ci"], ["ci" + k], an, A.bitwise_and)
+    vcopy(T.cf[:, 0:9], T.ci[:, 0:9], ["ci"] + ["ci" + k for k in names[1:9]], ["cf"])
+    vcopy(T.ulist[:, 0:16], T.il[:, 0:16], [("il", 0)], ["ul0"])
+    tails = [(4 * (M_AT[i] + (M_COLS[i] - 48 if i < 3 else 16)), 4 * (M_AT[i] + M_COLS[i])) for i in range(4)]
+    for i, (a, b) in enumerate(tails):
+        memset(T.mt[:, a:b], 0.0, [("mz", 0, i)])
+    memset(T.sb[:, 127:4096:2048], 0.0, ["sbz"])
+    memset(T.onesb[:], 1.0, ["onesb"])
+    ts(msk(0), T.it16[:], col("l"), A.is_gt, ["it16", "cf"], [("msk", 0)], BIG, A.mult)
+    ts(msk(1), T.it16[:], col("l"), A.is_equal, ["it16", "cf"], [("msk", 1)], BIG, A.mult)
+    ts(msk(4), T.it16[:], 0.0, A.not_equal, ["it16"], [("msk", 4)])
+    vcopy(T.rep[:], T.ir[:, 0:16], ["ir"], ["rep"])
+    vcopy(T.ulist[:, 16:40], T.il[:, 16:40], [("il", s) for s in (1, 2, 3)], ["ul1"])
     dmas("Y", [(cv("wq", 0, 512), T.wc[:, :])], [], ["wq"])
     dmas("Y", [(T.wq_s[:], T.ws[:, :])], [], ["wqs"])
+    dmas("Y", [(T.mt[:, 2816 + a:2816 + b], T.zero[:, 0:b - a]) for a, b in tails], ["zero"], [("mz", 1, i) for i in range(4)])
+    dmas("Y", [(T.kb[:, a:b], T.zero[:, 0:b - a]) for a, b in ((512, 1536), (1536, 2560), (2560, 3072))], ["zero"], ["kbz"])
+    dmas("Y", [(T.zc[:], T.zero[:, 0:528])], ["zero"], ["zz"])
     dmas("Y", [(T.vb[:], T.v[:, :])], [], ["vb"])
-
-    C = {k: i for i, k in enumerate(("p", "l", "a0", "a1", "h", "g", "a", "m", "e0", "e1", "x0", "x1", "x2", "k0", "k1", "ramp",
-                                     "off", "t0", "t1", "t2", "t3", "t4", "t5", "t6"))}
-
-    def col(k):
-        return T.cf[:, C[k]:C[k] + 1]
-
-    def aff(k, src, scale, bias):
-        rd = [x for x in (src, scale, bias) if isinstance(x, str)]
-        act(col(k), col(src), F.Identity, ["cf"] + rd, [k], scale=col(scale) if isinstance(scale, str) else scale,
-            bias=col(bias) if isinstance(bias, str) else bias)
-
-    iota("ci", [[0, 8]], 0, 1)
-    iota("il", [[1, 2], [16, 8]], 0, 0, 0, 16)
-    iota("it16", [[0, 16], [1, 16]], 0, 0)
-    iota("ir", [[16, 16]], 15, 0)
-    for s in (1, 2, 3):
-        iota("il", [[64, 2], [32 - 64 * (s // 2), 2], [16 - 32 * (s % 2), 2]], 16 * s, 0, 8 + 8 * s, 16 + 8 * s)
-    memset(T.zero[:], 0.0, ["zero"])
-    memset(T.onesb[:], 1.0, ["onesb"])
-    memset(T.halfb[:], 0.5, ["halfb"])
-    memset(T.acc[:], 0.0, ["acc"])
-    vcopy(T.ulist[:, 0:16], T.il[:, 0:16], [("il", 0)], ["ul0"])
-    for k, sh, an in (("l", 0, 15), ("a0", 4, 1), ("a1", 5, 1), ("h", 6, 1), ("g", 4, 7), ("a", 4, 3), ("m", 5, 3)):
-        ts(T.ci[:, C[k]:C[k] + 1], T.ci[:, 0:1], sh, A.logical_shift_right, ["ci"], ["ci" + k], an, A.bitwise_and)
-    vcopy(T.cf[:, 0:8], T.ci[:, 0:8], ["ci"] + ["ci" + k for k in ("l", "a0", "a1", "h", "g", "a", "m")], ["cf"])
-    ts(T.mk16[:], T.it16[:], col("l"), A.is_equal, ["it16", "cf"], ["mk16"])
-    ts(T.rs16[:], T.it16[:], 0.0, A.not_equal, ["it16"], ["rs16"])
-    vcopy(T.rep[:], T.ir[:], ["ir"], ["rep"])
-    vcopy(T.ulist[:, 16:40], T.il[:, 16:40], [("il", 16), ("il", 24), ("il", 32)], ["ul1"])
-    for i in range(3):
-        act(T.zc[:, 1024 * i:min(2600, 1024 * i + 1024)], T.zero[:, 0:min(1024, 2600 - 1024 * i)], F.Copy, ["zero"], ["zz%d" % i])
-    zz = ["zz0", "zz1", "zz2"]
-    act(T.rq[:], T.mk16[:], F.Copy, ["mk16"], ["rq"], scale=-1.0, bias=1.0)
-    act(T.dw[:], T.mk16[:], F.Copy, ["mk16"], ["dw"], scale=-BIG, bias=STEP)
-    act(T.dv[:], T.mk16[:], F.Copy, ["mk16"], ["dv"], scale=-BIG)
-    iota("gcol", [[1, 8], [0, 16]], 0, 0)
-    iota("colid", [[1, 128]], 0, 0)
+    aff("e0", "a0", 2.0, -1.0, 2)
+    aff("ramp", "l", STEP, -15.0 * STEP)
+    aff("bb", "l", STEP + 1.0, -15.0 * STEP - 15.0)
+    aff("x0", "e0", -1.0, "g")
+    aff("x1", "e1", -2.0, "g")
+    aff("off", "a", 256.0, "ramp")
+    aff("t0", "l", 16.0, 7.5)
+    aff("t1", "l", 16.0, -120.0)
+    aff("x2", "e0", -1.0, "x1")
+    aff("n0", "e0", 7.5, 7.5, 2)
     quant("qu", 0, 128, "ub", "qu", ["ub"])
 
     def pick_u(a, b, key):
@@ -206,100 +226,96 @@ def rank_program(g, core, T, topo):
         act(T.qr_s[:, a:b], T.qu_s[:, 0:128].indirect(lst), F.Copy, ["qu", key], [("qrs", a)])
     pick_u(0, 256, "ul0")
     quant("qx0", 0, 256, "xb", ("qx", 0), ["xb"])
+    aff("s0", "e0", 7.5, "t0", 2)
+    aff("w0", "e0", "t1", 135.0, 2, 2)
+    aff("y0", "x0", 16.0, 0.0, 3)
+    aff("wm", "odd", -15.0, 16.0)
+    aff("iqb", "l", 4.0 - STEP, "m")
+    aff("ak", "a", 1024.0, 0.0)
+    aff("hh", "a", -1536.0, "h")
 
-    def setup_signs():
-        aff("e0", "a0", 2.0, -1.0)
-        aff("e1", "a1", 2.0, -1.0)
-        aff("x0", "e0", -1.0, "g")
-        aff("x1", "e1", -2.0, "g")
-        aff("x2", "e0", -1.0, "x1")
-        aff("ramp", "l", STEP, -15.0 * STEP)
-        aff("off", "a", 256.0, "ramp")
+    def gcol(shift=0):
+        return T.gcol[:, 96 - 16 * shift:224 - 16 * shift]
+
+    def ktile(i, t, src, k, w):
+        ts(T.kb[:, 512 * i + t:512 * i + 512:4], src, col(k), A.is_equal, ["gcol", "colid", "cf", "kbz" if 0 < i < 6 else "cf", k] + ([w] if w else []),
+           [("kb", i, t)], *((col(w), A.mult) if w else ()))
+
+    def kquant(a, b):
+        quant("kq", 128 * a, 128 * b, "kb", ("kq", a), [("kb", i, t) for i in range(a, b) for t in range(4)], s0=512 * a)
+
+    def setup_ones():
+        for t in range(4):
+            ktile(0, t, gcol(), "g", None)
+        kquant(0, 1)
+        ts(msk(2), msk(1), -1.0, A.mult, [("msk", 1)], [("msk", 2)])
+        ts(msk(3), msk(1), -1.0, A.mult, [("msk", 1)], [("msk", 3)], STEP, A.add)
+        ts(T.iq[:, 16:32], T.ir[:, 0:16], col("bb"), A.add, ["ir", "bb"], ["ib"])
 
     def setup_search():
-        aff("t0", "l", 16.0, 7.5)
-        aff("t1", "l", 16.0, -120.0)
+        vcopy(T.cl[:, 0:5], col("s0", 5), ["s0", "s1", "w0", "w1"], ["cl"])
         for i in range(2):
-            e = "e%d" % i
-            ts(T.ic[:, i:i + 1], col(e), 7.5, A.mult, [e, "t0"], [("ic", i)], col("t0"), A.add)
-            ts(T.ic[:, 2 + 2 * i:3 + 2 * i], col("t1"), col(e), A.mult, [e, "t1"], [("ic", 2 + i)], 135.0, A.add)
-            ts(T.smask[:, 16 * i:16 * i + 16], T.mk16[:, 0:16], col(e), A.mult, [e, "mk16"], [("smask", i)])
-            aff("t2", e, 7.5, 7.5)
-            ts(col("k%d" % i), col("l"), col("t2"), A.not_equal, ["cf", "t2"], ["k%d" % i])
-        vcopy(T.cl[:, 0:3], T.ic[:, 0:3], [("ic", i) for i in range(3)], ["cl0"])
-        vcopy(T.cl[:, 4:5], T.ic[:, 4:5], [("ic", 3)], ["cl1"])
-        memset(T.m1[:, 3:1024:4], 0.0, ["m1z"])
-        memset(T.m2[:, 3:1024:4], 0.0, ["m2z"])
+            ts(T.smask[:, 16 * i:16 * i + 16], T.it16[:, 0:16], col("l"), A.is_equal, ["it16", "e%d" % i], [("smask", i)], col("e%d" % i), A.mult)
+        ts(col("k0", 2), col("n0", 2), col("l"), A.not_equal, ["cf", "n0", "n1"], ["k0", "k1"])
+        tt(col("ke0", 2), col("k0", 2), col("e0", 2), A.mult, ["k0", "k1", "e0", "e1"], ["ke0", "ke1"])
+        ts(col("kg"), col("k1"), 16.0, A.mult, ["k1"], ["kg"])
+        ts(col("kh"), col("k1"), 256.0, A.mult, ["k1"], ["kh"])
+        ts(col("kf0", 2), col("ke0", 2), 16.0, A.mult, ["ke0", "ke1"], ["kf0", "kf1"])
+        for t in range(3):
+            ktile(1, t, gcol(), "g", ("k0", "kg", "kh")[t])
+        kquant(1, 2)
 
     def setup_counts():
-        for i in range(3):
-            act(T.kb[:, 1024 * i + 3:1024 * i + 1024:4], T.zero[:, 0:256], F.Copy, ["zero"], [("kbz", i)])
         for t in range(3):
-            e, k, x = "e%d" % min(t, 1), "k%d" % min(t, 1), "x%d" % t
-            aff("t3", k, 16.0 ** t, 0.0)
-            ts(T.kb[:, t:512:4], T.gcol[:], col("g"), A.is_equal, ["gcol", "cf", "t3"], [("kb", 0, t)], col("t3"), A.mult)
-            ts(T.kb[:, 512 + t:1024:4], T.gcol[:], col(x), A.is_equal, ["gcol", x, e], [("kb", 1, t)], col(e), A.mult)
-            aff("t4", k, e, 0.0)
-            aff("t5", "t4", 16.0, 0.0)
-            ts(T.kb[:, 1024 + t:1536:4], T.gcol[:], col(x), A.is_equal, ["gcol", x, "t5"], [("kb", 2, t)], col("t5"), A.mult)
-            aff("t6", x, 16.0, 2.0 * t + 1.0)
-            ts(T.kb[:, 1536 + t:2048:4], T.colid[:], col("t6"), A.is_equal, ["colid", "t6", e], [("kb", 3, t)], col(e), A.mult)
-            aff("t6", x, 16.0, 2.0 * t)
-            ts(T.kb[:, 2048 + t:2560:4], T.colid[:], col("t6"), A.is_equal, ["colid", "t6", "t4"], [("kb", 4, t)], col("t4"), A.mult)
-        quant("kq", 0, 128, "kb", ("kq", 0), [("kb", 0, t) for t in range(3)] + [("kbz", 0)])
-
-    def setup_counts2():
-        quant("kq", 128, 640, "kb", ("kq", 1), [("kb", i, t) for i in range(1, 5) for t in range(3)] + [("kbz", i) for i in range(3)], s0=512)
+            i = min(t, 1)
+            ktile(2, t, gcol(), "x%d" % t, "e%d" % i)
+            ktile(3, t, gcol(), "x%d" % t, "kf%d" % i)
+            ktile(4, t, T.colid[:, 4 - 2 * t:132 - 2 * t], "y%d" % t, "e%d" % i)
+            ktile(5, t, T.colid[:, 5 - 2 * t:133 - 2 * t], "y%d" % t, "ke%d" % i)
+        kquant(2, 6)
 
     def setup_merge():
-        ts(T.ic[:, 6:7], T.ci[:, 0:1], 1, A.bitwise_and, ["ci"], [("ic", 6)])
-        ts(col("t3"), T.ic[:, 6:7], -15.0, A.mult, [("ic", 6)], ["t3"], 16.0, A.add)
         for t in range(4):
-            aff("t4", "h", 1.0, 2.0 * t)
-            ts(T.kb[:, 2560 + t:3072:4], T.gcol[:], col("t4"), A.is_equal, ["gcol", "t4", "t3", ("kbz", 2)], [("kb", 5, t)], col("t3"), A.mult)
-        quant("kq", 640, 768, "kb", ("kq", 5), [("kb", 5, t) for t in range(4)], s0=2560)
-        aff("t5", "l", 4.0 - STEP, "m")
-        act(T.iq[:], T.itb[:, 0:16], F.Identity, ["itb", "t5"], ["iq"], scale=64.0, bias=col("t5"))
-        act(T.iq[:], T.iq[:], F.Copy, ["iq"], ["iq"], bias=15.0 * STEP)
-        aff("t6", "a", 256.0, 0.0)
-        act(T.itb[:], T.itb[:], F.Identity, ["itb", "t6", "iq"], ["itb"], bias=col("t6"))
+            ktile(6, t, gcol(2 * t), "h", "wm")
+        kquant(6, 7)
+        ts(T.iq[:, 0:16], T.ir[:, 16:32], col("iqb"), A.add, ["ir2", "iqb"], ["iq"], 15.0 * STEP, A.add)
 
     def setup_pool():
-        iota("itb", [[1, 256]], 0, 0)
-        for s in range(4):
-            select(T.zc[:, s * 520 + 4:s * 520 + 516:4], T.halfb[:], [[0, 4], [-64, 2], [-1, 16]], A.is_equal, -16 * s, 1, ["halfb"] + zz, ["zc%d" % s])
-        select(T.zc[:, 2084:2596:4], T.onesb[:], [[-1, 128]], A.is_equal, 0, 1, ["onesb"] + zz, ["zc4"])
-        iota("il2", [[32, 16], [16, 2], [0, 4]], 0, 0)
+        iota(T.m1[:, 3:1024:4], "m1z", [[0, 256]], 0, 0)
+        iota(T.m2[:, 3:1024:4], "m2z", [[0, 256]], 0, 0)
+        iota(T.itb[:], "itb", [[1, 256]], 0, 0)
+        select(T.zc[:, 4:516:4], T.onesb[:], [[-1, 128]], A.is_equal, 0, 1, ["onesb", "zz"], ["zc"])
+        iota(T.il2[:], "il2", [[32, 16], [16, 2], [0, 4]], 0, 0)
 
-    def setup_windows(ss):
-        for s in ss:
-            for b in range(4):
-                if s < 4:
-                    a = 128 * (4 * s + b)
-                    quant("cwn", a, a + 128, "zc", ("cwn", s, b), zz + ["zc%d" % s], s0=520 * s + 4 - b)
-                else:
-                    quant("cid", 128 * b, 128 * b + 128, "zc", ("cid", b), zz + ["zc4"], s0=2084 - b)
+    def setup_unpack():
+        for b in range(4):
+            quant("cid", 128 * b, 128 * b + 128, "zc", ("cid", b), ["zz", "zc"], s0=4 - b)
 
-    def setup_w():
+    def setup_wlist():
         ts(T.il3[:], T.il2[:], col("l"), A.add, ["il2", "cf"], ["il3"])
         vcopy(T.wlist[:], T.il3[:], ["il3"], ["wlist"])
-        for b in range(4):
+
+    def setup_w(e, bs):
+        for b in bs:
             a, lst = 512 * b, T.wlist[:, 32 * b:32 * b + 32]
-            vcopy(T.qwr[:, a:a + 512].bitcast(dt.uint32), T.wq[:, 0:512].bitcast(dt.uint32).indirect(lst), ["wq", "wlist"], [("qwr", b)])
-            act(T.qwr_s[:, a:a + 512], T.wq_s[:, 0:512].indirect(lst), F.Copy, ["wqs", "wlist"], [("qwrs", b)])
+            if e == "V":
+                vcopy(T.qwr[:, a:a + 512].bitcast(dt.uint32), T.wq[:, 0:512].bitcast(dt.uint32).indirect(lst), ["wq", "wlist"], [("qwr", b)])
+            else:
+                act(T.qwr_s[:, a:a + 512], T.wq_s[:, 0:512].indirect(lst), F.Copy, ["wqs", "wlist"], [("qwrs", b)])
 
     def wrap(src, keys):
-        scan(T.scn[:], T.dw[:], src, 0.0, A.add, A.max, keys + ["dw"], ["scn"])
+        scan(T.scn[:], msk(3), src, 0.0, A.add, A.max, keys + [("msk", 3)], ["scn"])
         return T.scn[:, 15:256:16]
 
     for t in range(R):
         qx = "qx%d" % t
         X = ("qx", t)
+        first = t == 0
         remote(cv("land%d" % t, 0, 256), cv(qx, 0, 256), "arr%d" % t, [X])
         remote(T["land%d_s" % t][:], T[qx + "_s"][:], "arr%d" % t, [X])
-        if t == 0:
+        if first:
             setup_pool()
-        iota("ww", [[0, 1024]], 0, 0)
+        iota(T.ww[:], "ww", [[0, 1024]], 0, 0)
         land, lin = "land%d" % t, "lin%d" % t
         lastw[land] = ("arr%d" % t, 2 * n_in)
         lastw[lin] = ("lst%d" % t, n_in)
@@ -307,224 +323,232 @@ def rank_program(g, core, T, topo):
         total["lst%d" % t] = n_in
 
         u0, u1 = [("qr", 0), ("qrs", 0)], [("qr", 256), ("qrs", 256)]
-        mm(0, 256, "qr", 0, qx, 0, True, True, [X] + u0)
-        mm(1, 256, "qr", 0, qx, 0, True, True, [X] + u0)
-        mm(2, 256, "qr", 128, qx, 0, True, True, [X] + u0)
+        for k in range(4):
+            mm(k, 256, "qr", 128 * (k // 2), qx, 0, True, True, [X] + u0)
 
-        def row(s):
-            return T.rr[:, 256 * s:256 * s + 256]
+        def part(name, s):
+            return T[name][:, 256 * s:256 * s + 256]
 
         def mine(s, c):
             return T.sw[:, 256 * s + 16 * c + 15:256 * s + 16 * c + 16]
 
-        def lanes(s, src, keys):
-            tt(T.msk[:], src, T.mk16[:], A.mult, keys + ["mk16"], ["msk"])
-            scan(T.sw[:, 256 * s:256 * s + 256], T.rs16[:], T.msk[:], 0.0, A.mult, A.add, ["rs16", "msk"], [("sw", s)])
+        def slot(s, c, a, b):
+            o = 2816 * s + 4 * M_AT[(16 - c) // 4] + (16 - c) % 4
+            return T.mt[:, o + 4 * a:o + 4 * b - 3:4]
 
-        def ties(s):
-            o = 256 * s
-            tt(T.eq[:, o:o + 256], T.sw[:, o:o + 256].indirect(T.rep[:, 0:16]), row(s), A.is_equal, [("sw", s), "rep", ("rr", s)], [("eq", s)])
-            scan(T.cs[:, o:o + 256], T.rq[:], T.eq[:, o:o + 256], 0.0, A.mult, A.add, ["rq", ("eq", s)], [("cs", s)])
-            ts(T.cw[:, 16 * s:16 * s + 16], T.cs[:, o + 15:o + 256:16], -2.0, A.mult, [("cs", s)], [("cw", s)])
+        def lanes(s):
+            tt(part("rm", s), bank(2 * s, 256), msk(0), A.add, [("K", 2 * s), ("msk", 0)], [("rm", s)])
+            scan(part("sw", s), msk(1), part("rm", s), 0.0, A.add, A.min, [("msk", 1), ("rm", s)], [("sw", s)])
 
-        flip = [0, 0]
-        owed = []
+        def near(s):
+            tt(slot(s, 16, 0, 256), part("sw", s).indirect(T.rep[:, 0:16]), part("rm", s), A.is_gt,
+               [("sw", s), "rep", ("rm", s), ("mz", s, 0)], [("mt", s, 16)])
 
-        def sum_v():
-            if owed:
-                s, c, o = owed.pop(0)
-                a = 2048 * s + 128 * c
-                scan(T.sb[:, a:a + 128], T.mp[:, o:o + 128], T.mp[:, o + 128:o + 256], T.cw[:, 16 * s + c:16 * s + c + 1], A.add, A.add,
-                     [("mp", o, 0), ("mp", o, 1), ("cw", s)], [("sb", s, c), ("mp", o)])
+        def near_sum(s):
+            scan(part("cs", s), msk(4), slot(s, 16, 0, 256), 0.0, A.mult, A.add, [("msk", 4), ("mt", s, 16)], [("cs", s)])
 
         def pass_v(s, cs):
             for c in cs:
-                o, e = 256 * (flip[0] % 4), 16 * c + 16
-                flip[0] += 1
-                rd = [("rr", s), ("sw", s), ("mp", o)]
-                ts(T.mp[:, o:o + e], T.rr[:, 256 * s:256 * s + e], mine(s, c), A.is_ge, rd, [("mp", o, 0)], 2.0, A.mult)
-                ts(T.mp[:, o + e:o + 256], T.rr[:, 256 * s + e:256 * s + 256], mine(s, c), A.is_gt, rd, [("mp", o, 1)], 2.0, A.mult)
-                if len(owed) > 1:
-                    sum_v()
-                owed.append((s, c, o))
+                ts(slot(s, c, 0, 16 * c), T.rr[:, 256 * s:256 * s + 16 * c], mine(s, c), A.is_lt,
+                   [("rr", s), ("sw", s), ("mz", s, (16 - c) // 4)], [("mt", s, c)])
 
-        owes = []
+        def sum_v(s, cs):
+            for c in cs:
+                a = 2048 * s + 128 * c + 128
+                scan(T.sb[:, a - 8 * c:a], slot(s, c, 0, 8 * c), slot(s, c, 8 * c, 16 * c), 0.0, A.add, A.add, [("mt", s, c)], [("sb", s, c)])
+
+        flip, owes = [0], []
 
         def sum_s():
             if owes:
                 s, c, o = owes.pop(0)
-                e = 16 * c + 16
-                act(T.dd[:, o:o + e], T.dd[:, o:o + e], F.Sign, [("dd", o), "acc"], [("acc", s, c, 0), ("dd", o, 0)], scale=-1.0, bias=0.5,
-                    accum_out=T.acc[:, 32 * s + c:32 * s + c + 1])
-                if e < 256:
-                    act(T.dd[:, o + e:o + 256], T.dd[:, o + e:o + 256], F.Sign, [("dd", o), "acc"], [("acc", s, c, 1), ("dd", o, 1)],
-                        scale=-1.0, bias=-0.5, accum_out=T.acc[:, 32 * s + 16 + c:32 * s + 17 + c])
+                act(slot(s, c, 0, 16 * c), T.dd[:, o:o + 16 * c], F.Relu, [("dd", o), ("mz", s, (16 - c) // 4)], [("acc", s, c), ("mt", s, c)],
+                    accum_out=T.acc[:, 16 * s + c:16 * s + c + 1])
 
         def pass_s(s, cs):
             for c in cs:
-                o = 256 * (flip[1] % 4)
-                flip[1] += 1
-                act(T.dd[:, o:o + 256], row(s), F.Sign, [("rr", s), ("sw", s), ("dd", o, 0), ("dd", o, 1)], [("dd", o)], scale=-1.0, bias=mine(s, c))
+                o = 256 * (flip[0] % 4)
+                flip[0] += 1
+                act(T.dd[:, o:o + 16 * c], T.rr[:, 256 * s:256 * s + 16 * c], F.Sign, [("rr", s), ("sw", s)], [("dd", o)], scale=-1.0, bias=mine(s, c))
                 sum_s()
                 owes.append((s, c, o))
 
-        def numbers_s(s):
-            u = T.uu[:, 16 * s:16 * s + 16]
-            tt(u, T.acc[:, 32 * s:32 * s + 16], T.acc[:, 32 * s + 16:32 * s + 32], A.add,
-               [("acc", s, c, i) for c in range(16) for i in range(2)] + ["acc"], [("uu", s)])
-            tt(u, u, T.cw[:, 16 * s:16 * s + 16], A.add, [("uu", s), ("cw", s)], [("uu", s)])
-            ts(T.nl[:, 16 * s:16 * s + 16], u, 0.5, A.mult, [("uu", s)], [("nl", s)], 128.0, A.add)
+        def mquant(s, i, j):
+            a, b = M_AT[i], M_AT[j - 1] + M_COLS[j - 1]
+            op("V", V.quantize_mx, (T.mq[:, 704 * s + a:704 * s + b], T.mq_s[:, 704 * s + a:704 * s + b], T.mt[:, 2816 * s + 4 * a:2816 * s + 4 * b]),
+               [("mt", s, c) for c in range(1, 17) if i <= (16 - c) // 4 < j], [("mq", s, k) for k in range(i, j)])
 
-        def numbers_v(s):
-            a, b = ON_V[s][0], ON_V[s][-1] + 1
-            ts(T.nl[:, 16 * s + a:16 * s + b], T.sb[:, 2048 * s + 128 * a + 127:2048 * s + 128 * b:128], 0.5, A.mult,
-               [("sb", s, c) for c in ON_V[s]], [("nl", s)])
+        def over_lanes(s, tiles):
+            for i in tiles:
+                mm(2 * s, M_COLS[i], "kq", 0, "mq", 704 * s + M_AT[i], i == 0, i == 1, [("kq", 0), ("mq", s, i)])
+
+        def along(s, a, b, src, keys):
+            tt(T.uu[:, 16 * s + a:16 * s + b], T.bd[:, 16 * s + a:16 * s + b], src, A.subtract, [("bd", s)] + keys, [("uu", s, a)])
+
+        def along_v(s):
+            tt(T.bd[:, 16 * s:16 * s + 16], T.iq[:, 16:32], T.cs[:, 256 * s + 15:256 * s + 256:16], A.subtract, ["ib", ("cs", s)], [("bd", s)])
+            for a, b in ((0, ON_S[s][0]), (ON_S[s][-1] + 1, 16)):
+                along(s, a, b, T.sb[:, 2048 * s + 128 * a + 127:2048 * s + 128 * b:128], [("sb", s, c) for c in range(a, b)] + ["sbz"])
+
+        def along_s(s):
+            a, b = ON_S[s][0], ON_S[s][-1] + 1
+            along(s, a, b, T.acc[:, 16 * s + a:16 * s + b], [("acc", s, c) for c in range(a, b)])
+
+        def numbers(s):
+            f = T.nf[:, 16 * s:16 * s + 16]
+            tt(f, wrap(bank(2 * s, 256), [("K", 2 * s)]), T.uu[:, 16 * s:16 * s + 16], A.add,
+               ["scn"] + [("uu", s, a) for a in range(16)], [("nf", s)])
+            vcopy(T.nl[:, 16 * s:16 * s + 16], f, [("nf", s)], [("nl", s)])
 
         def raised(s):
-            ts(T.nx[:, 16 * s:16 * s + 16], T.nl[:, 16 * s:16 * s + 16], col("off"), A.add, [("nl", s), "off"], [("nx", s)])
+            ts(T.nx[:, 16 * s:16 * s + 16], T.nf[:, 16 * s:16 * s + 16], col("off"), A.add, [("nf", s), "off"], [("nx", s)])
 
-        on_s = [[c for c in range(16) if c not in ON_V[s]] for s in range(2)]
-        v1, v2 = list(ON_V[0]), list(ON_V[1])
-        lanes(0, bank(0, 256), [("K", 0)])
-        act(row(0), bank(1, 256), F.Copy, [("K", 1)], [("rr", 0)])
-        act(row(1), bank(2, 256), F.Copy, [("K", 2)], [("rr", 1)])
-        if t == 0:
+        def unpack(src, key, dst, banks, scale):
+            for b, k in enumerate(banks):
+                mm(k, 256, "cid", 128 * b, src, 0, True, True, [key, ("cid", b)])
+                act(part(dst, b), bank(k, 256), F.Copy, [("K", k)], [(dst, b)], scale=scale)
+
+        def second_step(s):
+            i = 16 * min(s, 1)
+            tt(T.m2[:, s:1024:4], T.w2[:, i:i + 16].indirect(T.kl[:, 16 * s:16 * s + 16]), part("qp", s), A.is_gt,
+               [("w2", min(s, 1)), "kl", ("qp", s)], [("m2", s)])
+
+        low = [list(range(ON_S[s][0] - 1, 0, -1)) for s in range(2)]
+        top = [list(range(15, ON_S[s][-1], -1)) for s in range(2)]
+        s2 = list(ON_S[1][::-1])
+        lanes(0)
+        act(part("rr", 0), bank(1, 256), F.Copy, [("K", 1)], [("rr", 0)])
+        pass_s(0, ON_S[0][::-1])
+        sum_s()
+        act(part("rr", 1), bank(3, 256), F.Copy, [("K", 3)], [("rr", 1)])
+        if first:
             pick_u(256, 640, "ul1")
-            setup_signs()
         for s in range(3):
             mm(4 + s, 256, "qr", 256 + 128 * s, qx, 0, True, True, [X] + u1)
-        ties(0)
-        pass_s(0, on_s[0])
-        sum_s()
-        pass_v(0, v1[:4])
-        lanes(1, bank(2, 256), [("K", 2)])
-        if t == 0:
-            setup_search()
-        pass_v(0, v1[4:])
+        near(0)
+        pass_v(0, top[0])
+        pass_v(0, low[0])
+        mquant(0, 0, 1)
+        lanes(1)
+        if first:
+            setup_ones()
+        over_lanes(0, (0,))
+        near_sum(0)
+        sum_v(0, top[0])
+        mquant(0, 3, 4)
+        sum_v(0, low[0])
+        along_v(0)
+        mquant(0, 1, 3)
+        over_lanes(0, (3, 2, 1))
+        pass_s(1, s2[:2])
         for s in range(3):
-            act(T.qp[:, 256 * s:256 * s + 256], bank(4 + s, 256), F.Copy, [("K", 4 + s), "e0", "e1"], [("qp", s)], scale=col("e%d" % min(s, 1)))
-        pass_s(1, on_s[1][:2])
-        sum_v()
-        numbers_s(0)
-        sum_v()
-        numbers_v(0)
+            act(part("qp", s), bank(4 + s, 256), F.Copy, [("K", 4 + s), "e0", "e1"], [("qp", s)], scale=col("e%d" % min(s, 1)))
+        pass_s(1, s2[2:6])
+        along_s(0)
+        near(1)
+        numbers(0)
 
-        vcopy(T.vv[:, 0:256].indirect(T.nl[:, 0:16]), row(0), [("nl", 0), ("rr", 0)], ["vv"])
-        tt(T.sg[:], T.vv[:, 0:256].indirect(T.cl[:, 0:2]), T.smask[:], A.mult, ["vv", "cl0", ("smask", 0), ("smask", 1)], ["sg"])
-        scan(T.vs[:], T.dv[:], T.vv[:], 0.0, A.add, A.max, ["dv", "vv"], ["vs"])
-        scan(T.sig[:], T.rs16[:, 0:32], T.sg[:], 0.0, A.mult, A.add, ["rs16", "sg"], ["sig"])
-        if t == 0:
-            setup_counts()
+        vcopy(T.vv[:, 0:256].indirect(T.nl[:, 0:16]), part("rr", 0), [("nl", 0), ("rr", 0)], ["vv"])
+        if first:
+            setup_search()
+        tt(T.sg[:], T.vv[:, 0:256].indirect(T.cl[:, 0:2]), T.smask[:], A.mult, ["vv", "cl", ("smask", 0), ("smask", 1)], ["sg"])
+        scan(T.vs[:], msk(2), T.vv[:], 0.0, A.add, A.max, [("msk", 2), "vv"], ["vs"])
+        scan(T.sig[:], msk(4, 32), T.sg[:], 0.0, A.mult, A.add, [("msk", 4), "sg"], ["sig"])
         for i in range(2):
-            act(T.w2[:, 16 * i:16 * i + 16], T.vs[:, 0:256].indirect(T.cl[:, 2 + 2 * i:3 + 2 * i]), F.Copy, ["vs", "cl0", "cl1", "e%d" % i],
+            act(T.w2[:, 16 * i:16 * i + 16], T.vs[:, 0:256].indirect(T.cl[:, 2 + 2 * i:3 + 2 * i]), F.Copy, ["vs", "cl", "e%d" % i],
                 [("w2", i)], scale=col("e%d" % i))
-        pass_s(1, on_s[1][2:])
+        pass_s(1, s2[6:])
         sum_s()
+        if first:
+            setup_unpack()
+        unpack(land, land, "fp", (4, 5, 6, 3), 0.5)
+        near_sum(1)
         for s in range(3):
             i = 16 * min(s, 1) + 15
-            ts(T.m1[:, s:1024:4], T.qp[:, 256 * s:256 * s + 256], T.sig[:, i:i + 1], A.is_lt, [("qp", s), "sig"], [("m1", s)])
+            ts(T.m1[:, s:1024:4], part("qp", s), T.sig[:, i:i + 1], A.is_lt, [("qp", s), "sig"], [("m1", s)])
         quant("m1q", 0, 256, "m1", "m1q", [("m1", s) for s in range(3)] + ["m1z"])
-        mm(7, 256, "kq", 0, "m1q", 0, True, True, [("kq", 0), "m1q"])
-        ties(1)
-        raised(0)
-        if t == 0:
-            setup_counts2()
+        mm(7, 256, "kq", 128, "m1q", 0, True, True, [("kq", 1), "m1q"])
+        pass_v(1, top[1][:2])
+        if first:
+            setup_counts()
         ts(T.ki[:, 48:64], wrap(bank(7, 256), [("K", 7)]), col("ramp"), A.add, ["scn", "ramp"], ["kp"])
-        pass_v(1, v2[:1])
+        pass_v(1, top[1][2:])
         for s in range(3):
             ts(T.ki[:, 16 * s:16 * s + 16], T.ki[:, 48:64], 4 * s, A.logical_shift_right, ["kp"], [("ki", s)], 15, A.bitwise_and)
-        pass_v(1, v2[1:2])
+        pass_v(1, low[1])
         vcopy(T.kl[:], T.ki[:, 0:48], [("ki", s) for s in range(3)], ["kl"])
-        pass_v(1, v2[2:3])
-        for s in range(3):
-            i = 16 * min(s, 1)
-            tt(T.m2[:, s:1024:4], T.w2[:, i:i + 16].indirect(T.kl[:, 16 * s:16 * s + 16]), T.qp[:, 256 * s:256 * s + 256], A.is_gt,
-               [("w2", min(s, 1)), "kl", ("qp", s)], [("m2", s)])
-        quant("m2q", 0, 256, "m2", "m2q", [("m2", s) for s in range(3)] + ["m2z"])
-        for k, a in ((0, 128), (1, 384), (4, 128)):
-            mm(k, 256, "kq", a + 128, "m1q", 0, True, False, [("kq", 1), "m1q"])
-            mm(k, 256, "kq", a, "m2q", 0, False, True, [("kq", 1), "m2q"])
-        pass_v(1, v2[3:])
-        sum_v()
-        numbers_s(1)
-        sum_v()
-        numbers_v(1)
-        if t == 0:
-            setup_merge()
+        mquant(1, 0, 1)
+        over_lanes(1, (0,))
+        sum_v(1, top[1])
+        sum_v(1, low[1])
+        second_step(0)
+        mquant(1, 1, 4)
+        over_lanes(1, (3, 2, 1))
+        along_v(1)
+        along_s(1)
+        second_step(1)
+        numbers(1)
+        if first:
+            ts(T.itb[:], T.itb[:], col("ak"), A.add, ["itb", "ak"], ["itb"])
         vcopy(T.leaf[:, 0:256].indirect(T.nl[:, 16:32]), T.itb[:], ["itb", ("nl", 1)], ["leaf"])
-        dmas("Y", [(T.ld[16 * (q // 4):16 * (q // 4) + 16, 256 * (q % 4):256 * (q % 4) + 256], T.leaf[16 * q:16 * q + 16, :]) for q in range(8)], ["leaf"], ["ld"])
-        dmas("Y", [(T.lw[16 * q:16 * q + 16, :], T.ld[16 * (q % 2):16 * (q % 2) + 16, :]) for q in range(8)], ["ld"], ["lw"])
-
-        wins = [(s, b) for b in range(4) for s in range(4)] + [(4, b) for b in range(4)]
-        wn = [0]
-
-        def windows(n):
-            for _i in range(n):
-                if wins:
-                    s, b = wins.pop(0)
-                    k = (2, 3, 6, 7)[wn[0] % 4]
-                    wn[0] += 1
-                    if s < 4:
-                        mm(k, 256, "cwn", 128 * (4 * s + b), land, 0, True, True, [land, ("cwn", s, b)])
-                        o = 1024 * b + 256 * s
-                        act(T.win[:, o:o + 256], bank(k, 256), F.Copy, [("K", k)], [("win", s, b)])
-                    else:
-                        mm(k, 256, "cid", 128 * b, qx, 0, True, True, [X, ("cid", b)])
-                        act(T.fx[:, 256 * b:256 * b + 256], bank(k, 256), F.Copy, [("K", k)], [("fx", b)])
+        spread("Y", "lw", "leaf", 256, ["leaf"])
+        second_step(2)
+        quant("m2q", 0, 256, "m2", "m2q", [("m2", s) for s in range(3)] + ["m2z"])
+        for k, a in ((0, 256), (1, 512), (7, 256)):
+            mm(k, 256, "kq", a + 128, "m1q", 0, True, False, [("kq", 2), "m1q"])
+            mm(k, 256, "kq", a, "m2q", 0, False, True, [("kq", 2), "m2q"])
+        raised(0)
 
         act(T.dat[:], bank(1, 256), F.Copy, [("K", 1)], ["dat"])
-        act(T.c0s[:], bank(4, 256), F.Copy, [("K", 4)], ["c0s"])
+        spread("S", "win", "fp", 1024, [("fp", b) for b in range(4)])
+        act(T.c0s[:], bank(7, 256), F.Copy, [("K", 7)], ["c0s"])
         tt(T.tq[:], wrap(bank(0, 256), [("K", 0)]), T.nx[:, 0:16], A.add, ["scn", ("nx", 0)], ["tq"])
-        if t == 0:
-            setup_windows((0,))
+        if first:
+            setup_merge()
         vcopy(T.pl[:], T.tq[:], ["tq"], ["pl"])
-        if t == 0:
-            setup_windows((1,))
         vcopy(T.ww[:, 0:1024].indirect(T.pl[:, 0:16]), T.dat[:], ["pl", "dat"], ["ww"])
-        if t:
-            windows(4)
+        unpack(qx, X, "fx", (2, 3, 4, 6), 1.0)
+        if first:
+            setup_wlist()
+            setup_w("S", range(4))
         quant("qw", 0, 256, "ww", "qw", ["ww"])
-        mm(5, 256, "kq", 640, "qw", 0, True, True, [("kq", 5), "qw"])
-        if t == 0:
-            setup_windows((2, 3, 4))
-        windows(20)
+        mm(5, 256, "kq", 768, "qw", 0, True, True, [("kq", 6), "qw"])
         raised(1)
-        tt(T.tq[:], T.iq[:], wrap(bank(5, 256), [("K", 5)]), A.subtract, ["scn", "iq"], ["tq"])
+        tt(T.tq[:], T.iq[:, 0:16], wrap(bank(5, 256), [("K", 5)]), A.subtract, ["scn", "iq"], ["tq"])
         vcopy(T.ql[:], T.tq[:], ["tq"], ["ql"])
-        vcopy(T.csort[:, 0:256].indirect(T.nl[:, 0:16]), T.c0s[:], [("nl", 0), "c0s"], ["csort"])
         vcopy(T.crow[:], T.lw[:, 0:1024].indirect(T.ql[:, 0:16]), ["lw", "ql"], ["crow"])
-        el = "el%d" % t
-        ts(T[el][:], wrap(T.crow[:], ["crow"]), col("ramp"), A.add, ["scn", "ramp"], [el])
-        remote(T[lin][:], T[el][:], "lst%d" % t, [el])
+        el = T.el[:, 16 * t:16 * t + 16]
+        ts(el, wrap(T.crow[:], ["crow"]), col("ramp"), A.add, ["scn", "ramp"], [("el", t)])
+        remote(T[lin][:], el, "lst%d" % t, [("el", t)])
 
+        vcopy(T.csort[:, 0:256].indirect(T.nl[:, 0:16]), T.c0s[:], [("nl", 0), "c0s"], ["csort"])
         vcopy(T.crow[:], T.csort[:, 0:256].indirect(T.nl[:, 16:32]), ["csort", ("nl", 1)], ["crow"])
         tt(T.xi[:, 0:16], wrap(T.crow[:], ["crow"]), T.nx[:, 16:32], A.add, ["scn", ("nx", 1)], ["xi"])
         ts(T.xi[:, 16:32], T.xi[:, 0:16], 511, A.bitwise_and, ["xi"], ["xi2"])
         vcopy(T.xl[:], T.xi[:, 16:32], ["xi2"], ["xl"])
         if t == R - 1:
-            tt(T.msk[:], T.csort[:], T.itb[:], A.add, ["csort", "itb"], ["msk"])
-            ts(T.dfull[:], T.msk[:, 0:256].indirect(T.nl[:, 16:32]), 2.0, A.mult, ["msk", ("nl", 1), "cf"], ["dfull"], col("h"), A.add)
-            dmas("Y", [(T.op[q:q + 1, :], T.dfull[16 * q:16 * q + 1, :]) for q in range(8)], ["dfull"], ["op"])
+            tt(T.vv[:], T.csort[:], T.itb[:], A.add, ["csort", "itb"], ["vv"])
+            ts(T.dfull[:], T.vv[:, 0:256].indirect(T.nl[:, 16:32]), 2.0, A.mult, ["vv", ("nl", 1), "hh"], ["dfull"], col("hh"), A.add)
+            dmas("Y", [(T.op[:, :], T.dfull[0:128:16, :])], ["dfull"], ["op"])
             quant("qv", 0, 128, "vb", "qv", ["vb"])
-        if t == 0:
-            setup_w()
+        if first:
+            setup_w("V", range(4))
 
         for b in range(4):
-            wk = [("win", s, b) for s in range(4)] + [lin]
-            w = T.win[:, 1024 * b:1024 * b + 1024]
-            act(T.etmp[:, 128 * b:128 * b + 128], w.indirect(T[lin][:, 0:8]), F.Copy, wk, [("etmp", b)])
-            tt(T.eb[:, b:512:4], w.indirect(T[lin][:, 8:16]), T.etmp[:, 128 * b:128 * b + 128], A.add, wk + [("etmp", b)], [("eb", b)])
+            w = T.win[:, 256 * b:256 * b + 3328]
+            act(T.etmp[:, 128 * b:128 * b + 128], w.indirect(T[lin][:, 0:8]), F.Copy, ["win", lin], [("etmp", b)])
+            tt(T.eb[:, b:512:4], w.indirect(T[lin][:, 8:16]), T.etmp[:, 128 * b:128 * b + 128], A.add, ["win", lin, ("etmp", b)], [("eb", b)])
         quant("qe", 0, 128, "eb", "qe", [("eb", b) for b in range(4)])
         for i in range(16):
             k, b, s = i % 8, i // 4, i % 4
             mm(k, 128, "qwr", 128 * i, "qe", 0, True, True, [("qwr", b), ("qwrs", b), "qe"])
             out = T.winh[:, 512 * b + s:512 * b + 512:4]
-            if i in (1, 3, 7, 11):
+            if i in H_ON_V:
                 ts(out, bank(k, 128), 0.015625, A.mult, [("K", k)], [("winh", i)])
             else:
                 act(out, bank(k, 128), F.Copy, [("K", k)], [("winh", i)], scale=0.015625)
             if s == 3:
-                tt(T.xs[:, b:1024:4], T.winh[:, 512 * b:512 * b + 512].indirect(T.xl[:, 0:16]), T.fx[:, 256 * b:256 * b + 256], A.add,
+                tt(T.xs[:, b:1024:4], T.winh[:, 512 * b:512 * b + 512].indirect(T.xl[:, 0:16]), part("fx", b), A.add,
                    [("winh", 4 * b + j) for j in range(4)] + ["xl", ("fx", b)], [("xs", b)])
         quant("qx%d" % (t + 1), 0, 256, "xs", ("qx", t + 1), [("xs", b) for b in range(4)])
 

@@ -19,10 +19,10 @@ for _t in range(R):
     _q("qx%d" % _t, 256)
     _q("land%d" % _t, 256)
     _b("lin%d" % _t, 16, "uint16")
-for _n, _w in (("qx3", 256), ("qu", 128), ("qr", 640), ("qv", 128), ("wq", 512), ("qwr", 2048), ("kq", 896), ("mq", 1408),
+for _n, _w in (("qx3", 256), ("qu", 128), ("qr", 640), ("qv", 128), ("wq", 512), ("qwr", 2048), ("kq", 768), ("mq", 1408),
                ("cid", 512), ("m1q", 256), ("m2q", 256), ("qw", 256), ("qe", 128)):
     _q(_n, _w)
-for _n, _w in (("xb", 1024), ("xs", 1024), ("ub", 512), ("vb", 512), ("zero", 1024), ("zc", 528), ("kb", 3584), ("onesb", 128),
+for _n, _w in (("xb", 1024), ("xs", 1024), ("ub", 512), ("vb", 512), ("zero", 1024), ("zc", 528), ("kb", 3072), ("onesb", 128),
                ("gcol", 224), ("colid", 136), ("it16", 256), ("msks", 1280), ("cs", 512), ("mt", 5632), ("sb", 4096),
                ("dd", 1024), ("m1", 1024), ("m2", 1024), ("win", 4096), ("winh", 2048), ("fx", 1024), ("fp", 1024), ("etmp", 512),
                ("eb", 512), ("ww", 1024), ("dat", 256)):
@@ -30,18 +30,19 @@ for _n, _w in (("xb", 1024), ("xs", 1024), ("ub", 512), ("vb", 512), ("zero", 10
 for _n in ("itb", "scn", "vv", "vs", "leaf", "c0s", "csort", "crow", "dfull", "ysb"):
     _b(_n, 256, "float32")
 for _n, _w in (("lw", 1024), ("rr", 512), ("rm", 512), ("sw", 512), ("qp", 768), ("cf", 48), ("acc", 32), ("bd", 32), ("uu", 32),
-               ("nf", 32), ("nx", 32), ("smask", 32), ("sg", 32), ("sig", 32), ("w2", 32), ("iq", 32), ("tq", 16)):
+               ("nf", 32), ("nx", 16), ("smask", 32), ("sg", 32), ("sig", 32), ("w2", 32), ("iq", 32), ("ir", 32), ("tq", 16)):
     _b(_n, _w, "float32")
-for _n, _w in (("ci", 16), ("il", 48), ("il2", 128), ("il3", 128), ("ir", 32), ("ki", 64), ("xi", 32)):
+for _n, _w in (("ci", 16), ("il", 48), ("il2", 128), ("il3", 128), ("ki", 64), ("xi", 32)):
     _b(_n, _w, "int32")
-for _n, _w in (("ulist", 48), ("wlist", 128), ("rep", 16), ("cl", 8), ("nl", 32), ("kl", 48), ("pl", 16), ("ql", 16), ("xl", 16), ("el", 48)):
+for _n, _w in (("ulist", 48), ("wlist", 128), ("cl", 8), ("nl", 32), ("kl", 48), ("pl", 16), ("ql", 16), ("xl", 16), ("el", 48)):
     _b(_n, _w, "uint16")
 for _k in range(8):
     _b("pb%d" % _k, 512, "float32", "psum")
 
-BIG = 1e29
+BIG = 2.0 ** 96
 STEP = 4096.0
 ON_S = (range(7, 13), range(1, 13))
+ON_S_FIRST = (range(7, 13), range(1, 14))
 M_AT, M_COLS = (0, 256, 448, 576), (256, 192, 128, 128)
 H_ON_V = (1, 3, 5, 7, 11)
 
@@ -163,7 +164,7 @@ def rank_program(g, core, T, topo):
     dmas("Y", [(T.xb[:], T.x[:, :])], [], ["xb"])
 
     names = ("p", "l", "a0", "a1", "h", "g", "a", "m", "odd", "e0", "e1", "x0", "x1", "x2", "y0", "y1", "y2", "ramp", "off", "t0", "t1",
-             "s0", "s1", "w0", "pad", "w1", "n0", "n1", "k0", "k1", "ke0", "ke1", "kf0", "kf1", "kg", "kh", "wm", "iqb", "ak", "bb", "hh")
+             "s0", "s1", "w0", "pad", "w1", "n0", "n1", "k0", "k1", "f0", "f1", "wm", "iqb", "ak", "bb", "hh")
     C = {k: i for i, k in enumerate(names)}
 
     def col(k, n=1, step=1):
@@ -180,12 +181,12 @@ def rank_program(g, core, T, topo):
     iota(T.ci[:, 0:9], "ci", [[0, 9]], 0, 1)
     iota(T.il[:, 0:16], ("il", 0), [[1, 2], [16, 8]], 0, 0)
     iota(T.it16[:], "it16", [[0, 16], [1, 16]], 0, 0)
+    iota(T.gcol[:], "gcol", [[1, 14], [0, 16]], -6, 0)
     iota(T.ir[:, 0:16], "ir", [[16, 16]], 15, 0)
     for s in (1, 2, 3):
         iota(T.il[:, 8 + 8 * s:16 + 8 * s], ("il", s), [[64, 2], [32 - 64 * (s // 2), 2], [16 - 32 * (s % 2), 2]], 16 * s, 0)
-    iota(T.gcol[:], "gcol", [[1, 14], [0, 16]], -6, 0)
     iota(T.colid[:], "colid", [[1, 136]], -5, 0)
-    iota(T.ir[:, 16:32], "ir2", [[64, 16]], 0, 0)
+    iota(T.ir[:, 16:32], "ir2", [[64, 16]], 15 * int(STEP), 0)
     memset(T.zero[:], 0.0, ["zero"])
     memset(T.cf[:], 0.0, ["cf"])
     for k, sh, an in (("l", 0, 15), ("a0", 4, 1), ("a1", 5, 1), ("h", 6, 1), ("g", 4, 7), ("a", 4, 3), ("m", 5, 3), ("odd", 0, 1)):
@@ -193,24 +194,22 @@ def rank_program(g, core, T, topo):
     vcopy(T.cf[:, 0:9], T.ci[:, 0:9], ["ci"] + ["ci" + k for k in names[1:9]], ["cf"])
     vcopy(T.ulist[:, 0:16], T.il[:, 0:16], [("il", 0)], ["ul0"])
     tails = [(4 * (M_AT[i] + (M_COLS[i] - 48 if i < 3 else 16)), 4 * (M_AT[i] + M_COLS[i])) for i in range(4)]
-    for i, (a, b) in enumerate(tails):
-        memset(T.mt[:, a:b], 0.0, [("mz", 0, i)])
     memset(T.sb[:, 127:4096:2048], 0.0, ["sbz"])
     memset(T.onesb[:], 1.0, ["onesb"])
-    ts(msk(0), T.it16[:], col("l"), A.is_gt, ["it16", "cf"], [("msk", 0)], BIG, A.mult)
-    ts(msk(1), T.it16[:], col("l"), A.is_equal, ["it16", "cf"], [("msk", 1)], BIG, A.mult)
+    ts(msk(0), T.it16[:], col("l"), A.not_equal, ["it16", "cf"], [("msk", 0)], -BIG, A.mult)
+    ts(msk(1), T.it16[:], 0.0, A.is_equal, ["it16"], [("msk", 1)], -2.0 * BIG, A.mult)
     ts(msk(4), T.it16[:], 0.0, A.not_equal, ["it16"], [("msk", 4)])
-    vcopy(T.rep[:], T.ir[:, 0:16], ["ir"], ["rep"])
-    vcopy(T.ulist[:, 16:40], T.il[:, 16:40], [("il", s) for s in (1, 2, 3)], ["ul1"])
+    for s in range(2):
+        dmas("Y", [(T.mt[:, 2816 * s + a:2816 * s + b], T.zero[:, 0:b - a]) for a, b in tails], ["zero"], [("mz", s, i) for i in range(4)])
     dmas("Y", [(cv("wq", 0, 512), T.wc[:, :])], [], ["wq"])
     dmas("Y", [(T.wq_s[:], T.ws[:, :])], [], ["wqs"])
-    dmas("Y", [(T.mt[:, 2816 + a:2816 + b], T.zero[:, 0:b - a]) for a, b in tails], ["zero"], [("mz", 1, i) for i in range(4)])
-    dmas("Y", [(T.kb[:, a:b], T.zero[:, 0:b - a]) for a, b in ((512, 1536), (1536, 2560), (2560, 3072))], ["zero"], ["kbz"])
+    dmas("Y", [(T.kb[:, a:b], T.zero[:, 0:b - a]) for a, b in ((512, 1536), (1536, 2560))], ["zero"], ["kbz"])
     dmas("Y", [(T.zc[:], T.zero[:, 0:528])], ["zero"], ["zz"])
     dmas("Y", [(T.vb[:], T.v[:, :])], [], ["vb"])
     aff("e0", "a0", 2.0, -1.0, 2)
     aff("ramp", "l", STEP, -15.0 * STEP)
-    aff("bb", "l", STEP + 1.0, -15.0 * STEP - 15.0)
+    aff("bb", "l", STEP - 1.0, -15.0 * STEP)
+    act(T.iq[:, 16:32], T.ir[:, 0:16], F.Identity, ["ir", "bb"], ["ib"], bias=col("bb"))
     aff("x0", "e0", -1.0, "g")
     aff("x1", "e1", -2.0, "g")
     aff("off", "a", 256.0, "ramp")
@@ -218,67 +217,67 @@ def rank_program(g, core, T, topo):
     aff("t1", "l", 16.0, -120.0)
     aff("x2", "e0", -1.0, "x1")
     aff("n0", "e0", 7.5, 7.5, 2)
-    quant("qu", 0, 128, "ub", "qu", ["ub"])
-
-    def pick_u(a, b, key):
-        lst = T.ulist[:, a // 16:b // 16]
-        vcopy(T.qr[:, a:b].bitcast(dt.uint32), T.qu[:, 0:128].bitcast(dt.uint32).indirect(lst), ["qu", key], [("qr", a)])
-        act(T.qr_s[:, a:b], T.qu_s[:, 0:128].indirect(lst), F.Copy, ["qu", key], [("qrs", a)])
-    pick_u(0, 256, "ul0")
-    quant("qx0", 0, 256, "xb", ("qx", 0), ["xb"])
-    aff("s0", "e0", 7.5, "t0", 2)
-    aff("w0", "e0", "t1", 135.0, 2, 2)
-    aff("y0", "x0", 16.0, 0.0, 3)
-    aff("wm", "odd", -15.0, 16.0)
-    aff("iqb", "l", 4.0 - STEP, "m")
-    aff("ak", "a", 1024.0, 0.0)
-    aff("hh", "a", -1536.0, "h")
 
     def gcol(shift=0):
         return T.gcol[:, 96 - 16 * shift:224 - 16 * shift]
 
     def ktile(i, t, src, k, w):
-        ts(T.kb[:, 512 * i + t:512 * i + 512:4], src, col(k), A.is_equal, ["gcol", "colid", "cf", "kbz" if 0 < i < 6 else "cf", k] + ([w] if w else []),
-           [("kb", i, t)], *((col(w), A.mult) if w else ()))
+        ts(T.kb[:, 512 * i + t:512 * i + 512:4], src, col(k), A.is_equal,
+           ["colid" if i in (3, 4) else "gcol", "cf", "kbz" if 0 < i < 5 else "cf", k] + [w] * isinstance(w, str),
+           [("kb", i, t)], col(w) if isinstance(w, str) else w, A.mult)
 
     def kquant(a, b):
         quant("kq", 128 * a, 128 * b, "kb", ("kq", a), [("kb", i, t) for i in range(a, b) for t in range(4)], s0=512 * a)
 
-    def setup_ones():
-        for t in range(4):
-            ktile(0, t, gcol(), "g", None)
-        kquant(0, 1)
-        ts(msk(2), msk(1), -1.0, A.mult, [("msk", 1)], [("msk", 2)])
-        ts(msk(3), msk(1), -1.0, A.mult, [("msk", 1)], [("msk", 3)], STEP, A.add)
-        ts(T.iq[:, 16:32], T.ir[:, 0:16], col("bb"), A.add, ["ir", "bb"], ["ib"])
+    for t in range(4):
+        ktile(0, t, gcol(), "g", 1.0)
+    kquant(0, 1)
+    vcopy(T.ulist[:, 16:40], T.il[:, 16:40], [("il", s) for s in (1, 2, 3)], ["ul1"])
+    ts(msk(2), msk(0), -1.0, A.mult, [("msk", 0)], [("msk", 2)], -BIG, A.add)
+    ts(msk(3), msk(2), STEP, A.add, [("msk", 2)], [("msk", 3)])
+    quant("qu", 0, 128, "ub", "qu", ["ub"])
+
+    def pick_u(e, a, b, key):
+        lst = T.ulist[:, a // 16:b // 16]
+        if e == "V":
+            vcopy(T.qr[:, a:b].bitcast(dt.uint32), T.qu[:, 0:128].bitcast(dt.uint32).indirect(lst), ["qu", key], [("qr", a)])
+        else:
+            act(T.qr_s[:, a:b], T.qu_s[:, 0:128].indirect(lst), F.Copy, ["qu", key], [("qrs", a)])
+    pick_u("V", 0, 256, "ul0")
+    pick_u("S", 0, 256, "ul0")
+    quant("qx0", 0, 256, "xb", ("qx", 0), ["xb"])
+    pick_u("V", 256, 640, "ul1")
+    aff("s0", "e0", 7.5, "t0", 2)
+    aff("w0", "e0", "t1", 135.0, 2, 2)
+    aff("y0", "x0", 16.0, 0.0, 3)
+    aff("f0", "e0", 0.0625, 0.0, 2)
+    aff("wm", "odd", -15.0, 16.0)
+    aff("iqb", "l", 4.0 - STEP, "m")
+    aff("ak", "a", 1024.0, 0.0)
+    aff("hh", "a", -1536.0, "h")
 
     def setup_search():
         vcopy(T.cl[:, 0:5], col("s0", 5), ["s0", "s1", "w0", "w1"], ["cl"])
         for i in range(2):
             ts(T.smask[:, 16 * i:16 * i + 16], T.it16[:, 0:16], col("l"), A.is_equal, ["it16", "e%d" % i], [("smask", i)], col("e%d" % i), A.mult)
-        ts(col("k0", 2), col("n0", 2), col("l"), A.not_equal, ["cf", "n0", "n1"], ["k0", "k1"])
-        tt(col("ke0", 2), col("k0", 2), col("e0", 2), A.mult, ["k0", "k1", "e0", "e1"], ["ke0", "ke1"])
-        ts(col("kg"), col("k1"), 16.0, A.mult, ["k1"], ["kg"])
-        ts(col("kh"), col("k1"), 256.0, A.mult, ["k1"], ["kh"])
-        ts(col("kf0", 2), col("ke0", 2), 16.0, A.mult, ["ke0", "ke1"], ["kf0", "kf1"])
+        ts(col("k0", 2), col("n0", 2), col("l"), A.not_equal, ["cf", "n0", "n1"], ["k0", "k1"], 16.0, A.mult)
         for t in range(3):
-            ktile(1, t, gcol(), "g", ("k0", "kg", "kh")[t])
+            ktile(1, t, gcol(), "g", 16.0 ** (t - 1))
         kquant(1, 2)
 
     def setup_counts():
         for t in range(3):
             i = min(t, 1)
             ktile(2, t, gcol(), "x%d" % t, "e%d" % i)
-            ktile(3, t, gcol(), "x%d" % t, "kf%d" % i)
-            ktile(4, t, T.colid[:, 4 - 2 * t:132 - 2 * t], "y%d" % t, "e%d" % i)
-            ktile(5, t, T.colid[:, 5 - 2 * t:133 - 2 * t], "y%d" % t, "ke%d" % i)
-        kquant(2, 6)
+            ktile(3, t, T.colid[:, 4 - 2 * t:132 - 2 * t], "y%d" % t, "e%d" % i)
+            ktile(4, t, T.colid[:, 5 - 2 * t:133 - 2 * t], "y%d" % t, "f%d" % i)
+        kquant(2, 5)
 
     def setup_merge():
         for t in range(4):
-            ktile(6, t, gcol(2 * t), "h", "wm")
-        kquant(6, 7)
-        ts(T.iq[:, 0:16], T.ir[:, 16:32], col("iqb"), A.add, ["ir2", "iqb"], ["iq"], 15.0 * STEP, A.add)
+            ktile(5, t, gcol(2 * t), "h", "wm")
+        kquant(5, 6)
+        act(T.iq[:, 0:16], T.ir[:, 16:32], F.Identity, ["ir2", "iqb"], ["iq"], bias=col("iqb"))
 
     def setup_pool():
         iota(T.m1[:, 3:1024:4], "m1z", [[0, 256]], 0, 0)
@@ -310,7 +309,8 @@ def rank_program(g, core, T, topo):
     for t in range(R):
         qx = "qx%d" % t
         X = ("qx", t)
-        first = t == 0
+        first, last = t == 0, t == R - 1
+        on_s = ON_S_FIRST if first else ON_S
         remote(cv("land%d" % t, 0, 256), cv(qx, 0, 256), "arr%d" % t, [X])
         remote(T["land%d_s" % t][:], T[qx + "_s"][:], "arr%d" % t, [X])
         if first:
@@ -338,11 +338,10 @@ def rank_program(g, core, T, topo):
 
         def lanes(s):
             tt(part("rm", s), bank(2 * s, 256), msk(0), A.add, [("K", 2 * s), ("msk", 0)], [("rm", s)])
-            scan(part("sw", s), msk(1), part("rm", s), 0.0, A.add, A.min, [("msk", 1), ("rm", s)], [("sw", s)])
+            scan(part("sw", s), msk(1), part("rm", s), 0.0, A.add, A.max, [("msk", 1), ("rm", s)], [("sw", s)])
 
         def near(s):
-            tt(slot(s, 16, 0, 256), part("sw", s).indirect(T.rep[:, 0:16]), part("rm", s), A.is_gt,
-               [("sw", s), "rep", ("rm", s), ("mz", s, 0)], [("mt", s, 16)])
+            tt(slot(s, 16, 0, 256), part("sw", s), bank(2 * s, 256), A.is_ge, [("sw", s), ("K", 2 * s), ("mz", s, 0)], [("mt", s, 16)])
 
         def near_sum(s):
             scan(part("cs", s), msk(4), slot(s, 16, 0, 256), 0.0, A.mult, A.add, [("msk", 4), ("mt", s, 16)], [("cs", s)])
@@ -387,11 +386,11 @@ def rank_program(g, core, T, topo):
 
         def along_v(s):
             tt(T.bd[:, 16 * s:16 * s + 16], T.iq[:, 16:32], T.cs[:, 256 * s + 15:256 * s + 256:16], A.subtract, ["ib", ("cs", s)], [("bd", s)])
-            for a, b in ((0, ON_S[s][0]), (ON_S[s][-1] + 1, 16)):
+            for a, b in ((0, on_s[s][0]), (on_s[s][-1] + 1, 16)):
                 along(s, a, b, T.sb[:, 2048 * s + 128 * a + 127:2048 * s + 128 * b:128], [("sb", s, c) for c in range(a, b)] + ["sbz"])
 
         def along_s(s):
-            a, b = ON_S[s][0], ON_S[s][-1] + 1
+            a, b = on_s[s][0], on_s[s][-1] + 1
             along(s, a, b, T.acc[:, 16 * s + a:16 * s + b], [("acc", s, c) for c in range(a, b)])
 
         def numbers(s):
@@ -399,9 +398,6 @@ def rank_program(g, core, T, topo):
             tt(f, wrap(bank(2 * s, 256), [("K", 2 * s)]), T.uu[:, 16 * s:16 * s + 16], A.add,
                ["scn"] + [("uu", s, a) for a in range(16)], [("nf", s)])
             vcopy(T.nl[:, 16 * s:16 * s + 16], f, [("nf", s)], [("nl", s)])
-
-        def raised(s):
-            ts(T.nx[:, 16 * s:16 * s + 16], T.nf[:, 16 * s:16 * s + 16], col("off"), A.add, [("nf", s), "off"], [("nx", s)])
 
         def unpack(src, key, dst, banks, scale):
             for b, k in enumerate(banks):
@@ -413,25 +409,21 @@ def rank_program(g, core, T, topo):
             tt(T.m2[:, s:1024:4], T.w2[:, i:i + 16].indirect(T.kl[:, 16 * s:16 * s + 16]), part("qp", s), A.is_gt,
                [("w2", min(s, 1)), "kl", ("qp", s)], [("m2", s)])
 
-        low = [list(range(ON_S[s][0] - 1, 0, -1)) for s in range(2)]
-        top = [list(range(15, ON_S[s][-1], -1)) for s in range(2)]
-        s2 = list(ON_S[1][::-1])
+        low = [list(range(on_s[s][0] - 1, 0, -1)) for s in range(2)]
+        top = [list(range(15, on_s[s][-1], -1)) for s in range(2)]
+        s2 = list(on_s[1][::-1])
         lanes(0)
         act(part("rr", 0), bank(1, 256), F.Copy, [("K", 1)], [("rr", 0)])
-        pass_s(0, ON_S[0][::-1])
+        pass_s(0, on_s[0][::-1])
         sum_s()
         act(part("rr", 1), bank(3, 256), F.Copy, [("K", 3)], [("rr", 1)])
         if first:
-            pick_u(256, 640, "ul1")
-        for s in range(3):
-            mm(4 + s, 256, "qr", 256 + 128 * s, qx, 0, True, True, [X] + u1)
+            pick_u("S", 256, 640, "ul1")
         near(0)
         pass_v(0, top[0])
         pass_v(0, low[0])
         mquant(0, 0, 1)
         lanes(1)
-        if first:
-            setup_ones()
         over_lanes(0, (0,))
         near_sum(0)
         sum_v(0, top[0])
@@ -440,6 +432,8 @@ def rank_program(g, core, T, topo):
         along_v(0)
         mquant(0, 1, 3)
         over_lanes(0, (3, 2, 1))
+        for s in range(3):
+            mm(4 + s, 256, "qr", 256 + 128 * s, qx, 0, True, True, [X] + u1)
         pass_s(1, s2[:2])
         for s in range(3):
             act(part("qp", s), bank(4 + s, 256), F.Copy, [("K", 4 + s), "e0", "e1"], [("qp", s)], scale=col("e%d" % min(s, 1)))
@@ -460,60 +454,65 @@ def rank_program(g, core, T, topo):
         pass_s(1, s2[6:])
         sum_s()
         if first:
+            act(T.itb[:], T.itb[:], F.Identity, ["itb", "ak"], ["itb"], bias=col("ak"))
             setup_unpack()
         unpack(land, land, "fp", (4, 5, 6, 3), 0.5)
+        spread("S", "win", "fp", 1024, [("fp", b) for b in range(4)])
         near_sum(1)
         for s in range(3):
             i = 16 * min(s, 1) + 15
-            ts(T.m1[:, s:1024:4], part("qp", s), T.sig[:, i:i + 1], A.is_lt, [("qp", s), "sig"], [("m1", s)])
+            ts(T.m1[:, s:1024:4], part("qp", s), T.sig[:, i:i + 1], A.is_lt, [("qp", s), "sig", "k0", "k1"], [("m1", s)],
+               col("k%d" % min(s, 1)), A.mult)
         quant("m1q", 0, 256, "m1", "m1q", [("m1", s) for s in range(3)] + ["m1z"])
         mm(7, 256, "kq", 128, "m1q", 0, True, True, [("kq", 1), "m1q"])
         pass_v(1, top[1][:2])
         if first:
             setup_counts()
+        for k, a in ((0, 256), (1, 512)):
+            mm(k, 256, "kq", a, "m1q", 0, True, False, [("kq", 2), "m1q"])
         ts(T.ki[:, 48:64], wrap(bank(7, 256), [("K", 7)]), col("ramp"), A.add, ["scn", "ramp"], ["kp"])
         pass_v(1, top[1][2:])
         for s in range(3):
             ts(T.ki[:, 16 * s:16 * s + 16], T.ki[:, 48:64], 4 * s, A.logical_shift_right, ["kp"], [("ki", s)], 15, A.bitwise_and)
         pass_v(1, low[1])
+        sum_v(1, top[1][:1])
         vcopy(T.kl[:], T.ki[:, 0:48], [("ki", s) for s in range(3)], ["kl"])
         mquant(1, 0, 1)
         over_lanes(1, (0,))
-        sum_v(1, top[1])
+        sum_v(1, top[1][1:])
         sum_v(1, low[1])
         second_step(0)
+        if first:
+            setup_wlist()
+            setup_merge()
         mquant(1, 1, 4)
         over_lanes(1, (3, 2, 1))
         along_v(1)
         along_s(1)
         second_step(1)
         numbers(1)
-        if first:
-            ts(T.itb[:], T.itb[:], col("ak"), A.add, ["itb", "ak"], ["itb"])
         vcopy(T.leaf[:, 0:256].indirect(T.nl[:, 16:32]), T.itb[:], ["itb", ("nl", 1)], ["leaf"])
         spread("Y", "lw", "leaf", 256, ["leaf"])
         second_step(2)
         quant("m2q", 0, 256, "m2", "m2q", [("m2", s) for s in range(3)] + ["m2z"])
-        for k, a in ((0, 256), (1, 512), (7, 256)):
-            mm(k, 256, "kq", a + 128, "m1q", 0, True, False, [("kq", 2), "m1q"])
+        for k, a in ((0, 256), (1, 384)):
             mm(k, 256, "kq", a, "m2q", 0, False, True, [("kq", 2), "m2q"])
-        raised(0)
+        ts(T.nx[:], T.nf[:, 16:32], col("off"), A.add, [("nf", 1), "off"], ["nx"])
+        if last:
+            quant("qv", 0, 128, "vb", "qv", ["vb"])
 
         act(T.dat[:], bank(1, 256), F.Copy, [("K", 1)], ["dat"])
-        spread("S", "win", "fp", 1024, [("fp", b) for b in range(4)])
-        act(T.c0s[:], bank(7, 256), F.Copy, [("K", 7)], ["c0s"])
-        tt(T.tq[:], wrap(bank(0, 256), [("K", 0)]), T.nx[:, 0:16], A.add, ["scn", ("nx", 0)], ["tq"])
-        if first:
-            setup_merge()
-        vcopy(T.pl[:], T.tq[:], ["tq"], ["pl"])
+        tt(T.tq[:], wrap(bank(0, 256), [("K", 0)]), T.nf[:, 0:16], A.add, ["scn", ("nf", 0)], ["tq"])
+        act(T.c0s[:], bank(0, 256), F.Copy, [("K", 0)], ["c0s"])
+        ts(T.pl[:], T.tq[:], col("off"), A.add, ["tq", "off"], ["pl"])
         vcopy(T.ww[:, 0:1024].indirect(T.pl[:, 0:16]), T.dat[:], ["pl", "dat"], ["ww"])
         unpack(qx, X, "fx", (2, 3, 4, 6), 1.0)
         if first:
-            setup_wlist()
             setup_w("S", range(4))
         quant("qw", 0, 256, "ww", "qw", ["ww"])
-        mm(5, 256, "kq", 768, "qw", 0, True, True, [("kq", 6), "qw"])
-        raised(1)
+        mm(5, 256, "kq", 640, "qw", 0, True, True, [("kq", 5), "qw"])
+        if first:
+            setup_w("V", (0,))
         tt(T.tq[:], T.iq[:, 0:16], wrap(bank(5, 256), [("K", 5)]), A.subtract, ["scn", "iq"], ["tq"])
         vcopy(T.ql[:], T.tq[:], ["tq"], ["ql"])
         vcopy(T.crow[:], T.lw[:, 0:1024].indirect(T.ql[:, 0:16]), ["lw", "ql"], ["crow"])
@@ -523,24 +522,26 @@ def rank_program(g, core, T, topo):
 
         vcopy(T.csort[:, 0:256].indirect(T.nl[:, 0:16]), T.c0s[:], [("nl", 0), "c0s"], ["csort"])
         vcopy(T.crow[:], T.csort[:, 0:256].indirect(T.nl[:, 16:32]), ["csort", ("nl", 1)], ["crow"])
-        tt(T.xi[:, 0:16], wrap(T.crow[:], ["crow"]), T.nx[:, 16:32], A.add, ["scn", ("nx", 1)], ["xi"])
+        tt(T.xi[:, 0:16], wrap(T.crow[:], ["crow"]), T.nx[:], A.add, ["scn", "nx"], ["xi"])
         ts(T.xi[:, 16:32], T.xi[:, 0:16], 511, A.bitwise_and, ["xi"], ["xi2"])
         vcopy(T.xl[:], T.xi[:, 16:32], ["xi2"], ["xl"])
-        if t == R - 1:
+        if last:
             tt(T.vv[:], T.csort[:], T.itb[:], A.add, ["csort", "itb"], ["vv"])
-            ts(T.dfull[:], T.vv[:, 0:256].indirect(T.nl[:, 16:32]), 2.0, A.mult, ["vv", ("nl", 1), "hh"], ["dfull"], col("hh"), A.add)
-            dmas("Y", [(T.op[:, :], T.dfull[0:128:16, :])], ["dfull"], ["op"])
-            quant("qv", 0, 128, "vb", "qv", ["vb"])
         if first:
-            setup_w("V", range(4))
+            setup_w("V", (1,))
 
         for b in range(4):
             w = T.win[:, 256 * b:256 * b + 3328]
             act(T.etmp[:, 128 * b:128 * b + 128], w.indirect(T[lin][:, 0:8]), F.Copy, ["win", lin], [("etmp", b)])
             tt(T.eb[:, b:512:4], w.indirect(T[lin][:, 8:16]), T.etmp[:, 128 * b:128 * b + 128], A.add, ["win", lin, ("etmp", b)], [("eb", b)])
+        if last:
+            act(T.dfull[:], T.vv[:, 0:256].indirect(T.nl[:, 16:32]), F.Identity, ["vv", ("nl", 1), "hh"], ["dfull"], scale=2.0, bias=col("hh"))
+            dmas("Y", [(T.op[:, :], T.dfull[0:128:16, :])], ["dfull"], ["op"])
         quant("qe", 0, 128, "eb", "qe", [("eb", b) for b in range(4)])
         for i in range(16):
             k, b, s = i % 8, i // 4, i % 4
+            if first and i in (0, 4):
+                setup_w("V", (2 + i // 4,))
             mm(k, 128, "qwr", 128 * i, "qe", 0, True, True, [("qwr", b), ("qwrs", b), "qe"])
             out = T.winh[:, 512 * b + s:512 * b + 512:4]
             if i in H_ON_V:

@@ -3,7 +3,7 @@ import comms_topo
 
 R = 3
 SCRATCH = {}
-SEMAPHORES = ["sV", "sS", "sP", "sG", "ls"] + ["arr%d" % t for t in range(R)] + ["lst%d" % t for t in range(R)] + ["d%d" % i for i in range(30)]
+SEMAPHORES = ["sV", "sS", "sP", "sG", "ls"] + ["arr%d" % t for t in range(R)] + ["lst%d" % t for t in range(R)] + ["d%d" % i for i in range(32)]
 
 
 def _b(name, n, d, where="sbuf"):
@@ -19,7 +19,7 @@ for _t in range(R):
     _q("qx%d" % _t, 256)
     _q("land%d" % _t, 256)
     _b("lin%d" % _t, 16, "uint16")
-for _n, _w in (("qx3", 256), ("qu", 128), ("qr", 640), ("qv", 128), ("wq", 512), ("qwr", 2048), ("kq", 768), ("mq", 1408),
+for _n, _w in (("qx3", 256), ("qu", 128), ("qr", 256), ("qv", 128), ("wq", 512), ("qwr", 2048), ("kq", 768), ("mq", 1408),
                ("cid", 512), ("m1q", 256), ("m2q", 256), ("qw", 256), ("qe", 128)):
     _q(_n, _w)
 for _n, _w in (("xb", 1024), ("xs", 1024), ("ub", 512), ("vb", 512), ("zero", 1024), ("zc", 528), ("kb", 3072), ("onesb", 128),
@@ -32,17 +32,17 @@ for _n in ("itb", "scn", "vv", "vs", "leaf", "c0s", "csort", "crow", "dfull", "y
 for _n, _w in (("lw", 1024), ("rr", 512), ("rm", 512), ("sw", 512), ("qp", 768), ("cf", 48), ("acc", 32), ("bd", 32), ("uu", 32),
                ("nf", 32), ("nx", 16), ("smask", 32), ("sg", 32), ("sig", 32), ("w2", 32), ("iq", 32), ("ir", 32), ("tq", 16)):
     _b(_n, _w, "float32")
-for _n, _w in (("ci", 16), ("il", 48), ("il2", 128), ("il3", 128), ("ki", 64), ("xi", 32)):
+for _n, _w in (("ci", 16), ("il", 16), ("il2", 128), ("il3", 128), ("ki", 64), ("xi", 32)):
     _b(_n, _w, "int32")
-for _n, _w in (("ulist", 48), ("wlist", 128), ("cl", 8), ("nl", 32), ("kl", 48), ("pl", 16), ("ql", 16), ("xl", 16), ("el", 48)):
+for _n, _w in (("ulist", 16), ("wlist", 128), ("cl", 8), ("nl", 32), ("kl", 48), ("pl", 16), ("ql", 16), ("xl", 16), ("el", 48)):
     _b(_n, _w, "uint16")
 for _k in range(8):
     _b("pb%d" % _k, 512, "float32", "psum")
 
 BIG = 2.0 ** 96
 STEP = 4096.0
-ON_S = (range(7, 13), range(1, 13))
-ON_S_FIRST = (range(7, 13), range(1, 14))
+ON_S = (8, 13)
+ON_S_FIRST = (8, 14)
 M_AT, M_COLS = (0, 256, 448, 576), (256, 192, 128, 128)
 H_ON_V = (1, 3, 5, 7, 11)
 
@@ -156,9 +156,9 @@ def rank_program(g, core, T, topo):
     def select(out, in_, pat, cmp, base, cm, reads, writes):
         op("G", g.affine_select, (out, in_, pat, cmp, 0.0, base, cm), reads, writes)
 
-    def spread(e, dst, src, n, reads):
+    def spread(e, dst, src, n, reads, qs=range(8)):
         dmas(e, [(T[dst][16 * q:16 * q + 16, n * a:n * a + n], T[src][64 * (q % 2) + 16 * a:64 * (q % 2) + 16 * a + 16, :])
-                 for q in range(8) for a in range(4)], reads, [dst])
+                 for q in qs for a in range(4)], reads, [(dst, q) for q in qs])
 
     dmas("S", [(T.ub[:], T.u[:, :])], [], ["ub"])
     dmas("Y", [(T.xb[:], T.x[:, :])], [], ["xb"])
@@ -179,23 +179,19 @@ def rank_program(g, core, T, topo):
         return T.msks[:, 256 * k:256 * k + n]
 
     iota(T.ci[:, 0:9], "ci", [[0, 9]], 0, 1)
-    iota(T.il[:, 0:16], ("il", 0), [[1, 2], [16, 8]], 0, 0)
+    iota(T.il[:], "il", [[1, 2], [16, 8]], 0, 0)
     iota(T.it16[:], "it16", [[0, 16], [1, 16]], 0, 0)
     iota(T.gcol[:], "gcol", [[1, 14], [0, 16]], -6, 0)
     iota(T.ir[:, 0:16], "ir", [[16, 16]], 15, 0)
-    for s in (1, 2, 3):
-        iota(T.il[:, 8 + 8 * s:16 + 8 * s], ("il", s), [[64, 2], [32 - 64 * (s // 2), 2], [16 - 32 * (s % 2), 2]], 16 * s, 0)
+    iota(col("pad"), "pad", [[0, 1]], 0, 0)
     iota(T.colid[:], "colid", [[1, 136]], -5, 0)
     iota(T.ir[:, 16:32], "ir2", [[64, 16]], 15 * int(STEP), 0)
     memset(T.zero[:], 0.0, ["zero"])
-    memset(T.cf[:], 0.0, ["cf"])
     for k, sh, an in (("l", 0, 15), ("a0", 4, 1), ("a1", 5, 1), ("h", 6, 1), ("g", 4, 7), ("a", 4, 3), ("m", 5, 3), ("odd", 0, 1)):
         ts(T.ci[:, C[k]:C[k] + 1], T.ci[:, 0:1], sh, A.logical_shift_right, ["ci"], ["ci" + k], an, A.bitwise_and)
     vcopy(T.cf[:, 0:9], T.ci[:, 0:9], ["ci"] + ["ci" + k for k in names[1:9]], ["cf"])
-    vcopy(T.ulist[:, 0:16], T.il[:, 0:16], [("il", 0)], ["ul0"])
+    vcopy(T.ulist[:], T.il[:], ["il"], ["ulist"])
     tails = [(4 * (M_AT[i] + (M_COLS[i] - 48 if i < 3 else 16)), 4 * (M_AT[i] + M_COLS[i])) for i in range(4)]
-    memset(T.sb[:, 127:4096:2048], 0.0, ["sbz"])
-    memset(T.onesb[:], 1.0, ["onesb"])
     ts(msk(0), T.it16[:], col("l"), A.not_equal, ["it16", "cf"], [("msk", 0)], -BIG, A.mult)
     ts(msk(1), T.it16[:], 0.0, A.is_equal, ["it16"], [("msk", 1)], -2.0 * BIG, A.mult)
     ts(msk(4), T.it16[:], 0.0, A.not_equal, ["it16"], [("msk", 4)])
@@ -232,21 +228,12 @@ def rank_program(g, core, T, topo):
     for t in range(4):
         ktile(0, t, gcol(), "g", 1.0)
     kquant(0, 1)
-    vcopy(T.ulist[:, 16:40], T.il[:, 16:40], [("il", s) for s in (1, 2, 3)], ["ul1"])
     ts(msk(2), msk(0), -1.0, A.mult, [("msk", 0)], [("msk", 2)], -BIG, A.add)
     ts(msk(3), msk(2), STEP, A.add, [("msk", 2)], [("msk", 3)])
     quant("qu", 0, 128, "ub", "qu", ["ub"])
-
-    def pick_u(e, a, b, key):
-        lst = T.ulist[:, a // 16:b // 16]
-        if e == "V":
-            vcopy(T.qr[:, a:b].bitcast(dt.uint32), T.qu[:, 0:128].bitcast(dt.uint32).indirect(lst), ["qu", key], [("qr", a)])
-        else:
-            act(T.qr_s[:, a:b], T.qu_s[:, 0:128].indirect(lst), F.Copy, ["qu", key], [("qrs", a)])
-    pick_u("V", 0, 256, "ul0")
-    pick_u("S", 0, 256, "ul0")
+    vcopy(T.qr[:].bitcast(dt.uint32), T.qu[:, 0:128].bitcast(dt.uint32).indirect(T.ulist[:, 0:16]), ["qu", "ulist"], ["qr"])
+    act(T.qr_s[:], T.qu_s[:, 0:128].indirect(T.ulist[:, 0:16]), F.Copy, ["qu", "ulist"], ["qrs"])
     quant("qx0", 0, 256, "xb", ("qx", 0), ["xb"])
-    pick_u("V", 256, 640, "ul1")
     aff("s0", "e0", 7.5, "t0", 2)
     aff("w0", "e0", "t1", 135.0, 2, 2)
     aff("y0", "x0", 16.0, 0.0, 3)
@@ -257,7 +244,7 @@ def rank_program(g, core, T, topo):
     aff("hh", "a", -1536.0, "h")
 
     def setup_search():
-        vcopy(T.cl[:, 0:5], col("s0", 5), ["s0", "s1", "w0", "w1"], ["cl"])
+        vcopy(T.cl[:, 0:5], col("s0", 5), ["s0", "s1", "w0", "pad", "w1"], ["cl"])
         for i in range(2):
             ts(T.smask[:, 16 * i:16 * i + 16], T.it16[:, 0:16], col("l"), A.is_equal, ["it16", "e%d" % i], [("smask", i)], col("e%d" % i), A.mult)
         ts(col("k0", 2), col("n0", 2), col("l"), A.not_equal, ["cf", "n0", "n1"], ["k0", "k1"], 16.0, A.mult)
@@ -280,6 +267,9 @@ def rank_program(g, core, T, topo):
         act(T.iq[:, 0:16], T.ir[:, 16:32], F.Identity, ["ir2", "iqb"], ["iq"], bias=col("iqb"))
 
     def setup_pool():
+        for s in range(2):
+            iota(T.acc[:, 16 * s:16 * s + 1], ("acc", s, 0), [[0, 1]], 0, 0)
+        iota(T.onesb[:], "onesb", [[0, 128]], 1, 0)
         iota(T.m1[:, 3:1024:4], "m1z", [[0, 256]], 0, 0)
         iota(T.m2[:, 3:1024:4], "m2z", [[0, 256]], 0, 0)
         iota(T.itb[:], "itb", [[1, 256]], 0, 0)
@@ -322,9 +312,8 @@ def rank_program(g, core, T, topo):
         total["arr%d" % t] = 2 * n_in
         total["lst%d" % t] = n_in
 
-        u0, u1 = [("qr", 0), ("qrs", 0)], [("qr", 256), ("qrs", 256)]
         for k in range(4):
-            mm(k, 256, "qr", 128 * (k // 2), qx, 0, True, True, [X] + u0)
+            mm(k, 256, "qr", 128 * (k // 2), qx, 0, True, True, [X, "qr", "qrs"])
 
         def part(name, s):
             return T[name][:, 256 * s:256 * s + 256]
@@ -336,8 +325,10 @@ def rank_program(g, core, T, topo):
             o = 2816 * s + 4 * M_AT[(16 - c) // 4] + (16 - c) % 4
             return T.mt[:, o + 4 * a:o + 4 * b - 3:4]
 
-        def lanes(s):
+        def own(s):
             tt(part("rm", s), bank(2 * s, 256), msk(0), A.add, [("K", 2 * s), ("msk", 0)], [("rm", s)])
+
+        def held(s):
             scan(part("sw", s), msk(1), part("rm", s), 0.0, A.add, A.max, [("msk", 1), ("rm", s)], [("sw", s)])
 
         def near(s):
@@ -348,8 +339,8 @@ def rank_program(g, core, T, topo):
 
         def pass_v(s, cs):
             for c in cs:
-                ts(slot(s, c, 0, 16 * c), T.rr[:, 256 * s:256 * s + 16 * c], mine(s, c), A.is_lt,
-                   [("rr", s), ("sw", s), ("mz", s, (16 - c) // 4)], [("mt", s, c)])
+                ts(slot(s, c, 0, 16 * c), bank(2 * s, 16 * c), mine(s, c), A.is_lt,
+                   [("K", 2 * s), ("sw", s), ("mz", s, (16 - c) // 4)], [("mt", s, c)])
 
         def sum_v(s, cs):
             for c in cs:
@@ -368,7 +359,7 @@ def rank_program(g, core, T, topo):
             for c in cs:
                 o = 256 * (flip[0] % 4)
                 flip[0] += 1
-                act(T.dd[:, o:o + 16 * c], T.rr[:, 256 * s:256 * s + 16 * c], F.Sign, [("rr", s), ("sw", s)], [("dd", o)], scale=-1.0, bias=mine(s, c))
+                act(T.dd[:, o:o + 16 * c], bank(2 * s + 1, 16 * c), F.Sign, [("K", 2 * s + 1), ("sw", s)], [("dd", o)], scale=-1.0, bias=mine(s, c))
                 sum_s()
                 owes.append((s, c, o))
 
@@ -379,25 +370,37 @@ def rank_program(g, core, T, topo):
 
         def over_lanes(s, tiles):
             for i in tiles:
-                mm(2 * s, M_COLS[i], "kq", 0, "mq", 704 * s + M_AT[i], i == 0, i == 1, [("kq", 0), ("mq", s, i)])
+                mm(2 * s, M_COLS[i], "kq", 0, "mq", 704 * s + M_AT[i], i == 0, i == 3, [("kq", 0), ("mq", s, i)])
 
         def along(s, a, b, src, keys):
             tt(T.uu[:, 16 * s + a:16 * s + b], T.bd[:, 16 * s + a:16 * s + b], src, A.subtract, [("bd", s)] + keys, [("uu", s, a)])
 
-        def along_v(s):
+        def along_near(s):
             tt(T.bd[:, 16 * s:16 * s + 16], T.iq[:, 16:32], T.cs[:, 256 * s + 15:256 * s + 256:16], A.subtract, ["ib", ("cs", s)], [("bd", s)])
-            for a, b in ((0, on_s[s][0]), (on_s[s][-1] + 1, 16)):
-                along(s, a, b, T.sb[:, 2048 * s + 128 * a + 127:2048 * s + 128 * b:128], [("sb", s, c) for c in range(a, b)] + ["sbz"])
+
+        def along_v(s):
+            a = on_s[s] + 1
+            along(s, a, 16, T.sb[:, 2048 * s + 128 * a + 127:2048 * s + 2048:128], [("sb", s, c) for c in range(a, 16)])
 
         def along_s(s):
-            a, b = on_s[s][0], on_s[s][-1] + 1
-            along(s, a, b, T.acc[:, 16 * s + a:16 * s + b], [("acc", s, c) for c in range(a, b)])
+            b = on_s[s] + 1
+            along(s, 0, b, T.acc[:, 16 * s:16 * s + b], [("acc", s, c) for c in range(b)])
+
+        spare = []
+
+        def fill(n=1):
+            for _i in range(min(n, len(spare))):
+                f, *args = spare.pop(0)
+                f(*args)
 
         def numbers(s):
             f = T.nf[:, 16 * s:16 * s + 16]
-            tt(f, wrap(bank(2 * s, 256), [("K", 2 * s)]), T.uu[:, 16 * s:16 * s + 16], A.add,
-               ["scn"] + [("uu", s, a) for a in range(16)], [("nf", s)])
+            row = wrap(bank(2 * s, 256), [("K", 2 * s)])
+            fill()
+            tt(f, row, T.uu[:, 16 * s:16 * s + 16], A.add, ["scn"] + [("uu", s, a) for a in range(16)], [("nf", s)])
+            fill()
             vcopy(T.nl[:, 16 * s:16 * s + 16], f, [("nf", s)], [("nl", s)])
+            fill()
 
         def unpack(src, key, dst, banks, scale):
             for b, k in enumerate(banks):
@@ -409,99 +412,95 @@ def rank_program(g, core, T, topo):
             tt(T.m2[:, s:1024:4], T.w2[:, i:i + 16].indirect(T.kl[:, 16 * s:16 * s + 16]), part("qp", s), A.is_gt,
                [("w2", min(s, 1)), "kl", ("qp", s)], [("m2", s)])
 
-        low = [list(range(on_s[s][0] - 1, 0, -1)) for s in range(2)]
-        top = [list(range(15, on_s[s][-1], -1)) for s in range(2)]
-        s2 = list(on_s[1][::-1])
-        lanes(0)
-        act(part("rr", 0), bank(1, 256), F.Copy, [("K", 1)], [("rr", 0)])
-        pass_s(0, on_s[0][::-1])
+        top = [list(range(15, on_s[s], -1)) for s in range(2)]
+        s1, s2 = (list(range(on_s[s], 0, -1)) for s in range(2))
+        own(0)
+        for i in range(2):
+            act(part("rr", i), bank(1, 256), F.Copy, [("K", 1)], [("rr", i)], scale=1.0 - 2.0 * i)
+        dmas("Y", [(T.qp[16 * q:16 * q + 16, 256 * s:256 * s + 256], T.rr[16 * o:16 * o + 16, 256 * (q < o):256 * (q < o) + 256])
+                   for s in range(3) for q in range(8) for o in [q ^ (s + 1)]], [("rr", 0), ("rr", 1)], [("qp", s) for s in range(3)])
+        own(1)
+        held(0)
+        pass_s(0, s1)
         sum_s()
-        act(part("rr", 1), bank(3, 256), F.Copy, [("K", 3)], [("rr", 1)])
-        if first:
-            pick_u("S", 256, 640, "ul1")
+        held(1)
         near(0)
         pass_v(0, top[0])
-        pass_v(0, low[0])
-        mquant(0, 0, 1)
-        lanes(1)
-        over_lanes(0, (0,))
         near_sum(0)
+        mquant(0, 0, 1)
+        over_lanes(0, (0,))
         sum_v(0, top[0])
-        mquant(0, 3, 4)
-        sum_v(0, low[0])
+        along_near(0)
+        mquant(0, 1, 2)
         along_v(0)
-        mquant(0, 1, 3)
-        over_lanes(0, (3, 2, 1))
-        for s in range(3):
-            mm(4 + s, 256, "qr", 256 + 128 * s, qx, 0, True, True, [X] + u1)
-        pass_s(1, s2[:2])
-        for s in range(3):
-            act(part("qp", s), bank(4 + s, 256), F.Copy, [("K", 4 + s), "e0", "e1"], [("qp", s)], scale=col("e%d" % min(s, 1)))
-        pass_s(1, s2[2:6])
-        along_s(0)
         near(1)
+        if first:
+            setup_search()
+        mquant(0, 2, 4)
+        over_lanes(0, (1, 2, 3))
+        pass_s(1, s2[:10])
+        along_s(0)
+        spare += [(pass_v, 1, [c]) for c in top[1]] + [(near_sum, 1)] + [(sum_v, 1, [c]) for c in top[1]] + [(along_near, 1), (along_v, 1)]
+        fill()
         numbers(0)
 
         vcopy(T.vv[:, 0:256].indirect(T.nl[:, 0:16]), part("rr", 0), [("nl", 0), ("rr", 0)], ["vv"])
-        if first:
-            setup_search()
+        fill()
         tt(T.sg[:], T.vv[:, 0:256].indirect(T.cl[:, 0:2]), T.smask[:], A.mult, ["vv", "cl", ("smask", 0), ("smask", 1)], ["sg"])
         scan(T.vs[:], msk(2), T.vv[:], 0.0, A.add, A.max, [("msk", 2), "vv"], ["vs"])
         scan(T.sig[:], msk(4, 32), T.sg[:], 0.0, A.mult, A.add, [("msk", 4), "sg"], ["sig"])
         for i in range(2):
             act(T.w2[:, 16 * i:16 * i + 16], T.vs[:, 0:256].indirect(T.cl[:, 2 + 2 * i:3 + 2 * i]), F.Copy, ["vs", "cl", "e%d" % i],
                 [("w2", i)], scale=col("e%d" % i))
-        pass_s(1, s2[6:])
+        pass_s(1, s2[10:])
         sum_s()
         if first:
             act(T.itb[:], T.itb[:], F.Identity, ["itb", "ak"], ["itb"], bias=col("ak"))
-            setup_unpack()
-        unpack(land, land, "fp", (4, 5, 6, 3), 0.5)
-        spread("S", "win", "fp", 1024, [("fp", b) for b in range(4)])
-        near_sum(1)
+        fill()
         for s in range(3):
             i = 16 * min(s, 1) + 15
             ts(T.m1[:, s:1024:4], part("qp", s), T.sig[:, i:i + 1], A.is_lt, [("qp", s), "sig", "k0", "k1"], [("m1", s)],
                col("k%d" % min(s, 1)), A.mult)
+        fill()
         quant("m1q", 0, 256, "m1", "m1q", [("m1", s) for s in range(3)] + ["m1z"])
         mm(7, 256, "kq", 128, "m1q", 0, True, True, [("kq", 1), "m1q"])
-        pass_v(1, top[1][:2])
-        if first:
-            setup_counts()
-        for k, a in ((0, 256), (1, 512)):
-            mm(k, 256, "kq", a, "m1q", 0, True, False, [("kq", 2), "m1q"])
-        ts(T.ki[:, 48:64], wrap(bank(7, 256), [("K", 7)]), col("ramp"), A.add, ["scn", "ramp"], ["kp"])
-        pass_v(1, top[1][2:])
-        for s in range(3):
-            ts(T.ki[:, 16 * s:16 * s + 16], T.ki[:, 48:64], 4 * s, A.logical_shift_right, ["kp"], [("ki", s)], 15, A.bitwise_and)
-        pass_v(1, low[1])
-        sum_v(1, top[1][:1])
-        vcopy(T.kl[:], T.ki[:, 0:48], [("ki", s) for s in range(3)], ["kl"])
         mquant(1, 0, 1)
         over_lanes(1, (0,))
-        sum_v(1, top[1][1:])
-        sum_v(1, low[1])
-        second_step(0)
+        fill()
+        if first:
+            setup_counts()
+            setup_unpack()
+        for k, a in ((0, 256), (1, 512)):
+            mm(k, 256, "kq", a, "m1q", 0, True, False, [("kq", 2), "m1q"])
+        unpack(land, land, "fp", (4, 5, 6, 3), 0.5)
+        spread("S", "win", "fp", 1024, [("fp", b) for b in range(4)])
+        row = wrap(bank(7, 256), [("K", 7)])
+        fill()
+        ts(T.ki[:, 48:64], row, col("ramp"), A.add, ["scn", "ramp"], ["kp"])
+        fill()
+        for s in range(3):
+            ts(T.ki[:, 16 * s:16 * s + 16], T.ki[:, 48:64], 4 * s, A.logical_shift_right, ["kp"], [("ki", s)], 15, A.bitwise_and)
+        fill()
+        vcopy(T.kl[:], T.ki[:, 0:48], [("ki", s) for s in range(3)], ["kl"])
+        fill(16)
         if first:
             setup_wlist()
             setup_merge()
+        second_step(0)
         mquant(1, 1, 4)
-        over_lanes(1, (3, 2, 1))
-        along_v(1)
+        over_lanes(1, (1, 2, 3))
         along_s(1)
         second_step(1)
+        spare.append((second_step, 2))
         numbers(1)
-        vcopy(T.leaf[:, 0:256].indirect(T.nl[:, 16:32]), T.itb[:], ["itb", ("nl", 1)], ["leaf"])
-        spread("Y", "lw", "leaf", 256, ["leaf"])
-        second_step(2)
         quant("m2q", 0, 256, "m2", "m2q", [("m2", s) for s in range(3)] + ["m2z"])
         for k, a in ((0, 256), (1, 384)):
             mm(k, 256, "kq", a, "m2q", 0, False, True, [("kq", 2), "m2q"])
-        ts(T.nx[:], T.nf[:, 16:32], col("off"), A.add, [("nf", 1), "off"], ["nx"])
-        if last:
-            quant("qv", 0, 128, "vb", "qv", ["vb"])
+        vcopy(T.leaf[:, 0:256].indirect(T.nl[:, 16:32]), T.itb[:], ["itb", ("nl", 1)], ["leaf"])
+        spread("Y", "lw", "leaf", 256, ["leaf"], range(5))
 
         act(T.dat[:], bank(1, 256), F.Copy, [("K", 1)], ["dat"])
+        spread("S", "lw", "leaf", 256, ["leaf"], range(5, 8))
         tt(T.tq[:], wrap(bank(0, 256), [("K", 0)]), T.nf[:, 0:16], A.add, ["scn", ("nf", 0)], ["tq"])
         act(T.c0s[:], bank(0, 256), F.Copy, [("K", 0)], ["c0s"])
         ts(T.pl[:], T.tq[:], col("off"), A.add, ["tq", "off"], ["pl"])
@@ -513,14 +512,17 @@ def rank_program(g, core, T, topo):
         mm(5, 256, "kq", 640, "qw", 0, True, True, [("kq", 5), "qw"])
         if first:
             setup_w("V", (0,))
+        if last:
+            quant("qv", 0, 128, "vb", "qv", ["vb"])
         tt(T.tq[:], T.iq[:, 0:16], wrap(bank(5, 256), [("K", 5)]), A.subtract, ["scn", "iq"], ["tq"])
         vcopy(T.ql[:], T.tq[:], ["tq"], ["ql"])
-        vcopy(T.crow[:], T.lw[:, 0:1024].indirect(T.ql[:, 0:16]), ["lw", "ql"], ["crow"])
+        vcopy(T.crow[:], T.lw[:, 0:1024].indirect(T.ql[:, 0:16]), [("lw", q) for q in range(8)] + ["ql"], ["crow"])
         el = T.el[:, 16 * t:16 * t + 16]
         ts(el, wrap(T.crow[:], ["crow"]), col("ramp"), A.add, ["scn", "ramp"], [("el", t)])
         remote(T[lin][:], el, "lst%d" % t, [("el", t)])
 
         vcopy(T.csort[:, 0:256].indirect(T.nl[:, 0:16]), T.c0s[:], [("nl", 0), "c0s"], ["csort"])
+        ts(T.nx[:], T.nf[:, 16:32], col("off"), A.add, [("nf", 1), "off"], ["nx"])
         vcopy(T.crow[:], T.csort[:, 0:256].indirect(T.nl[:, 16:32]), ["csort", ("nl", 1)], ["crow"])
         tt(T.xi[:, 0:16], wrap(T.crow[:], ["crow"]), T.nx[:], A.add, ["scn", "nx"], ["xi"])
         ts(T.xi[:, 16:32], T.xi[:, 0:16], 511, A.bitwise_and, ["xi"], ["xi2"])
@@ -530,10 +532,13 @@ def rank_program(g, core, T, topo):
         if first:
             setup_w("V", (1,))
 
+        def picked(b, i):
+            return T.win[:, 256 * b:256 * b + 3328].indirect(T[lin][:, 8 * i:8 * i + 8])
+        vcopy(T.etmp[:, 384:512], picked(3, 0), [("win", 0), lin], [("etmp", 3)])
         for b in range(4):
-            w = T.win[:, 256 * b:256 * b + 3328]
-            act(T.etmp[:, 128 * b:128 * b + 128], w.indirect(T[lin][:, 0:8]), F.Copy, ["win", lin], [("etmp", b)])
-            tt(T.eb[:, b:512:4], w.indirect(T[lin][:, 8:16]), T.etmp[:, 128 * b:128 * b + 128], A.add, ["win", lin, ("etmp", b)], [("eb", b)])
+            if b < 3:
+                act(T.etmp[:, 128 * b:128 * b + 128], picked(b, 0), F.Copy, [("win", 0), lin], [("etmp", b)])
+            tt(T.eb[:, b:512:4], picked(b, 1), T.etmp[:, 128 * b:128 * b + 128], A.add, [("win", 0), lin, ("etmp", b)], [("eb", b)])
         if last:
             act(T.dfull[:], T.vv[:, 0:256].indirect(T.nl[:, 16:32]), F.Identity, ["vv", ("nl", 1), "hh"], ["dfull"], scale=2.0, bias=col("hh"))
             dmas("Y", [(T.op[:, :], T.dfull[0:128:16, :])], ["dfull"], ["op"])

@@ -19,20 +19,20 @@ for _t in range(R):
     _q("qx%d" % _t, 256)
     _q("land%d" % _t, 256)
     _b("lin%d" % _t, 16, "uint16")
-for _n, _w in (("qx3", 256), ("qu", 128), ("qr", 256), ("qv", 128), ("wq", 512), ("qwr", 2048), ("kq", 768), ("mq", 1408),
+for _n, _w in (("qx3", 256), ("qu", 128), ("qr", 256), ("qv", 128), ("wq", 512), ("qwr", 2048), ("kq", 642), ("mq", 1408),
                ("cid", 512), ("m1q", 256), ("m2q", 256), ("qw", 256), ("qe", 128)):
     _q(_n, _w)
-for _n, _w in (("xb", 1024), ("xs", 1024), ("ub", 512), ("vb", 512), ("zero", 1024), ("zc", 528), ("kb", 3072), ("onesb", 128),
-               ("gcol", 224), ("colid", 136), ("it16", 256), ("msks", 1280), ("cs", 512), ("mt", 5632), ("sb", 4096),
+for _n, _w in (("xb", 1024), ("xs", 1024), ("ub", 512), ("vb", 512), ("zero", 1024), ("zc", 528), ("kb", 2568), ("onesb", 128),
+               ("gcol", 128), ("colid", 140), ("it16", 256), ("msks", 1536), ("cs", 512), ("mt", 5632), ("sb", 4096),
                ("dd", 1024), ("m1", 1024), ("m2", 1024), ("win", 4096), ("winh", 2048), ("fx", 1024), ("fp", 1024), ("etmp", 512),
                ("eb", 512), ("ww", 1024), ("dat", 256)):
     _b(_n, _w, "bfloat16")
 for _n in ("itb", "scn", "vv", "vs", "leaf", "c0s", "csort", "crow", "dfull", "ysb"):
     _b(_n, 256, "float32")
-for _n, _w in (("lw", 1024), ("rr", 512), ("rm", 512), ("sw", 512), ("qp", 768), ("cf", 48), ("acc", 32), ("bd", 32), ("uu", 32),
-               ("nf", 32), ("nx", 16), ("smask", 32), ("sg", 32), ("sig", 32), ("w2", 32), ("iq", 32), ("ir", 32), ("tq", 16)):
+for _n, _w in (("lw", 1024), ("rr", 512), ("rm", 512), ("sw", 512), ("qp", 768), ("cf", 48), ("acc", 32), ("nf", 32), ("nx", 16),
+               ("smask", 32), ("sg", 32), ("sig", 32), ("w2", 32), ("iq", 16), ("ir", 32), ("tq", 16)):
     _b(_n, _w, "float32")
-for _n, _w in (("ci", 16), ("il", 16), ("il2", 128), ("il3", 128), ("ki", 64), ("xi", 32)):
+for _n, _w in (("ci", 8), ("il", 16), ("il2", 128), ("il3", 128), ("ki", 64), ("xi", 32)):
     _b(_n, _w, "int32")
 for _n, _w in (("ulist", 16), ("wlist", 128), ("cl", 8), ("nl", 32), ("kl", 48), ("pl", 16), ("ql", 16), ("xl", 16), ("el", 48)):
     _b(_n, _w, "uint16")
@@ -45,6 +45,7 @@ ON_S = (8, 13)
 ON_S_FIRST = (8, 14)
 M_AT, M_COLS = (0, 256, 448, 576), (256, 192, 128, 128)
 H_ON_V = (1, 3, 5, 7, 11)
+H_ON_V_FIRST = (5, 7, 11)
 
 
 def rank_program(g, core, T, topo):
@@ -147,14 +148,8 @@ def rank_program(g, core, T, topo):
     def act(out, in_, f, reads, writes, **kw):
         op("S", S.activation, (out, in_, f), reads, writes, **kw)
 
-    def memset(ap, c, writes, reads=()):
-        op("V", V.memset, (ap, c), list(reads), writes)
-
-    def iota(ap, key, pat, base, cm):
-        op("G", g.iota, (ap, pat, base, cm), [], [key], allow_small_or_imprecise_dtypes=True)
-
-    def select(out, in_, pat, cmp, base, cm, reads, writes):
-        op("G", g.affine_select, (out, in_, pat, cmp, 0.0, base, cm), reads, writes)
+    def iota(ap, key, pat, base, cm, reads=()):
+        op("G", g.iota, (ap, pat, base, cm), reads, [key], allow_small_or_imprecise_dtypes=True)
 
     def spread(e, dst, src, n, reads, qs=range(8)):
         dmas(e, [(T[dst][16 * q:16 * q + 16, n * a:n * a + n], T[src][64 * (q % 2) + 16 * a:64 * (q % 2) + 16 * a + 16, :])
@@ -163,8 +158,8 @@ def rank_program(g, core, T, topo):
     dmas("S", [(T.ub[:], T.u[:, :])], [], ["ub"])
     dmas("Y", [(T.xb[:], T.x[:, :])], [], ["xb"])
 
-    names = ("p", "l", "a0", "a1", "h", "g", "a", "m", "odd", "e0", "e1", "x0", "x1", "x2", "y0", "y1", "y2", "ramp", "off", "t0", "t1",
-             "s0", "s1", "w0", "pad", "w1", "n0", "n1", "k0", "k1", "f0", "f1", "wm", "iqb", "ak", "bb", "hh")
+    names = ("p", "l", "a0", "a1", "h", "g", "a", "m", "e0", "e1", "x0", "x1", "x2", "y0", "y1", "y2", "ramp", "off", "t0", "t1",
+             "s0", "s1", "w0", "pad", "w1", "n0", "n1", "k0", "k1", "iqb", "ak", "bb", "hh")
     C = {k: i for i, k in enumerate(names)}
 
     def col(k, n=1, step=1):
@@ -178,18 +173,19 @@ def rank_program(g, core, T, topo):
     def msk(k, n=256):
         return T.msks[:, 256 * k:256 * k + n]
 
-    iota(T.ci[:, 0:9], "ci", [[0, 9]], 0, 1)
+    iota(T.ci[:], "ci", [[0, 8]], 0, 1)
     iota(T.il[:], "il", [[1, 2], [16, 8]], 0, 0)
     iota(T.it16[:], "it16", [[0, 16], [1, 16]], 0, 0)
-    iota(T.gcol[:], "gcol", [[1, 14], [0, 16]], -6, 0)
+    iota(T.gcol[:], "gcol", [[1, 8], [0, 16]], 0, 0)
     iota(T.ir[:, 0:16], "ir", [[16, 16]], 15, 0)
     iota(col("pad"), "pad", [[0, 1]], 0, 0)
-    iota(T.colid[:], "colid", [[1, 136]], -5, 0)
+    iota(msk(5), "m5", [[0, 256]], int(STEP), 0)
+    iota(T.colid[:], "colid", [[1, 140]], -10, 0)
     iota(T.ir[:, 16:32], "ir2", [[64, 16]], 15 * int(STEP), 0)
-    memset(T.zero[:], 0.0, ["zero"])
-    for k, sh, an in (("l", 0, 15), ("a0", 4, 1), ("a1", 5, 1), ("h", 6, 1), ("g", 4, 7), ("a", 4, 3), ("m", 5, 3), ("odd", 0, 1)):
+    op("V", V.memset, (T.zero[:], 0.0), [], ["zero"])
+    for k, sh, an in (("l", 0, 15), ("a0", 4, 1), ("a1", 5, 1), ("h", 6, 1), ("g", 4, 7), ("a", 4, 3), ("m", 5, 3)):
         ts(T.ci[:, C[k]:C[k] + 1], T.ci[:, 0:1], sh, A.logical_shift_right, ["ci"], ["ci" + k], an, A.bitwise_and)
-    vcopy(T.cf[:, 0:9], T.ci[:, 0:9], ["ci"] + ["ci" + k for k in names[1:9]], ["cf"])
+    vcopy(T.cf[:, 0:8], T.ci[:], ["ci"] + ["ci" + k for k in names[1:8]], ["cf"])
     vcopy(T.ulist[:], T.il[:], ["il"], ["ulist"])
     tails = [(4 * (M_AT[i] + (M_COLS[i] - 48 if i < 3 else 16)), 4 * (M_AT[i] + M_COLS[i])) for i in range(4)]
     ts(msk(0), T.it16[:], col("l"), A.not_equal, ["it16", "cf"], [("msk", 0)], -BIG, A.mult)
@@ -199,46 +195,43 @@ def rank_program(g, core, T, topo):
         dmas("Y", [(T.mt[:, 2816 * s + a:2816 * s + b], T.zero[:, 0:b - a]) for a, b in tails], ["zero"], [("mz", s, i) for i in range(4)])
     dmas("Y", [(cv("wq", 0, 512), T.wc[:, :])], [], ["wq"])
     dmas("Y", [(T.wq_s[:], T.ws[:, :])], [], ["wqs"])
-    dmas("Y", [(T.kb[:, a:b], T.zero[:, 0:b - a]) for a, b in ((512, 1536), (1536, 2560))], ["zero"], ["kbz"])
+    dmas("Y", [(T.kb[:, a:b], T.zero[:, 0:b - a]) for a, b in ((1024, 2048), (2048, 2568))], ["zero"], ["kbz"])
     dmas("Y", [(T.zc[:], T.zero[:, 0:528])], ["zero"], ["zz"])
     dmas("Y", [(T.vb[:], T.v[:, :])], [], ["vb"])
     aff("e0", "a0", 2.0, -1.0, 2)
     aff("ramp", "l", STEP, -15.0 * STEP)
-    aff("bb", "l", STEP - 1.0, -15.0 * STEP)
-    act(T.iq[:, 16:32], T.ir[:, 0:16], F.Identity, ["ir", "bb"], ["ib"], bias=col("bb"))
+    act(T.msks[:, 1280:1536:16], T.ir[:, 0:16], F.Identity, ["ir", "cf", "m5"], [("msk", 5)], scale=-1.0, bias=col("l"))
+    aff("bb", "ramp", 2.0, 0.0)
     aff("x0", "e0", -1.0, "g")
     aff("x1", "e1", -2.0, "g")
-    aff("off", "a", 256.0, "ramp")
+    aff("off", "a", 256.0, "bb")
     aff("t0", "l", 16.0, 7.5)
     aff("t1", "l", 16.0, -120.0)
     aff("x2", "e0", -1.0, "x1")
     aff("n0", "e0", 7.5, 7.5, 2)
 
-    def gcol(shift=0):
-        return T.gcol[:, 96 - 16 * shift:224 - 16 * shift]
-
-    def ktile(i, t, src, k, w):
-        ts(T.kb[:, 512 * i + t:512 * i + 512:4], src, col(k), A.is_equal,
-           ["colid" if i in (3, 4) else "gcol", "cf", "kbz" if 0 < i < 5 else "cf", k] + [w] * isinstance(w, str),
+    def ktile(i, t, src, k, w, n=128):
+        ts(T.kb[:, 512 * i + t:512 * i + 4 * n:4], src, col(k), A.is_equal,
+           ["colid" if i == 3 else "gcol", "cf", "kbz" if i > 1 else "cf", k] + [w] * isinstance(w, str),
            [("kb", i, t)], col(w) if isinstance(w, str) else w, A.mult)
 
-    def kquant(a, b):
-        quant("kq", 128 * a, 128 * b, "kb", ("kq", a), [("kb", i, t) for i in range(a, b) for t in range(4)], s0=512 * a)
+    def kquant(i, a, b, tiles):
+        quant("kq", a, b, "kb", ("kq", i), [("kb", j, t) for j in tiles for t in range(4)], s0=4 * a)
 
     for t in range(4):
-        ktile(0, t, gcol(), "g", 1.0)
-    kquant(0, 1)
+        ktile(0, t, T.gcol[:], "g", 1.0)
+    kquant(0, 0, 128, (0,))
     ts(msk(2), msk(0), -1.0, A.mult, [("msk", 0)], [("msk", 2)], -BIG, A.add)
     ts(msk(3), msk(2), STEP, A.add, [("msk", 2)], [("msk", 3)])
     quant("qu", 0, 128, "ub", "qu", ["ub"])
     vcopy(T.qr[:].bitcast(dt.uint32), T.qu[:, 0:128].bitcast(dt.uint32).indirect(T.ulist[:, 0:16]), ["qu", "ulist"], ["qr"])
     act(T.qr_s[:], T.qu_s[:, 0:128].indirect(T.ulist[:, 0:16]), F.Copy, ["qu", "ulist"], ["qrs"])
     quant("qx0", 0, 256, "xb", ("qx", 0), ["xb"])
+    for t in range(4):
+        ktile(1, t, T.gcol[:], "g", 16.0 ** (t - 1) * (t < 3))
     aff("s0", "e0", 7.5, "t0", 2)
     aff("w0", "e0", "t1", 135.0, 2, 2)
     aff("y0", "x0", 16.0, 0.0, 3)
-    aff("f0", "e0", 0.0625, 0.0, 2)
-    aff("wm", "odd", -15.0, 16.0)
     aff("iqb", "l", 4.0 - STEP, "m")
     aff("ak", "a", 1024.0, 0.0)
     aff("hh", "a", -1536.0, "h")
@@ -248,23 +241,15 @@ def rank_program(g, core, T, topo):
         for i in range(2):
             ts(T.smask[:, 16 * i:16 * i + 16], T.it16[:, 0:16], col("l"), A.is_equal, ["it16", "e%d" % i], [("smask", i)], col("e%d" % i), A.mult)
         ts(col("k0", 2), col("n0", 2), col("l"), A.not_equal, ["cf", "n0", "n1"], ["k0", "k1"], 16.0, A.mult)
-        for t in range(3):
-            ktile(1, t, gcol(), "g", 16.0 ** (t - 1))
-        kquant(1, 2)
+        kquant(1, 128, 256, (1,))
 
-    def setup_counts():
-        for t in range(3):
-            i = min(t, 1)
-            ktile(2, t, gcol(), "x%d" % t, "e%d" % i)
-            ktile(3, t, T.colid[:, 4 - 2 * t:132 - 2 * t], "y%d" % t, "e%d" % i)
-            ktile(4, t, T.colid[:, 5 - 2 * t:133 - 2 * t], "y%d" % t, "f%d" % i)
-        kquant(2, 5)
+    def setup_counts(t):
+        ktile(2, t, T.gcol[:], "x%d" % t, "e%d" % min(t, 1))
+        ktile(3, t, T.colid[:, 8 - 4 * t:138 - 4 * t], "y%d" % t, "e%d" % min(t, 1), 130)
 
     def setup_merge():
-        for t in range(4):
-            ktile(5, t, gcol(2 * t), "h", "wm")
-        kquant(5, 6)
-        act(T.iq[:, 0:16], T.ir[:, 16:32], F.Identity, ["ir2", "iqb"], ["iq"], bias=col("iqb"))
+        kquant(4, 514, 642, (4, 5))
+        act(T.iq[:], T.ir[:, 16:32], F.Identity, ["ir2", "iqb"], ["iq"], bias=col("iqb"))
 
     def setup_pool():
         for s in range(2):
@@ -273,24 +258,31 @@ def rank_program(g, core, T, topo):
         iota(T.m1[:, 3:1024:4], "m1z", [[0, 256]], 0, 0)
         iota(T.m2[:, 3:1024:4], "m2z", [[0, 256]], 0, 0)
         iota(T.itb[:], "itb", [[1, 256]], 0, 0)
-        select(T.zc[:, 4:516:4], T.onesb[:], [[-1, 128]], A.is_equal, 0, 1, ["onesb", "zz"], ["zc"])
-        iota(T.il2[:], "il2", [[32, 16], [16, 2], [0, 4]], 0, 0)
+        op("G", g.affine_select, (T.zc[:, 4:516:4], T.onesb[:], [[-1, 128]], A.is_equal, 0.0, 0, 1), ["onesb", "zz"], ["zc"])
+        before = "zc"
+        for t in range(4):
+            for h in range(2):
+                a = 2056 + 128 * t + 64 * h + t
+                iota(T.kb[64 * h:64 * h + 64, a:a + 61:4], ("kb", 4 + h, t), [[0, 16]], 1, 0, ["kbz", before])
+                before = ("kb", 4 + h, t)
+        iota(T.il2[:], "il2", [[32, 16], [16, 2], [0, 4]], 0, 0, [before])
 
-    def setup_unpack():
-        for b in range(4):
-            quant("cid", 128 * b, 128 * b + 128, "zc", ("cid", b), ["zz", "zc"], s0=4 - b)
+    def setup_unpack(b):
+        quant("cid", 128 * b, 128 * b + 128, "zc", ("cid", b), ["zz", "zc"], s0=4 - b)
 
-    def setup_wlist():
-        ts(T.il3[:], T.il2[:], col("l"), A.add, ["il2", "cf"], ["il3"])
-        vcopy(T.wlist[:], T.il3[:], ["il3"], ["wlist"])
+    def setup_wlist(i):
+        if i == 0:
+            ts(T.il3[:], T.il2[:], col("l"), A.add, ["il2", "cf"], ["il3"])
+        else:
+            vcopy(T.wlist[:], T.il3[:], ["il3"], ["wlist"])
 
-    def setup_w(e, bs):
-        for b in bs:
-            a, lst = 512 * b, T.wlist[:, 32 * b:32 * b + 32]
+    def setup_w(e, *pieces):
+        for i in pieces:
+            a, lst = 256 * i, T.wlist[:, 16 * i:16 * i + 16]
             if e == "V":
-                vcopy(T.qwr[:, a:a + 512].bitcast(dt.uint32), T.wq[:, 0:512].bitcast(dt.uint32).indirect(lst), ["wq", "wlist"], [("qwr", b)])
+                vcopy(T.qwr[:, a:a + 256].bitcast(dt.uint32), T.wq[:, 0:512].bitcast(dt.uint32).indirect(lst), ["wq", "wlist"], [("qwr", i)])
             else:
-                act(T.qwr_s[:, a:a + 512], T.wq_s[:, 0:512].indirect(lst), F.Copy, ["wqs", "wlist"], [("qwrs", b)])
+                act(T.qwr_s[:, a:a + 256], T.wq_s[:, 0:512].indirect(lst), F.Copy, ["wqs", "wlist"], [("qwrs", i)])
 
     def wrap(src, keys):
         scan(T.scn[:], msk(3), src, 0.0, A.add, A.max, keys + [("msk", 3)], ["scn"])
@@ -335,7 +327,7 @@ def rank_program(g, core, T, topo):
             tt(slot(s, 16, 0, 256), part("sw", s), bank(2 * s, 256), A.is_ge, [("sw", s), ("K", 2 * s), ("mz", s, 0)], [("mt", s, 16)])
 
         def near_sum(s):
-            scan(part("cs", s), msk(4), slot(s, 16, 0, 256), 0.0, A.mult, A.add, [("msk", 4), ("mt", s, 16)], [("cs", s)])
+            scan(part("cs", s), msk(5), slot(s, 16, 0, 256), 0.0, A.min, A.add, [("msk", 5), ("mt", s, 16)], [("cs", s)])
 
         def pass_v(s, cs):
             for c in cs:
@@ -345,7 +337,8 @@ def rank_program(g, core, T, topo):
         def sum_v(s, cs):
             for c in cs:
                 a = 2048 * s + 128 * c + 128
-                scan(T.sb[:, a - 8 * c:a], slot(s, c, 0, 8 * c), slot(s, c, 8 * c, 16 * c), 0.0, A.add, A.add, [("mt", s, c)], [("sb", s, c)])
+                scan(T.sb[:, a - 8 * c:a], slot(s, c, 0, 8 * c), slot(s, c, 8 * c, 16 * c),
+                     T.cs[:, 256 * s + 16 * c + 15:256 * s + 16 * c + 16], A.add, A.add, [("mt", s, c), ("cs", s)], [("sb", s, c)])
 
         flip, owes = [0], []
 
@@ -363,6 +356,11 @@ def rank_program(g, core, T, topo):
                 sum_s()
                 owes.append((s, c, o))
 
+        def along_s(s):
+            b = on_s[s] + 1
+            tt(T.sb[:, 2048 * s + 127:2048 * s + 128 * b:128], T.acc[:, 16 * s:16 * s + b], T.cs[:, 256 * s + 15:256 * s + 16 * b:16], A.add,
+               [("acc", s, c) for c in range(b)] + [("cs", s)], [("sb", s, c) for c in range(b)])
+
         def mquant(s, i, j):
             a, b = M_AT[i], M_AT[j - 1] + M_COLS[j - 1]
             op("V", V.quantize_mx, (T.mq[:, 704 * s + a:704 * s + b], T.mq_s[:, 704 * s + a:704 * s + b], T.mt[:, 2816 * s + 4 * a:2816 * s + 4 * b]),
@@ -371,20 +369,6 @@ def rank_program(g, core, T, topo):
         def over_lanes(s, tiles):
             for i in tiles:
                 mm(2 * s, M_COLS[i], "kq", 0, "mq", 704 * s + M_AT[i], i == 0, i == 3, [("kq", 0), ("mq", s, i)])
-
-        def along(s, a, b, src, keys):
-            tt(T.uu[:, 16 * s + a:16 * s + b], T.bd[:, 16 * s + a:16 * s + b], src, A.subtract, [("bd", s)] + keys, [("uu", s, a)])
-
-        def along_near(s):
-            tt(T.bd[:, 16 * s:16 * s + 16], T.iq[:, 16:32], T.cs[:, 256 * s + 15:256 * s + 256:16], A.subtract, ["ib", ("cs", s)], [("bd", s)])
-
-        def along_v(s):
-            a = on_s[s] + 1
-            along(s, a, 16, T.sb[:, 2048 * s + 128 * a + 127:2048 * s + 2048:128], [("sb", s, c) for c in range(a, 16)])
-
-        def along_s(s):
-            b = on_s[s] + 1
-            along(s, 0, b, T.acc[:, 16 * s:16 * s + b], [("acc", s, c) for c in range(b)])
 
         spare = []
 
@@ -397,9 +381,9 @@ def rank_program(g, core, T, topo):
             f = T.nf[:, 16 * s:16 * s + 16]
             row = wrap(bank(2 * s, 256), [("K", 2 * s)])
             fill()
-            tt(f, row, T.uu[:, 16 * s:16 * s + 16], A.add, ["scn"] + [("uu", s, a) for a in range(16)], [("nf", s)])
+            tt(f, row, T.sb[:, 2048 * s + 127:2048 * s + 2048:128], A.subtract, ["scn"] + [("sb", s, c) for c in range(16)], [("nf", s)])
             fill()
-            vcopy(T.nl[:, 16 * s:16 * s + 16], f, [("nf", s)], [("nl", s)])
+            ts(T.nl[:, 16 * s:16 * s + 16], f, col("ramp"), A.add, [("nf", s), "ramp"], [("nl", s)])
             fill()
 
         def unpack(src, key, dst, banks, scale):
@@ -430,17 +414,16 @@ def rank_program(g, core, T, topo):
         mquant(0, 0, 1)
         over_lanes(0, (0,))
         sum_v(0, top[0])
-        along_near(0)
         mquant(0, 1, 2)
-        along_v(0)
-        near(1)
         if first:
             setup_search()
         mquant(0, 2, 4)
         over_lanes(0, (1, 2, 3))
         pass_s(1, s2[:10])
         along_s(0)
-        spare += [(pass_v, 1, [c]) for c in top[1]] + [(near_sum, 1)] + [(sum_v, 1, [c]) for c in top[1]] + [(along_near, 1), (along_v, 1)]
+        spare += [(near, 1)] + [(pass_v, 1, [c]) for c in top[1]] + [(near_sum, 1)] + [(sum_v, 1, [c]) for c in top[1]]
+        if first:
+            spare += [(setup_counts, i) for i in range(3)] + [(kquant, 2, 256, 514, (2, 3))] + [(setup_unpack, b) for b in range(4)]
         fill()
         numbers(0)
 
@@ -466,11 +449,10 @@ def rank_program(g, core, T, topo):
         mm(7, 256, "kq", 128, "m1q", 0, True, True, [("kq", 1), "m1q"])
         mquant(1, 0, 1)
         over_lanes(1, (0,))
-        fill()
+        fill(16)
         if first:
-            setup_counts()
-            setup_unpack()
-        for k, a in ((0, 256), (1, 512)):
+            spare += [(setup_wlist, 0), (setup_merge,), (setup_wlist, 1)]
+        for k, a in ((0, 256), (1, 386)):
             mm(k, 256, "kq", a, "m1q", 0, True, False, [("kq", 2), "m1q"])
         unpack(land, land, "fp", (4, 5, 6, 3), 0.5)
         spread("S", "win", "fp", 1024, [("fp", b) for b in range(4)])
@@ -482,10 +464,6 @@ def rank_program(g, core, T, topo):
             ts(T.ki[:, 16 * s:16 * s + 16], T.ki[:, 48:64], 4 * s, A.logical_shift_right, ["kp"], [("ki", s)], 15, A.bitwise_and)
         fill()
         vcopy(T.kl[:], T.ki[:, 0:48], [("ki", s) for s in range(3)], ["kl"])
-        fill(16)
-        if first:
-            setup_wlist()
-            setup_merge()
         second_step(0)
         mquant(1, 1, 4)
         over_lanes(1, (1, 2, 3))
@@ -507,49 +485,63 @@ def rank_program(g, core, T, topo):
         vcopy(T.ww[:, 0:1024].indirect(T.pl[:, 0:16]), T.dat[:], ["pl", "dat"], ["ww"])
         unpack(qx, X, "fx", (2, 3, 4, 6), 1.0)
         if first:
-            setup_w("S", range(4))
+            spare += [(setup_w, "V", i) for i in range(8)]
+            setup_w("S", 0, 1)
+
+        def gather(out, src, reads, writes):
+            if first:
+                act(out, src, F.Copy, reads, writes)
+                fill()
+            else:
+                vcopy(out, src, reads, writes)
         quant("qw", 0, 256, "ww", "qw", ["ww"])
-        mm(5, 256, "kq", 640, "qw", 0, True, True, [("kq", 5), "qw"])
-        if first:
-            setup_w("V", (0,))
+        mm(5, 256, "kq", 514, "qw", 0, True, True, [("kq", 4), "qw"])
+        fill()
         if last:
             quant("qv", 0, 128, "vb", "qv", ["vb"])
-        tt(T.tq[:], T.iq[:, 0:16], wrap(bank(5, 256), [("K", 5)]), A.subtract, ["scn", "iq"], ["tq"])
+        tt(T.tq[:], T.iq[:], wrap(bank(5, 256), [("K", 5)]), A.subtract, ["scn", "iq"], ["tq"])
         vcopy(T.ql[:], T.tq[:], ["tq"], ["ql"])
-        vcopy(T.crow[:], T.lw[:, 0:1024].indirect(T.ql[:, 0:16]), [("lw", q) for q in range(8)] + ["ql"], ["crow"])
+        gather(T.crow[:], T.lw[:, 0:1024].indirect(T.ql[:, 0:16]), [("lw", q) for q in range(8)] + ["ql"], ["crow"])
         el = T.el[:, 16 * t:16 * t + 16]
         ts(el, wrap(T.crow[:], ["crow"]), col("ramp"), A.add, ["scn", "ramp"], [("el", t)])
         remote(T[lin][:], el, "lst%d" % t, [("el", t)])
+        if first:
+            setup_w("S", 2, 3)
 
         vcopy(T.csort[:, 0:256].indirect(T.nl[:, 0:16]), T.c0s[:], [("nl", 0), "c0s"], ["csort"])
         ts(T.nx[:], T.nf[:, 16:32], col("off"), A.add, [("nf", 1), "off"], ["nx"])
-        vcopy(T.crow[:], T.csort[:, 0:256].indirect(T.nl[:, 16:32]), ["csort", ("nl", 1)], ["crow"])
+        gather(T.crow[:], T.csort[:, 0:256].indirect(T.nl[:, 16:32]), ["csort", ("nl", 1)], ["crow"])
         tt(T.xi[:, 0:16], wrap(T.crow[:], ["crow"]), T.nx[:], A.add, ["scn", "nx"], ["xi"])
         ts(T.xi[:, 16:32], T.xi[:, 0:16], 511, A.bitwise_and, ["xi"], ["xi2"])
         vcopy(T.xl[:], T.xi[:, 16:32], ["xi2"], ["xl"])
         if last:
             tt(T.vv[:], T.csort[:], T.itb[:], A.add, ["csort", "itb"], ["vv"])
         if first:
-            setup_w("V", (1,))
+            setup_w("S", 4, 5)
+        fill()
 
         def picked(b, i):
             return T.win[:, 256 * b:256 * b + 3328].indirect(T[lin][:, 8 * i:8 * i + 8])
-        vcopy(T.etmp[:, 384:512], picked(3, 0), [("win", 0), lin], [("etmp", 3)])
+        if first:
+            fill()
+        else:
+            vcopy(T.etmp[:, 384:512], picked(3, 0), [("win", 0), lin], [("etmp", 3)])
         for b in range(4):
-            if b < 3:
+            if b < 3 or first:
                 act(T.etmp[:, 128 * b:128 * b + 128], picked(b, 0), F.Copy, [("win", 0), lin], [("etmp", b)])
             tt(T.eb[:, b:512:4], picked(b, 1), T.etmp[:, 128 * b:128 * b + 128], A.add, [("win", 0), lin, ("etmp", b)], [("eb", b)])
         if last:
             act(T.dfull[:], T.vv[:, 0:256].indirect(T.nl[:, 16:32]), F.Identity, ["vv", ("nl", 1), "hh"], ["dfull"], scale=2.0, bias=col("hh"))
             dmas("Y", [(T.op[:, :], T.dfull[0:128:16, :])], ["dfull"], ["op"])
+        if first:
+            setup_w("S", 6, 7)
         quant("qe", 0, 128, "eb", "qe", [("eb", b) for b in range(4)])
+        fill(8)
         for i in range(16):
             k, b, s = i % 8, i // 4, i % 4
-            if first and i in (0, 4):
-                setup_w("V", (2 + i // 4,))
-            mm(k, 128, "qwr", 128 * i, "qe", 0, True, True, [("qwr", b), ("qwrs", b), "qe"])
+            mm(k, 128, "qwr", 128 * i, "qe", 0, True, True, [("qwr", i // 2), ("qwrs", i // 2), "qe"])
             out = T.winh[:, 512 * b + s:512 * b + 512:4]
-            if i in H_ON_V:
+            if i in (H_ON_V_FIRST if first else H_ON_V):
                 ts(out, bank(k, 128), 0.015625, A.mult, [("K", k)], [("winh", i)])
             else:
                 act(out, bank(k, 128), F.Copy, [("K", k)], [("winh", i)], scale=0.015625)
@@ -559,13 +551,14 @@ def rank_program(g, core, T, topo):
         quant("qx%d" % (t + 1), 0, 256, "xs", ("qx", t + 1), [("xs", b) for b in range(4)])
 
     X = ("qx", R)
-    mm(0, 256, "qv", 0, "qx3", 0, True, True, ["qv", X])
+    for i in range(2):
+        mm(i, 128, "qv", 0, "qx3", 128 * i, True, True, ["qv", X])
     dmas("Y", [(T.oc[:, :], cv("qx3", 0, 256))], [X], ["oc"])
+    act(T.ysb[:, 0:128], bank(0, 128), F.Copy, [("K", 0)], ["ysb0"])
     dmas("S", [(T.osc[4 * k:4 * k + 4, :], T.qx3_s[32 * k:32 * k + 4, 0:256]) for k in range(4)], [X], ["osc"])
-    vcopy(T.ysb[:], bank(0, 256), [("K", 0)], ["ysb"])
-    dmas("Y", [(T.y[:, :], T.ysb[:])], ["ysb"], ["y"])
+    vcopy(T.ysb[:, 128:256], bank(1, 128), [("K", 1)], ["ysb1"])
+    dmas("Y", [(T.y[:, :], T.ysb[:])], ["ysb0", "ysb1"], ["y"])
     total["ls"] = nrem[0] * n_eng
-    for e in cnt:
-        total["s" + e] = cnt[e]
-    for s in sorted(total):
-        g.wait_ge(T.sem[s], total[s])
+    for s in total:
+        if max(waited[e].get(s, 0) for e in eng) < total[s]:
+            g.wait_ge(T.sem[s], total[s])

from concourse.mybir import dt, AluOpType as A, ActivationFunctionType as F
import comms_topo

R = 3
SCRATCH = {}
SEMAPHORES = ["sV", "sS", "sP", "sG", "ls"] + ["arr%d" % t for t in range(R)] + ["lst%d" % t for t in range(R)] + ["d%d" % i for i in range(32)]


def _b(name, n, d, where="sbuf"):
    SCRATCH[name] = (where, [128, n], d)


def _q(name, n):
    _b(name, n, "float8_e4m3fn_x4")
    _b(name + "_s", n, "uint8")


for _t in range(R):
    _q("qx%d" % _t, 256)
    _q("land%d" % _t, 256)
    _b("lin%d" % _t, 16, "uint16")
for _n, _w in (("qx3", 256), ("qu", 128), ("qr", 256), ("qv", 128), ("wq", 512), ("qwr", 2048), ("kq", 642), ("mq", 1408),
               ("cid", 512), ("m1q", 256), ("m2q", 256), ("qw", 256), ("qe", 128)):
    _q(_n, _w)
for _n, _w in (("xb", 1024), ("xs", 1024), ("ub", 512), ("vb", 512), ("zero", 1024), ("zc", 528), ("kb", 2568), ("onesb", 128),
               ("gcol", 128), ("colid", 140), ("it16", 256), ("msks", 1536), ("cs", 512), ("mt", 5632), ("sb", 4096),
               ("dd", 1024), ("m1", 1024), ("m2", 1024), ("win", 4096), ("winh", 2048), ("fx", 1024), ("fp", 1024), ("etmp", 512),
               ("eb", 512), ("ww", 1024), ("dat", 256)):
    _b(_n, _w, "bfloat16")
for _n in ("itb", "scn", "vv", "vs", "leaf", "c0s", "csort", "crow", "dfull", "ysb"):
    _b(_n, 256, "float32")
for _n, _w in (("lw", 1024), ("rr", 512), ("rm", 512), ("sw", 512), ("qp", 768), ("cf", 48), ("acc", 32), ("nf", 32), ("nx", 16),
               ("smask", 32), ("sg", 32), ("sig", 32), ("w2", 32), ("iq", 16), ("ir", 32), ("tq", 16)):
    _b(_n, _w, "float32")
for _n, _w in (("ci", 8), ("il", 16), ("il2", 128), ("il3", 128), ("ki", 64), ("xi", 32)):
    _b(_n, _w, "int32")
for _n, _w in (("ulist", 16), ("wlist", 128), ("cl", 8), ("nl", 32), ("kl", 48), ("pl", 16), ("ql", 16), ("xl", 16), ("el", 48)):
    _b(_n, _w, "uint16")
for _k in range(8):
    _b("pb%d" % _k, 512, "float32", "psum")

BIG = 2.0 ** 96
STEP = 4096.0
ON_S = (8, 13)
ON_S_FIRST = (8, 14)
M_AT, M_COLS = (0, 256, 448, 576), (256, 192, 128, 128)
H_ON_V = (1, 3, 5, 7, 11)
H_ON_V_FIRST = (5, 7, 11)


def rank_program(g, core, T, topo):
    rank = T.rank_of(core)
    if rank is None:
        return
    nxt = T.cores[(rank + 1) % len(T.cores)]
    prv = T.cores[(rank - 1) % len(T.cores)]
    rid, pid, _se = topo.addr(nxt)
    mask = topo.mask(core, nxt)
    n_eng = len(topo.engines(core, nxt))
    n_in = len(topo.engines(prv, core))

    eng = {"V": g.vector, "S": g.scalar, "P": g.tensor, "G": g, "Y": g.sync}
    cnt = {"V": 0, "S": 0, "P": 0, "G": 0}
    waited = {e: {} for e in eng}
    lastw, readers, total = {}, {}, {}
    ndma, nrem = [0], [0]

    def need(e, reads, writes, acc=False):
        w = {}
        own = "s" + e

        def add(sv):
            if w.get(sv[0], 0) < sv[1]:
                w[sv[0]] = sv[1]
        for k in reads:
            if k in lastw:
                add(lastw[k])
            if k[0] == "K":
                for sv in readers.get(k, ()):
                    if sv[0] != own:
                        add(sv)
        for k in writes:
            if k in lastw and not (acc and lastw[k][0] == own):
                add(lastw[k])
            for sv in readers.get(k, ()):
                if sv[0] != own:
                    add(sv)
        for s, v in w.items():
            if waited[e].get(s, 0) < v:
                eng[e].wait_ge(T.sem[s], v)
                waited[e][s] = v

    def note(sv, reads, writes):
        for k in reads:
            readers.setdefault(k, []).append(sv)
        for k in writes:
            lastw[k] = sv
            readers[k] = []
        total[sv[0]] = max(total.get(sv[0], 0), sv[1])

    def op(e, fn, args, reads, writes, acc=False, **kw):
        need(e, reads, writes, acc)
        cnt[e] += 1
        fn(*args, **kw).then_inc(T.sem["s" + e], 1)
        note(("s" + e, cnt[e]), reads, writes)

    def dmas(e, pairs, reads, writes):
        need(e, reads, writes)
        s = "d%d" % ndma[0]
        ndma[0] += 1
        for out, in_ in pairs:
            eng[e].dma_start(out, in_).then_inc(T.sem[s], 16)
        note((s, 16 * len(pairs)), reads, writes)

    def remote(out, in_, sem, reads):
        need("G", reads, [])
        g.remote_dma(out, in_, T.sem[sem], T.sem.ls, pid, rid, mask)
        nrem[0] += 1

    V, S, P = g.vector, g.scalar, g.tensor

    def cv(name, a, b):
        return T[name][:, a:b].bitcast(dt.uint8)

    def quant(name, a, b, src, key, reads, s0=0):
        op("V", V.quantize_mx, (T[name][:, a:b], T[name + "_s"][:, a:b], T[src][:, s0:s0 + 4 * (b - a)]), reads, [key])

    def bank(k, n):
        return T["pb%d" % k][:, 0:n]

    def mm(k, n, l, la, r, ra, start, stop, reads):
        op("P", P.matmul_mx, (bank(k, n), T[l][:, la:la + 128], T[l + "_s"][:, la:la + 128],
                              T[r][:, ra:ra + n], T[r + "_s"][:, ra:ra + n], start, stop),
           reads, [("K", k)], acc=not start)

    def ts(out, in0, s1, o0, reads, writes, s2=None, o1=None):
        op("V", V.tensor_scalar, (out, in0, s1, s2, o0) if o1 is None else (out, in0, s1, s2, o0, o1), reads, writes)

    def tt(out, a, b, o, reads, writes):
        op("V", V.tensor_tensor, (out, a, b, o), reads, writes)

    def scan(out, d0, d1, init, o0, o1, reads, writes):
        op("V", V.tensor_tensor_scan, (out, d0, d1, init, o0, o1), reads, writes)

    def vcopy(out, in_, reads, writes):
        op("V", V.tensor_copy, (out, in_), reads, writes)

    def act(out, in_, f, reads, writes, **kw):
        op("S", S.activation, (out, in_, f), reads, writes, **kw)

    def iota(ap, key, pat, base, cm, reads=()):
        op("G", g.iota, (ap, pat, base, cm), reads, [key], allow_small_or_imprecise_dtypes=True)

    def spread(e, dst, src, n, reads, qs=range(8)):
        dmas(e, [(T[dst][16 * q:16 * q + 16, n * a:n * a + n], T[src][64 * (q % 2) + 16 * a:64 * (q % 2) + 16 * a + 16, :])
                 for q in qs for a in range(4)], reads, [(dst, q) for q in qs])

    dmas("S", [(T.ub[:], T.u[:, :])], [], ["ub"])
    dmas("Y", [(T.xb[:], T.x[:, :])], [], ["xb"])

    names = ("p", "l", "a0", "a1", "h", "g", "a", "m", "e0", "e1", "x0", "x1", "x2", "y0", "y1", "y2", "ramp", "off", "t0", "t1",
             "s0", "s1", "w0", "pad", "w1", "n0", "n1", "k0", "k1", "iqb", "ak", "bb", "hh")
    C = {k: i for i, k in enumerate(names)}

    def col(k, n=1, step=1):
        return T.cf[:, C[k]:C[k] + (n - 1) * step + 1:step]

    def aff(k, src, scale, bias, n=1, step=1):
        rd = [x for x in (scale, bias) if isinstance(x, str)] + [names[C[src] + i] for i in range(n)]
        act(col(k, n, step), col(src, n), F.Identity, ["cf"] + rd, [names[C[k] + i * step] for i in range(n)],
            scale=col(scale) if isinstance(scale, str) else scale, bias=col(bias) if isinstance(bias, str) else bias)

    def msk(k, n=256):
        return T.msks[:, 256 * k:256 * k + n]

    iota(T.ci[:], "ci", [[0, 8]], 0, 1)
    iota(T.il[:], "il", [[1, 2], [16, 8]], 0, 0)
    iota(T.it16[:], "it16", [[0, 16], [1, 16]], 0, 0)
    iota(T.gcol[:], "gcol", [[1, 8], [0, 16]], 0, 0)
    iota(T.ir[:, 0:16], "ir", [[16, 16]], 15, 0)
    iota(col("pad"), "pad", [[0, 1]], 0, 0)
    iota(msk(5), "m5", [[0, 256]], int(STEP), 0)
    iota(T.colid[:], "colid", [[1, 140]], -10, 0)
    iota(T.ir[:, 16:32], "ir2", [[64, 16]], 15 * int(STEP), 0)
    op("V", V.memset, (T.zero[:], 0.0), [], ["zero"])
    for k, sh, an in (("l", 0, 15), ("a0", 4, 1), ("a1", 5, 1), ("h", 6, 1), ("g", 4, 7), ("a", 4, 3), ("m", 5, 3)):
        ts(T.ci[:, C[k]:C[k] + 1], T.ci[:, 0:1], sh, A.logical_shift_right, ["ci"], ["ci" + k], an, A.bitwise_and)
    vcopy(T.cf[:, 0:8], T.ci[:], ["ci"] + ["ci" + k for k in names[1:8]], ["cf"])
    vcopy(T.ulist[:], T.il[:], ["il"], ["ulist"])
    tails = [(4 * (M_AT[i] + (M_COLS[i] - 48 if i < 3 else 16)), 4 * (M_AT[i] + M_COLS[i])) for i in range(4)]
    ts(msk(0), T.it16[:], col("l"), A.not_equal, ["it16", "cf"], [("msk", 0)], -BIG, A.mult)
    ts(msk(1), T.it16[:], 0.0, A.is_equal, ["it16"], [("msk", 1)], -2.0 * BIG, A.mult)
    ts(msk(4), T.it16[:], 0.0, A.not_equal, ["it16"], [("msk", 4)])
    for s in range(2):
        dmas("Y", [(T.mt[:, 2816 * s + a:2816 * s + b], T.zero[:, 0:b - a]) for a, b in tails], ["zero"], [("mz", s, i) for i in range(4)])
    dmas("Y", [(cv("wq", 0, 512), T.wc[:, :])], [], ["wq"])
    dmas("Y", [(T.wq_s[:], T.ws[:, :])], [], ["wqs"])
    dmas("Y", [(T.kb[:, a:b], T.zero[:, 0:b - a]) for a, b in ((1024, 2048), (2048, 2568))], ["zero"], ["kbz"])
    dmas("Y", [(T.zc[:], T.zero[:, 0:528])], ["zero"], ["zz"])
    dmas("Y", [(T.vb[:], T.v[:, :])], [], ["vb"])
    aff("e0", "a0", 2.0, -1.0, 2)
    aff("ramp", "l", STEP, -15.0 * STEP)
    act(T.msks[:, 1280:1536:16], T.ir[:, 0:16], F.Identity, ["ir", "cf", "m5"], [("msk", 5)], scale=-1.0, bias=col("l"))
    aff("bb", "ramp", 2.0, 0.0)
    aff("x0", "e0", -1.0, "g")
    aff("x1", "e1", -2.0, "g")
    aff("off", "a", 256.0, "bb")
    aff("t0", "l", 16.0, 7.5)
    aff("t1", "l", 16.0, -120.0)
    aff("x2", "e0", -1.0, "x1")
    aff("n0", "e0", 7.5, 7.5, 2)

    def ktile(i, t, src, k, w, n=128):
        ts(T.kb[:, 512 * i + t:512 * i + 4 * n:4], src, col(k), A.is_equal,
           ["colid" if i == 3 else "gcol", "cf", "kbz" if i > 1 else "cf", k] + [w] * isinstance(w, str),
           [("kb", i, t)], col(w) if isinstance(w, str) else w, A.mult)

    def kquant(i, a, b, tiles):
        quant("kq", a, b, "kb", ("kq", i), [("kb", j, t) for j in tiles for t in range(4)], s0=4 * a)

    for t in range(4):
        ktile(0, t, T.gcol[:], "g", 1.0)
    kquant(0, 0, 128, (0,))
    ts(msk(2), msk(0), -1.0, A.mult, [("msk", 0)], [("msk", 2)], -BIG, A.add)
    ts(msk(3), msk(2), STEP, A.add, [("msk", 2)], [("msk", 3)])
    quant("qu", 0, 128, "ub", "qu", ["ub"])
    vcopy(T.qr[:].bitcast(dt.uint32), T.qu[:, 0:128].bitcast(dt.uint32).indirect(T.ulist[:, 0:16]), ["qu", "ulist"], ["qr"])
    act(T.qr_s[:], T.qu_s[:, 0:128].indirect(T.ulist[:, 0:16]), F.Copy, ["qu", "ulist"], ["qrs"])
    quant("qx0", 0, 256, "xb", ("qx", 0), ["xb"])
    for t in range(4):
        ktile(1, t, T.gcol[:], "g", 16.0 ** (t - 1) * (t < 3))
    aff("s0", "e0", 7.5, "t0", 2)
    aff("w0", "e0", "t1", 135.0, 2, 2)
    aff("y0", "x0", 16.0, 0.0, 3)
    aff("iqb", "l", 4.0 - STEP, "m")
    aff("ak", "a", 1024.0, 0.0)
    aff("hh", "a", -1536.0, "h")

    def setup_search():
        vcopy(T.cl[:, 0:5], col("s0", 5), ["s0", "s1", "w0", "pad", "w1"], ["cl"])
        for i in range(2):
            ts(T.smask[:, 16 * i:16 * i + 16], T.it16[:, 0:16], col("l"), A.is_equal, ["it16", "e%d" % i], [("smask", i)], col("e%d" % i), A.mult)
        ts(col("k0", 2), col("n0", 2), col("l"), A.not_equal, ["cf", "n0", "n1"], ["k0", "k1"], 16.0, A.mult)
        kquant(1, 128, 256, (1,))

    def setup_counts(t):
        ktile(2, t, T.gcol[:], "x%d" % t, "e%d" % min(t, 1))
        ktile(3, t, T.colid[:, 8 - 4 * t:138 - 4 * t], "y%d" % t, "e%d" % min(t, 1), 130)

    def setup_merge():
        kquant(4, 514, 642, (4, 5))
        act(T.iq[:], T.ir[:, 16:32], F.Identity, ["ir2", "iqb"], ["iq"], bias=col("iqb"))

    def setup_pool():
        for s in range(2):
            iota(T.acc[:, 16 * s:16 * s + 1], ("acc", s, 0), [[0, 1]], 0, 0)
        iota(T.onesb[:], "onesb", [[0, 128]], 1, 0)
        iota(T.m1[:, 3:1024:4], "m1z", [[0, 256]], 0, 0)
        iota(T.m2[:, 3:1024:4], "m2z", [[0, 256]], 0, 0)
        iota(T.itb[:], "itb", [[1, 256]], 0, 0)
        op("G", g.affine_select, (T.zc[:, 4:516:4], T.onesb[:], [[-1, 128]], A.is_equal, 0.0, 0, 1), ["onesb", "zz"], ["zc"])
        before = "zc"
        for t in range(4):
            for h in range(2):
                a = 2056 + 128 * t + 64 * h + t
                iota(T.kb[64 * h:64 * h + 64, a:a + 61:4], ("kb", 4 + h, t), [[0, 16]], 1, 0, ["kbz", before])
                before = ("kb", 4 + h, t)
        iota(T.il2[:], "il2", [[32, 16], [16, 2], [0, 4]], 0, 0, [before])

    def setup_unpack(b):
        quant("cid", 128 * b, 128 * b + 128, "zc", ("cid", b), ["zz", "zc"], s0=4 - b)

    def setup_wlist(i):
        if i == 0:
            ts(T.il3[:], T.il2[:], col("l"), A.add, ["il2", "cf"], ["il3"])
        else:
            vcopy(T.wlist[:], T.il3[:], ["il3"], ["wlist"])

    def setup_w(e, *pieces):
        for i in pieces:
            a, lst = 256 * i, T.wlist[:, 16 * i:16 * i + 16]
            if e == "V":
                vcopy(T.qwr[:, a:a + 256].bitcast(dt.uint32), T.wq[:, 0:512].bitcast(dt.uint32).indirect(lst), ["wq", "wlist"], [("qwr", i)])
            else:
                act(T.qwr_s[:, a:a + 256], T.wq_s[:, 0:512].indirect(lst), F.Copy, ["wqs", "wlist"], [("qwrs", i)])

    def wrap(src, keys):
        scan(T.scn[:], msk(3), src, 0.0, A.add, A.max, keys + [("msk", 3)], ["scn"])
        return T.scn[:, 15:256:16]

    for t in range(R):
        qx = "qx%d" % t
        X = ("qx", t)
        first, last = t == 0, t == R - 1
        on_s = ON_S_FIRST if first else ON_S
        remote(cv("land%d" % t, 0, 256), cv(qx, 0, 256), "arr%d" % t, [X])
        remote(T["land%d_s" % t][:], T[qx + "_s"][:], "arr%d" % t, [X])
        if first:
            setup_pool()
        iota(T.ww[:], "ww", [[0, 1024]], 0, 0)
        land, lin = "land%d" % t, "lin%d" % t
        lastw[land] = ("arr%d" % t, 2 * n_in)
        lastw[lin] = ("lst%d" % t, n_in)
        total["arr%d" % t] = 2 * n_in
        total["lst%d" % t] = n_in

        for k in range(4):
            mm(k, 256, "qr", 128 * (k // 2), qx, 0, True, True, [X, "qr", "qrs"])

        def part(name, s):
            return T[name][:, 256 * s:256 * s + 256]

        def mine(s, c):
            return T.sw[:, 256 * s + 16 * c + 15:256 * s + 16 * c + 16]

        def slot(s, c, a, b):
            o = 2816 * s + 4 * M_AT[(16 - c) // 4] + (16 - c) % 4
            return T.mt[:, o + 4 * a:o + 4 * b - 3:4]

        def own(s):
            tt(part("rm", s), bank(2 * s, 256), msk(0), A.add, [("K", 2 * s), ("msk", 0)], [("rm", s)])

        def held(s):
            scan(part("sw", s), msk(1), part("rm", s), 0.0, A.add, A.max, [("msk", 1), ("rm", s)], [("sw", s)])

        def near(s):
            tt(slot(s, 16, 0, 256), part("sw", s), bank(2 * s, 256), A.is_ge, [("sw", s), ("K", 2 * s), ("mz", s, 0)], [("mt", s, 16)])

        def near_sum(s):
            scan(part("cs", s), msk(5), slot(s, 16, 0, 256), 0.0, A.min, A.add, [("msk", 5), ("mt", s, 16)], [("cs", s)])

        def pass_v(s, cs):
            for c in cs:
                ts(slot(s, c, 0, 16 * c), bank(2 * s, 16 * c), mine(s, c), A.is_lt,
                   [("K", 2 * s), ("sw", s), ("mz", s, (16 - c) // 4)], [("mt", s, c)])

        def sum_v(s, cs):
            for c in cs:
                a = 2048 * s + 128 * c + 128
                scan(T.sb[:, a - 8 * c:a], slot(s, c, 0, 8 * c), slot(s, c, 8 * c, 16 * c),
                     T.cs[:, 256 * s + 16 * c + 15:256 * s + 16 * c + 16], A.add, A.add, [("mt", s, c), ("cs", s)], [("sb", s, c)])

        flip, owes = [0], []

        def sum_s():
            if owes:
                s, c, o = owes.pop(0)
                act(slot(s, c, 0, 16 * c), T.dd[:, o:o + 16 * c], F.Relu, [("dd", o), ("mz", s, (16 - c) // 4)], [("acc", s, c), ("mt", s, c)],
                    accum_out=T.acc[:, 16 * s + c:16 * s + c + 1])

        def pass_s(s, cs):
            for c in cs:
                o = 256 * (flip[0] % 4)
                flip[0] += 1
                act(T.dd[:, o:o + 16 * c], bank(2 * s + 1, 16 * c), F.Sign, [("K", 2 * s + 1), ("sw", s)], [("dd", o)], scale=-1.0, bias=mine(s, c))
                sum_s()
                owes.append((s, c, o))

        def along_s(s):
            b = on_s[s] + 1
            tt(T.sb[:, 2048 * s + 127:2048 * s + 128 * b:128], T.acc[:, 16 * s:16 * s + b], T.cs[:, 256 * s + 15:256 * s + 16 * b:16], A.add,
               [("acc", s, c) for c in range(b)] + [("cs", s)], [("sb", s, c) for c in range(b)])

        def mquant(s, i, j):
            a, b = M_AT[i], M_AT[j - 1] + M_COLS[j - 1]
            op("V", V.quantize_mx, (T.mq[:, 704 * s + a:704 * s + b], T.mq_s[:, 704 * s + a:704 * s + b], T.mt[:, 2816 * s + 4 * a:2816 * s + 4 * b]),
               [("mt", s, c) for c in range(1, 17) if i <= (16 - c) // 4 < j], [("mq", s, k) for k in range(i, j)])

        def over_lanes(s, tiles):
            for i in tiles:
                mm(2 * s, M_COLS[i], "kq", 0, "mq", 704 * s + M_AT[i], i == 0, i == 3, [("kq", 0), ("mq", s, i)])

        spare = []

        def fill(n=1):
            for _i in range(min(n, len(spare))):
                f, *args = spare.pop(0)
                f(*args)

        def numbers(s):
            f = T.nf[:, 16 * s:16 * s + 16]
            row = wrap(bank(2 * s, 256), [("K", 2 * s)])
            fill()
            tt(f, row, T.sb[:, 2048 * s + 127:2048 * s + 2048:128], A.subtract, ["scn"] + [("sb", s, c) for c in range(16)], [("nf", s)])
            fill()
            ts(T.nl[:, 16 * s:16 * s + 16], f, col("ramp"), A.add, [("nf", s), "ramp"], [("nl", s)])
            fill()

        def unpack(src, key, dst, banks, scale):
            for b, k in enumerate(banks):
                mm(k, 256, "cid", 128 * b, src, 0, True, True, [key, ("cid", b)])
                act(part(dst, b), bank(k, 256), F.Copy, [("K", k)], [(dst, b)], scale=scale)

        def second_step(s):
            i = 16 * min(s, 1)
            tt(T.m2[:, s:1024:4], T.w2[:, i:i + 16].indirect(T.kl[:, 16 * s:16 * s + 16]), part("qp", s), A.is_gt,
               [("w2", min(s, 1)), "kl", ("qp", s)], [("m2", s)])

        top = [list(range(15, on_s[s], -1)) for s in range(2)]
        s1, s2 = (list(range(on_s[s], 0, -1)) for s in range(2))
        own(0)
        for i in range(2):
            act(part("rr", i), bank(1, 256), F.Copy, [("K", 1)], [("rr", i)], scale=1.0 - 2.0 * i)
        dmas("Y", [(T.qp[16 * q:16 * q + 16, 256 * s:256 * s + 256], T.rr[16 * o:16 * o + 16, 256 * (q < o):256 * (q < o) + 256])
                   for s in range(3) for q in range(8) for o in [q ^ (s + 1)]], [("rr", 0), ("rr", 1)], [("qp", s) for s in range(3)])
        own(1)
        held(0)
        pass_s(0, s1)
        sum_s()
        held(1)
        near(0)
        pass_v(0, top[0])
        near_sum(0)
        mquant(0, 0, 1)
        over_lanes(0, (0,))
        sum_v(0, top[0])
        mquant(0, 1, 2)
        if first:
            setup_search()
        mquant(0, 2, 4)
        over_lanes(0, (1, 2, 3))
        pass_s(1, s2[:10])
        along_s(0)
        spare += [(near, 1)] + [(pass_v, 1, [c]) for c in top[1]] + [(near_sum, 1)] + [(sum_v, 1, [c]) for c in top[1]]
        if first:
            spare += [(setup_counts, i) for i in range(3)] + [(kquant, 2, 256, 514, (2, 3))] + [(setup_unpack, b) for b in range(4)]
        fill()
        numbers(0)

        vcopy(T.vv[:, 0:256].indirect(T.nl[:, 0:16]), part("rr", 0), [("nl", 0), ("rr", 0)], ["vv"])
        fill()
        tt(T.sg[:], T.vv[:, 0:256].indirect(T.cl[:, 0:2]), T.smask[:], A.mult, ["vv", "cl", ("smask", 0), ("smask", 1)], ["sg"])
        scan(T.vs[:], msk(2), T.vv[:], 0.0, A.add, A.max, [("msk", 2), "vv"], ["vs"])
        scan(T.sig[:], msk(4, 32), T.sg[:], 0.0, A.mult, A.add, [("msk", 4), "sg"], ["sig"])
        for i in range(2):
            act(T.w2[:, 16 * i:16 * i + 16], T.vs[:, 0:256].indirect(T.cl[:, 2 + 2 * i:3 + 2 * i]), F.Copy, ["vs", "cl", "e%d" % i],
                [("w2", i)], scale=col("e%d" % i))
        pass_s(1, s2[10:])
        sum_s()
        if first:
            act(T.itb[:], T.itb[:], F.Identity, ["itb", "ak"], ["itb"], bias=col("ak"))
        fill()
        for s in range(3):
            i = 16 * min(s, 1) + 15
            ts(T.m1[:, s:1024:4], part("qp", s), T.sig[:, i:i + 1], A.is_lt, [("qp", s), "sig", "k0", "k1"], [("m1", s)],
               col("k%d" % min(s, 1)), A.mult)
        fill()
        quant("m1q", 0, 256, "m1", "m1q", [("m1", s) for s in range(3)] + ["m1z"])
        mm(7, 256, "kq", 128, "m1q", 0, True, True, [("kq", 1), "m1q"])
        mquant(1, 0, 1)
        over_lanes(1, (0,))
        fill(16)
        if first:
            spare += [(setup_wlist, 0), (setup_merge,), (setup_wlist, 1)]
        for k, a in ((0, 256), (1, 386)):
            mm(k, 256, "kq", a, "m1q", 0, True, False, [("kq", 2), "m1q"])
        unpack(land, land, "fp", (4, 5, 6, 3), 0.5)
        spread("S", "win", "fp", 1024, [("fp", b) for b in range(4)])
        row = wrap(bank(7, 256), [("K", 7)])
        fill()
        ts(T.ki[:, 48:64], row, col("ramp"), A.add, ["scn", "ramp"], ["kp"])
        fill()
        for s in range(3):
            ts(T.ki[:, 16 * s:16 * s + 16], T.ki[:, 48:64], 4 * s, A.logical_shift_right, ["kp"], [("ki", s)], 15, A.bitwise_and)
        fill()
        vcopy(T.kl[:], T.ki[:, 0:48], [("ki", s) for s in range(3)], ["kl"])
        second_step(0)
        mquant(1, 1, 4)
        over_lanes(1, (1, 2, 3))
        along_s(1)
        second_step(1)
        spare.append((second_step, 2))
        numbers(1)
        quant("m2q", 0, 256, "m2", "m2q", [("m2", s) for s in range(3)] + ["m2z"])
        for k, a in ((0, 256), (1, 384)):
            mm(k, 256, "kq", a, "m2q", 0, False, True, [("kq", 2), "m2q"])
        vcopy(T.leaf[:, 0:256].indirect(T.nl[:, 16:32]), T.itb[:], ["itb", ("nl", 1)], ["leaf"])
        spread("Y", "lw", "leaf", 256, ["leaf"], range(5))

        act(T.dat[:], bank(1, 256), F.Copy, [("K", 1)], ["dat"])
        spread("S", "lw", "leaf", 256, ["leaf"], range(5, 8))
        tt(T.tq[:], wrap(bank(0, 256), [("K", 0)]), T.nf[:, 0:16], A.add, ["scn", ("nf", 0)], ["tq"])
        act(T.c0s[:], bank(0, 256), F.Copy, [("K", 0)], ["c0s"])
        ts(T.pl[:], T.tq[:], col("off"), A.add, ["tq", "off"], ["pl"])
        vcopy(T.ww[:, 0:1024].indirect(T.pl[:, 0:16]), T.dat[:], ["pl", "dat"], ["ww"])
        unpack(qx, X, "fx", (2, 3, 4, 6), 1.0)
        if first:
            spare += [(setup_w, "V", i) for i in range(8)]
            setup_w("S", 0, 1)

        def gather(out, src, reads, writes):
            if first:
                act(out, src, F.Copy, reads, writes)
                fill()
            else:
                vcopy(out, src, reads, writes)
        quant("qw", 0, 256, "ww", "qw", ["ww"])
        mm(5, 256, "kq", 514, "qw", 0, True, True, [("kq", 4), "qw"])
        fill()
        if last:
            quant("qv", 0, 128, "vb", "qv", ["vb"])
        tt(T.tq[:], T.iq[:], wrap(bank(5, 256), [("K", 5)]), A.subtract, ["scn", "iq"], ["tq"])
        vcopy(T.ql[:], T.tq[:], ["tq"], ["ql"])
        gather(T.crow[:], T.lw[:, 0:1024].indirect(T.ql[:, 0:16]), [("lw", q) for q in range(8)] + ["ql"], ["crow"])
        el = T.el[:, 16 * t:16 * t + 16]
        ts(el, wrap(T.crow[:], ["crow"]), col("ramp"), A.add, ["scn", "ramp"], [("el", t)])
        remote(T[lin][:], el, "lst%d" % t, [("el", t)])
        if first:
            setup_w("S", 2, 3)

        vcopy(T.csort[:, 0:256].indirect(T.nl[:, 0:16]), T.c0s[:], [("nl", 0), "c0s"], ["csort"])
        ts(T.nx[:], T.nf[:, 16:32], col("off"), A.add, [("nf", 1), "off"], ["nx"])
        gather(T.crow[:], T.csort[:, 0:256].indirect(T.nl[:, 16:32]), ["csort", ("nl", 1)], ["crow"])
        tt(T.xi[:, 0:16], wrap(T.crow[:], ["crow"]), T.nx[:], A.add, ["scn", "nx"], ["xi"])
        ts(T.xi[:, 16:32], T.xi[:, 0:16], 511, A.bitwise_and, ["xi"], ["xi2"])
        vcopy(T.xl[:], T.xi[:, 16:32], ["xi2"], ["xl"])
        if last:
            tt(T.vv[:], T.csort[:], T.itb[:], A.add, ["csort", "itb"], ["vv"])
        if first:
            setup_w("S", 4, 5)
        fill()

        def picked(b, i):
            return T.win[:, 256 * b:256 * b + 3328].indirect(T[lin][:, 8 * i:8 * i + 8])
        if first:
            fill()
        else:
            vcopy(T.etmp[:, 384:512], picked(3, 0), [("win", 0), lin], [("etmp", 3)])
        for b in range(4):
            if b < 3 or first:
                act(T.etmp[:, 128 * b:128 * b + 128], picked(b, 0), F.Copy, [("win", 0), lin], [("etmp", b)])
            tt(T.eb[:, b:512:4], picked(b, 1), T.etmp[:, 128 * b:128 * b + 128], A.add, [("win", 0), lin, ("etmp", b)], [("eb", b)])
        if last:
            act(T.dfull[:], T.vv[:, 0:256].indirect(T.nl[:, 16:32]), F.Identity, ["vv", ("nl", 1), "hh"], ["dfull"], scale=2.0, bias=col("hh"))
            dmas("Y", [(T.op[:, :], T.dfull[0:128:16, :])], ["dfull"], ["op"])
        if first:
            setup_w("S", 6, 7)
        quant("qe", 0, 128, "eb", "qe", [("eb", b) for b in range(4)])
        fill(8)
        for i in range(16):
            k, b, s = i % 8, i // 4, i % 4
            mm(k, 128, "qwr", 128 * i, "qe", 0, True, True, [("qwr", i // 2), ("qwrs", i // 2), "qe"])
            out = T.winh[:, 512 * b + s:512 * b + 512:4]
            if i in (H_ON_V_FIRST if first else H_ON_V):
                ts(out, bank(k, 128), 0.015625, A.mult, [("K", k)], [("winh", i)])
            else:
                act(out, bank(k, 128), F.Copy, [("K", k)], [("winh", i)], scale=0.015625)
            if s == 3:
                tt(T.xs[:, b:1024:4], T.winh[:, 512 * b:512 * b + 512].indirect(T.xl[:, 0:16]), part("fx", b), A.add,
                   [("winh", 4 * b + j) for j in range(4)] + ["xl", ("fx", b)], [("xs", b)])
        quant("qx%d" % (t + 1), 0, 256, "xs", ("qx", t + 1), [("xs", b) for b in range(4)])

    X = ("qx", R)
    for i in range(2):
        mm(i, 128, "qv", 0, "qx3", 128 * i, True, True, ["qv", X])
    dmas("Y", [(T.oc[:, :], cv("qx3", 0, 256))], [X], ["oc"])
    act(T.ysb[:, 0:128], bank(0, 128), F.Copy, [("K", 0)], ["ysb0"])
    dmas("S", [(T.osc[4 * k:4 * k + 4, :], T.qx3_s[32 * k:32 * k + 4, 0:256]) for k in range(4)], [X], ["osc"])
    vcopy(T.ysb[:, 128:256], bank(1, 128), [("K", 1)], ["ysb1"])
    dmas("Y", [(T.y[:, :], T.ysb[:])], ["ysb0", "ysb1"], ["y"])
    total["ls"] = nrem[0] * n_eng
    for s in total:
        if max(waited[e].get(s, 0) for e in eng) < total[s]:
            g.wait_ge(T.sem[s], total[s])
